import numpy as np
import ml_dtypes


def mxq(x, axis, fmt="e4m3"):
    dtype, down = {"e4m3": (ml_dtypes.float8_e4m3fn, 7), "e5m2": (ml_dtypes.float8_e5m2, 14)}[fmt]
    v = np.moveaxis(np.asarray(x, np.float32).astype(ml_dtypes.bfloat16).astype(np.float64), axis, -1)
    blocks = v.reshape(v.shape[:-1] + (-1, 32))
    amax = np.abs(blocks).max(-1, keepdims=True)
    byte = np.maximum(np.where(amax > 0, np.frexp(amax)[1] - 1 + 127, 0) - down, 1)
    scale = np.exp2(byte - 127.0)
    codes = (blocks / scale).astype(np.float32).astype(dtype).astype(np.float64)
    return np.moveaxis((codes * scale).reshape(v.shape), -1, axis)


WIDE = False


def mx_kscale(k):
    if not WIDE:
        return np.ones(k)
    levels = np.array([18, -18])
    if k % 512:
        return np.exp2(np.random.permutation(np.resize(levels, k // 32))).repeat(32)
    a = np.empty((k // 512, 16))
    for p in range(k // 512):
        a[p, :8] = np.random.permutation(np.resize(levels, 8))
        for g in range(8):
            far = levels[np.abs(levels - a[p, g]) >= 10]
            a[p, g + 8] = far[np.random.randint(len(far))]
    return np.exp2(a.ravel()).repeat(32)


def f64(x):
    return np.asarray(x).astype(np.float64)


def striped(idx):
    return np.tile(np.asarray(idx).reshape(-1, 16).T, (8, 1)).astype(np.uint16)


def unstriped(offs):
    return offs[:16].T.reshape(-1).astype(np.int64)


def setup_inputs():
    n = np.random.standard_normal
    uni = np.random.uniform
    hd = np.random.permutation(2048)[:512]
    tl = np.random.permutation(2048)[:512]
    f_d = mx_kscale(512)
    f_f = mx_kscale(512)
    return {
        "eT": (np.round(n((512, 2048)) * 32) / 32 * f_d[:, None]).astype(np.float32),
        "M": (n((512, 512)) / np.sqrt(512) / f_d[:, None] * f_f[None, :]).astype(np.float32),
        "rv": (uni(0.75, 1.3, (512, 1)) * f_f[:, None]).astype(np.float32),
        "wi": np.tile(uni(0.75, 1.3, 512), (128, 1)).astype(np.float32),
        "cf": (uni(0.75, 1.3, (512, 1)) / f_f[:, None]).astype(np.float32),
        "hoffs": striped(hd),
        "toffs": striped(tl),
    }


def reference(eT, M, rv, wi, cf, hoffs, toffs):
    hd = unstriped(hoffs)
    tl = unstriped(toffs)
    h = f64(eT)[:, hd]
    t = f64(eT)[:, tl]
    q = h - t
    u = mxq(f64(M), 0, "e4m3").T @ mxq(q, 0, "e4m3")
    e = f64(wi)[:1] * np.square(f64(cf)) * (u + f64(rv))
    dd = mxq(f64(M), 1, "e4m3") @ mxq(e, 0, "e5m2")
    pa = np.zeros((512, 2048))
    pa[:, hd] = dd
    pb = np.zeros((512, 2048))
    pb[:, tl] = dd
    out = pa - pb
    return out

@@ -1,0 +1,194 @@
+from contextlib import ExitStack
+
+import concourse.mybir as mybir
+from concourse.masks import make_identity
+
+F32 = mybir.dt.float32
+BF16 = mybir.dt.bfloat16
+U32 = mybir.dt.uint32
+U16 = mybir.dt.uint16
+U8 = mybir.dt.uint8
+E4M3 = mybir.dt.float8_e4m3fn_x4
+E5M2 = mybir.dt.float8_e5m2_x4
+ALU = mybir.AluOpType
+ACT = mybir.ActivationFunctionType
+
+P = 128
+PACK = 4
+D = 512
+F = 512
+PAIRS = 512
+T = 2048
+HALF = PAIRS // 2
+LIST_COLS = PAIRS // 16
+HALF_COLS = LIST_COLS // 2
+TAIL_CHUNK = 512
+
+FLOPS = 2 * 2 * D * F * PAIRS
+
+
+def tile_attend_gtransr_E_kernel(tc, eT, M, rv, wi, cf, hoffs, toffs, out):
+    nc = tc.nc
+    with ExitStack() as ctx:
+        lists = ctx.enter_context(tc.tile_pool(name="lists", bufs=1))
+        keep = ctx.enter_context(tc.tile_pool(name="keep", bufs=1))
+        ring = ctx.enter_context(tc.tile_pool(name="ring", bufs=2))
+        psum = ctx.enter_context(tc.psum_pool(name="psum", bufs=8))
+
+        heads = lists.tile([P, LIST_COLS], U16, name="heads")
+        tails = lists.tile([P, LIST_COLS], U16, name="tails")
+        e_rows = eT.rearrange("(p j) n -> p j n", j=PACK)
+        out_rows = out.rearrange("(p j) n -> p j n", j=PACK)
+        table = [keep.tile([P, T], F32, name="table%d" % j) for j in range(PACK)]
+        m_raw = keep.tile([P, PACK, F], F32, name="m_raw")
+        wi_sb = keep.tile([P, PAIRS], F32, name="wi_sb")
+        rv_sb = keep.tile([P, PACK], F32, name="rv_sb")
+        cf_sb = keep.tile([P, PACK], F32, name="cf_sb")
+
+        nc.sync.dma_start(table[0][:], e_rows[:, 0, :])
+        nc.sync.dma_start(tails[:], toffs)
+        nc.sync.dma_start(heads[:], hoffs)
+        nc.sync.dma_start(m_raw[:], M.rearrange("(p j) f -> p j f", j=PACK))
+        for j in range(1, PACK):
+            nc.sync.dma_start(table[j][:], e_rows[:, j, :])
+        nc.sync.dma_start(wi_sb[:], wi)
+        nc.sync.dma_start(cf_sb[:], cf.rearrange("(p t) o -> p (t o)", t=PACK))
+        nc.sync.dma_start(rv_sb[:], rv.rearrange("(p t) o -> p (t o)", t=PACK))
+
+        ident = keep.tile([P, P], F32, name="ident")
+        make_identity(nc, ident[:])
+
+        head_win = [keep.tile([P, T], F32, name="head_win%d" % b) for b in range(2)]
+        tail_win = [keep.tile([P, T], F32, name="tail_win%d" % b) for b in range(2)]
+        for b in range(2):
+            nc.vector.memset(head_win[b][:].bitcast(U32), 0)
+            nc.vector.memset(tail_win[b][:].bitcast(U32), 0)
+
+        e_codes = keep.tile([P, PAIRS], U32, name="e_codes", align_bytes=64)
+        e_scales = keep.tile([P, PAIRS], U8, name="e_scales", align_bytes=64)
+        nc.gpsimd.memset(e_codes[:, HALF:], 0)
+        nc.gpsimd.memset(e_scales[:, HALF:].bitcast(U32), 0)
+
+        cf2 = keep.tile([P, PACK], F32, name="cf2")
+        rv_cf2 = keep.tile([P, PACK], F32, name="rv_cf2")
+        nc.gpsimd.tensor_tensor(cf2[:], cf_sb[:], cf_sb[:], ALU.mult)
+        nc.gpsimd.tensor_tensor(rv_cf2[:], rv_sb[:], cf2[:], ALU.mult)
+
+        q_f32 = [keep.tile([P, PACK, HALF], F32, name="q_f32_%d" % h) for h in range(2)]
+
+        def gather(j, h):
+            cols = slice(h * HALF_COLS, (h + 1) * HALF_COLS)
+            picked = ring.tile([P, HALF], F32, name="picked")
+            nc.vector.tensor_copy(picked[:], table[j][:].indirect(tails[:, cols]))
+            nc.vector.tensor_tensor(q_f32[h][:, j, :], table[j][:].indirect(heads[:, cols]), picked[:], ALU.subtract)
+
+        gather(0, 0)
+        gather(0, 1)
+
+        md_bf = keep.tile([P, PACK, P, PACK], BF16, name="md_bf", align_bytes=64)
+        nc.vector.tensor_copy(
+            md_bf[:].rearrange("p t m j -> p m j t"),
+            m_raw[:].rearrange("p j (m t) -> p m j t", t=PACK),
+        )
+        md_codes = keep.tile([P, F], U32, name="md_codes", align_bytes=64)
+        md_scales = keep.tile([P, F], U8, name="md_scales", align_bytes=64)
+        nc.vector.quantize_mx(md_codes[:].bitcast(E4M3), md_scales[:], md_bf[:].rearrange("p t m j -> p (t m j)"))
+
+        mf_bf = keep.tile([P, PACK, P, PACK], BF16, name="mf_bf", align_bytes=64)
+        m_dealt = m_raw[:].rearrange("p j (m t) -> p j t m", t=PACK)
+        for j in range(PACK):
+            turned = psum.tile([P, PACK, P], F32, name="turned", tag="bank")
+            for t in range(PACK):
+                nc.tensor.transpose(turned[:, t, :], m_dealt[:, j, t, :], ident[:])
+            nc.scalar.copy(mf_bf[:, j, :, :], turned[:].rearrange("m t c -> m c t"))
+        mf_codes = keep.tile([P, D], U32, name="mf_codes", align_bytes=64)
+        mf_scales = keep.tile([P, D], U8, name="mf_scales", align_bytes=64)
+
+        for j in range(1, PACK):
+            gather(j, 0)
+            gather(j, 1)
+
+        q_codes = [keep.tile([P, HALF], U32, name="q_codes%d" % h, align_bytes=64) for h in range(2)]
+        q_scales = [keep.tile([P, HALF], U8, name="q_scales%d" % h, align_bytes=64) for h in range(2)]
+        q_bf = [keep.tile([P, HALF, PACK], BF16, name="q_bf%d" % h, align_bytes=64) for h in range(2)]
+        affine = [keep.tile([P, PACK, HALF], F32, name="affine%d" % h) for h in range(2)]
+        e_bf = [keep.tile([P, HALF, PACK], BF16, name="e_bf%d" % h, align_bytes=64) for h in range(2)]
+
+        def project(h):
+            nc.scalar.copy(
+                q_bf[h][:].rearrange("p (c i) t -> p c t i", i=4),
+                q_f32[h][:].rearrange("p t (c i) -> p c t i", i=4),
+            )
+            nc.vector.quantize_mx(q_codes[h][:].bitcast(E4M3), q_scales[h][:], q_bf[h][:].rearrange("p i t -> p (i t)"))
+            for t in range(PACK):
+                cols = slice(t * P, (t + 1) * P)
+                u = psum.tile([P, PAIRS], F32, name="u", tag="bank")
+                nc.tensor.matmul_mx(
+                    out=u[:, :HALF],
+                    lhsT=md_codes[:, cols].bitcast(E4M3),
+                    lhsT_scale=md_scales[:, cols],
+                    rhs=q_codes[h][:].bitcast(E4M3),
+                    rhs_scale=q_scales[h][:],
+                    start=True,
+                    stop=True,
+                )
+                nc.scalar.activation(
+                    affine[h][:, t, :], u[:, :HALF], ACT.Identity, bias=rv_cf2[:, t : t + 1], scale=cf2[:, t : t + 1]
+                )
+
+        def weigh(h):
+            cols = slice(h * HALF, (h + 1) * HALF)
+            nc.vector.tensor_tensor(
+                e_bf[h][:].rearrange("p (c i) t -> p c t i", i=4),
+                affine[h][:].rearrange("p t (c i) -> p c t i", i=4),
+                wi_sb[:, cols].rearrange("p (c i) -> p c i", i=4).unsqueeze(2).to_broadcast([P, HALF // 4, PACK, 4]),
+                ALU.mult,
+            )
+            nc.vector.quantize_mx(e_codes[:, cols].bitcast(E5M2), e_scales[:, cols], e_bf[h][:].rearrange("p i t -> p (i t)"))
+
+        def back(j):
+            cols = slice(j * P, (j + 1) * P)
+            acc = psum.tile([P, PAIRS], F32, name="acc", tag="bank")
+            nc.tensor.matmul_mx(
+                out=acc[:],
+                lhsT=mf_codes[:, cols].bitcast(E4M3),
+                lhsT_scale=mf_scales[:, cols],
+                rhs=e_codes[:].bitcast(E5M2),
+                rhs_scale=e_scales[:],
+                start=True,
+                stop=True,
+            )
+            return acc
+
+        def put(j, dd, cols):
+            nc.vector.tensor_copy(head_win[j % 2][:].indirect(heads[:, cols]), dd)
+            nc.vector.tensor_copy(tail_win[j % 2][:].indirect(tails[:, cols]), dd)
+
+        project(0)
+        nc.vector.quantize_mx(mf_codes[:].bitcast(E4M3), mf_scales[:], mf_bf[:].rearrange("p j c t -> p (j c t)"))
+        project(1)
+        weigh(0)
+        early = back(0)
+        dd_early = keep.tile([P, HALF], F32, name="dd_early")
+        nc.scalar.copy(dd_early[:], early[:, :HALF])
+        weigh(1)
+        put(0, dd_early[:], slice(0, HALF_COLS))
+
+        for j in range(PACK):
+            acc = back(j)
+            dd = keep.tile([P, PAIRS], F32, name="dd%d" % j)
+            if j == 0:
+                nc.scalar.copy(dd[:, HALF:], acc[:, HALF:])
+                put(j, dd[:, HALF:], slice(HALF_COLS, LIST_COLS))
+            else:
+                nc.scalar.copy(dd[:], acc[:])
+                put(j, dd[:], slice(0, LIST_COLS))
+            res = keep.tile([P, T], F32, name="res%d" % j)
+            if j < PACK - 1:
+                nc.gpsimd.tensor_tensor(res[:], head_win[j % 2][:], tail_win[j % 2][:], ALU.subtract)
+                nc.sync.dma_start(out_rows[:, j, :], res[:])
+            else:
+                for c in range(0, T, TAIL_CHUNK):
+                    cols = slice(c, c + TAIL_CHUNK)
+                    nc.vector.tensor_tensor(res[:, cols], head_win[j % 2][:, cols], tail_win[j % 2][:, cols], ALU.subtract)
+                    nc.sync.dma_start(out_rows[:, j, cols], res[:, cols])

@@ -33,14 +33,16 @@ def tile_attend_gtransr_E_kernel(tc, eT, M, rv, wi, cf, hoffs, toffs, out):
         lists = ctx.enter_context(tc.tile_pool(name="lists", bufs=1))
         keep = ctx.enter_context(tc.tile_pool(name="keep", bufs=1))
         ring = ctx.enter_context(tc.tile_pool(name="ring", bufs=2))
-        psum = ctx.enter_context(tc.psum_pool(name="psum", bufs=8))
+        psum = ctx.enter_context(tc.psum_pool(name="psum", bufs=2))
+        psum_u = ctx.enter_context(tc.psum_pool(name="psum_u", bufs=4))
 
         heads = lists.tile([P, LIST_COLS], U16, name="heads")
         tails = lists.tile([P, LIST_COLS], U16, name="tails")
         e_rows = eT.rearrange("(p j) n -> p j n", j=PACK)
         out_rows = out.rearrange("(p j) n -> p j n", j=PACK)
         table = [keep.tile([P, T], F32, name="table%d" % j) for j in range(PACK)]
-        m_raw = keep.tile([P, PACK, F], F32, name="m_raw")
+        m_raw = [keep.tile([P, 2, F], F32, name="m_raw%d" % a) for a in range(2)]
+        m_rows = M.rearrange("(p a j) f -> p a j f", a=2, j=2)
         wi_sb = keep.tile([P, PAIRS], F32, name="wi_sb")
         rv_sb = keep.tile([P, PACK], F32, name="rv_sb")
         cf_sb = keep.tile([P, PACK], F32, name="cf_sb")
@@ -48,9 +50,11 @@ def tile_attend_gtransr_E_kernel(tc, eT, M, rv, wi, cf, hoffs, toffs, out):
         nc.sync.dma_start(table[0][:], e_rows[:, 0, :])
         nc.sync.dma_start(tails[:], toffs)
         nc.sync.dma_start(heads[:], hoffs)
-        nc.sync.dma_start(m_raw[:], M.rearrange("(p j) f -> p j f", j=PACK))
-        for j in range(1, PACK):
-            nc.sync.dma_start(table[j][:], e_rows[:, j, :])
+        nc.sync.dma_start(table[1][:], e_rows[:, 1, :])
+        nc.sync.dma_start(m_raw[0][:], m_rows[:, 0, :, :])
+        nc.sync.dma_start(table[2][:], e_rows[:, 2, :])
+        nc.sync.dma_start(m_raw[1][:], m_rows[:, 1, :, :])
+        nc.sync.dma_start(table[3][:], e_rows[:, 3, :])
         nc.sync.dma_start(wi_sb[:], wi)
         nc.sync.dma_start(cf_sb[:], cf.rearrange("(p t) o -> p (t o)", t=PACK))
         nc.sync.dma_start(rv_sb[:], rv.rearrange("(p t) o -> p (t o)", t=PACK))
@@ -60,9 +64,9 @@ def tile_attend_gtransr_E_kernel(tc, eT, M, rv, wi, cf, hoffs, toffs, out):
 
         head_win = [keep.tile([P, T], F32, name="head_win%d" % b) for b in range(2)]
         tail_win = [keep.tile([P, T], F32, name="tail_win%d" % b) for b in range(2)]
-        for b in range(2):
-            nc.vector.memset(head_win[b][:].bitcast(U32), 0)
-            nc.vector.memset(tail_win[b][:].bitcast(U32), 0)
+        for eng, b in ((nc.vector, 0), (nc.gpsimd, 1)):
+            eng.memset(head_win[b][:].bitcast(U32), 0)
+            eng.memset(tail_win[b][:].bitcast(U32), 0)
 
         e_codes = keep.tile([P, PAIRS], U32, name="e_codes", align_bytes=64)
         e_scales = keep.tile([P, PAIRS], U8, name="e_scales", align_bytes=64)
@@ -76,53 +80,75 @@ def tile_attend_gtransr_E_kernel(tc, eT, M, rv, wi, cf, hoffs, toffs, out):
 
         q_f32 = [keep.tile([P, PACK, HALF], F32, name="q_f32_%d" % h) for h in range(2)]
 
-        def gather(j, h):
+        def pick_tails(j, h, tag):
+            picked = keep.tile([P, HALF], F32, name="picked", tag=tag)
+            nc.vector.tensor_copy(picked[:], table[j][:].indirect(tails[:, h * HALF_COLS : (h + 1) * HALF_COLS]))
+            return picked
+
+        def subtract(j, h, picked):
             cols = slice(h * HALF_COLS, (h + 1) * HALF_COLS)
-            picked = ring.tile([P, HALF], F32, name="picked")
-            nc.vector.tensor_copy(picked[:], table[j][:].indirect(tails[:, cols]))
             nc.vector.tensor_tensor(q_f32[h][:, j, :], table[j][:].indirect(heads[:, cols]), picked[:], ALU.subtract)
 
-        gather(0, 0)
-        gather(0, 1)
+        def gather(j):
+            if j < PACK - 1:
+                both = [pick_tails(j, h, "picked%d" % h) for h in range(2)]
+                for h in range(2):
+                    subtract(j, h, both[h])
+            else:
+                for h in range(2):
+                    subtract(j, h, pick_tails(j, h, "picked0"))
 
         md_bf = keep.tile([P, PACK, P, PACK], BF16, name="md_bf", align_bytes=64)
-        nc.vector.tensor_copy(
-            md_bf[:].rearrange("p t m j -> p m j t"),
-            m_raw[:].rearrange("p j (m t) -> p m j t", t=PACK),
-        )
         md_codes = keep.tile([P, F], U32, name="md_codes", align_bytes=64)
         md_scales = keep.tile([P, F], U8, name="md_scales", align_bytes=64)
-        nc.vector.quantize_mx(md_codes[:].bitcast(E4M3), md_scales[:], md_bf[:].rearrange("p t m j -> p (t m j)"))
+        mf_bf = [keep.tile([P, 2, P, PACK], BF16, name="mf_bf%d" % a, align_bytes=64) for a in range(2)]
+        mf_codes = []
+        mf_scales = [keep.tile([P, 2 * P], U8, name="mf_scales%d" % a, align_bytes=64) for a in range(2)]
 
-        mf_bf = keep.tile([P, PACK, P, PACK], BF16, name="mf_bf", align_bytes=64)
-        m_dealt = m_raw[:].rearrange("p j (m t) -> p j t m", t=PACK)
+        def deal(a):
+            nc.scalar.copy(
+                md_bf[:, :, :, 2 * a : 2 * a + 2].rearrange("p t m j -> p m j t"),
+                m_raw[a][:].rearrange("p j (m t) -> p m j t", t=PACK),
+            )
+
+        def turn(a):
+            m_dealt = m_raw[a][:].rearrange("p j (m t) -> p j t m", t=PACK)
+            for j in range(2):
+                turned = psum.tile([P, PACK, P], F32, name="turned")
+                for t in range(PACK):
+                    nc.tensor.transpose(turned[:, t, :], m_dealt[:, j, t, :], ident[:])
+                nc.scalar.copy(mf_bf[a][:, j, :, :], turned[:].rearrange("m t c -> m c t"))
+
+        def quantize_mf(a, tag):
+            mf_codes.append(keep.tile([P, 2 * P], U32, name="mf_codes", tag=tag, align_bytes=64))
+            nc.vector.quantize_mx(mf_codes[a][:].bitcast(E4M3), mf_scales[a][:], mf_bf[a][:].rearrange("p j c t -> p (j c t)"))
+
         for j in range(PACK):
-            turned = psum.tile([P, PACK, P], F32, name="turned", tag="bank")
-            for t in range(PACK):
-                nc.tensor.transpose(turned[:, t, :], m_dealt[:, j, t, :], ident[:])
-            nc.scalar.copy(mf_bf[:, j, :, :], turned[:].rearrange("m t c -> m c t"))
-        mf_codes = keep.tile([P, D], U32, name="mf_codes", align_bytes=64)
-        mf_scales = keep.tile([P, D], U8, name="mf_scales", align_bytes=64)
-
-        for j in range(1, PACK):
-            gather(j, 0)
-            gather(j, 1)
+            gather(j)
+        deal(0)
+        turn(0)
+        quantize_mf(0, "mf_codes0")
+        deal(1)
+        turn(1)
+        nc.vector.quantize_mx(md_codes[:].bitcast(E4M3), md_scales[:], md_bf[:].rearrange("p t m j -> p (t m j)"))
 
         q_codes = [keep.tile([P, HALF], U32, name="q_codes%d" % h, align_bytes=64) for h in range(2)]
         q_scales = [keep.tile([P, HALF], U8, name="q_scales%d" % h, align_bytes=64) for h in range(2)]
-        q_bf = [keep.tile([P, HALF, PACK], BF16, name="q_bf%d" % h, align_bytes=64) for h in range(2)]
-        affine = [keep.tile([P, PACK, HALF], F32, name="affine%d" % h) for h in range(2)]
+        q_bf = [keep.tile([P, HALF, PACK], BF16, name="q_bf%d" % h, tag="q_bf%d" % h, align_bytes=64) for h in range(2)]
+        affine = [keep.tile([P, PACK, HALF], F32, name="affine%d" % h, tag="affine%d" % h) for h in range(2)]
         e_bf = [keep.tile([P, HALF, PACK], BF16, name="e_bf%d" % h, align_bytes=64) for h in range(2)]
 
-        def project(h):
+        def weave(h):
             nc.scalar.copy(
                 q_bf[h][:].rearrange("p (c i) t -> p c t i", i=4),
                 q_f32[h][:].rearrange("p t (c i) -> p c t i", i=4),
             )
             nc.vector.quantize_mx(q_codes[h][:].bitcast(E4M3), q_scales[h][:], q_bf[h][:].rearrange("p i t -> p (i t)"))
+
+        def project(h):
             for t in range(PACK):
                 cols = slice(t * P, (t + 1) * P)
-                u = psum.tile([P, PAIRS], F32, name="u", tag="bank")
+                u = psum_u.tile([P, PAIRS], F32, name="u")
                 nc.tensor.matmul_mx(
                     out=u[:, :HALF],
                     lhsT=md_codes[:, cols].bitcast(E4M3),
@@ -132,9 +158,14 @@ def tile_attend_gtransr_E_kernel(tc, eT, M, rv, wi, cf, hoffs, toffs, out):
                     start=True,
                     stop=True,
                 )
-                nc.scalar.activation(
-                    affine[h][:, t, :], u[:, :HALF], ACT.Identity, bias=rv_cf2[:, t : t + 1], scale=cf2[:, t : t + 1]
-                )
+                if h == 0 and t < 2:
+                    nc.vector.tensor_scalar(
+                        affine[h][:, t, :], u[:, :HALF], cf2[:, t : t + 1], rv_cf2[:, t : t + 1], ALU.mult, ALU.add
+                    )
+                else:
+                    nc.scalar.activation(
+                        affine[h][:, t, :], u[:, :HALF], ACT.Identity, bias=rv_cf2[:, t : t + 1], scale=cf2[:, t : t + 1]
+                    )
 
         def weigh(h):
             cols = slice(h * HALF, (h + 1) * HALF)
@@ -147,12 +178,12 @@ def tile_attend_gtransr_E_kernel(tc, eT, M, rv, wi, cf, hoffs, toffs, out):
             nc.vector.quantize_mx(e_codes[:, cols].bitcast(E5M2), e_scales[:, cols], e_bf[h][:].rearrange("p i t -> p (i t)"))
 
         def back(j):
-            cols = slice(j * P, (j + 1) * P)
-            acc = psum.tile([P, PAIRS], F32, name="acc", tag="bank")
+            cols = slice((j % 2) * P, (j % 2 + 1) * P)
+            acc = psum.tile([P, PAIRS], F32, name="acc")
             nc.tensor.matmul_mx(
                 out=acc[:],
-                lhsT=mf_codes[:, cols].bitcast(E4M3),
-                lhsT_scale=mf_scales[:, cols],
+                lhsT=mf_codes[j // 2][:, cols].bitcast(E4M3),
+                lhsT_scale=mf_scales[j // 2][:, cols],
                 rhs=e_codes[:].bitcast(E5M2),
                 rhs_scale=e_scales[:],
                 start=True,
@@ -164,14 +195,16 @@ def tile_attend_gtransr_E_kernel(tc, eT, M, rv, wi, cf, hoffs, toffs, out):
             nc.vector.tensor_copy(head_win[j % 2][:].indirect(heads[:, cols]), dd)
             nc.vector.tensor_copy(tail_win[j % 2][:].indirect(tails[:, cols]), dd)
 
+        weave(0)
+        weave(1)
         project(0)
-        nc.vector.quantize_mx(mf_codes[:].bitcast(E4M3), mf_scales[:], mf_bf[:].rearrange("p j c t -> p (j c t)"))
+        quantize_mf(1, "q_bf0")
         project(1)
         weigh(0)
         early = back(0)
-        dd_early = keep.tile([P, HALF], F32, name="dd_early")
-        nc.scalar.copy(dd_early[:], early[:, :HALF])
         weigh(1)
+        dd_early = keep.tile([P, HALF], F32, name="dd_early", tag="affine1")
+        nc.scalar.copy(dd_early[:], early[:, :HALF])
         put(0, dd_early[:], slice(0, HALF_COLS))
 
         for j in range(PACK):
@@ -185,8 +218,10 @@ def tile_attend_gtransr_E_kernel(tc, eT, M, rv, wi, cf, hoffs, toffs, out):
                 put(j, dd[:], slice(0, LIST_COLS))
             res = keep.tile([P, T], F32, name="res%d" % j)
             if j < PACK - 1:
-                nc.gpsimd.tensor_tensor(res[:], head_win[j % 2][:], tail_win[j % 2][:], ALU.subtract)
-                nc.sync.dma_start(out_rows[:, j, :], res[:])
+                for c in range(0, T, T // 2):
+                    cols = slice(c, c + T // 2)
+                    nc.gpsimd.tensor_tensor(res[:, cols], head_win[j % 2][:, cols], tail_win[j % 2][:, cols], ALU.subtract)
+                    nc.sync.dma_start(out_rows[:, j, cols], res[:, cols])
             else:
                 for c in range(0, T, TAIL_CHUNK):
                     cols = slice(c, c + TAIL_CHUNK)

@@ -22,7 +22,7 @@ T = 2048
 HALF = PAIRS // 2
 LIST_COLS = PAIRS // 16
 HALF_COLS = LIST_COLS // 2
-TAIL_CHUNK = 512
+TAIL_EDGES = (0, 256, 768, 1280, 1792, 2048)
 
 FLOPS = 2 * 2 * D * F * PAIRS
 
@@ -50,26 +50,25 @@ def tile_attend_gtransr_E_kernel(tc, eT, M, rv, wi, cf, hoffs, toffs, out):
         nc.sync.dma_start(table[0][:], e_rows[:, 0, :])
         nc.sync.dma_start(tails[:], toffs)
         nc.sync.dma_start(heads[:], hoffs)
+        nc.sync.dma_start(cf_sb[:], cf.rearrange("(p t) o -> p (t o)", t=PACK))
+        nc.sync.dma_start(rv_sb[:], rv.rearrange("(p t) o -> p (t o)", t=PACK))
         nc.sync.dma_start(table[1][:], e_rows[:, 1, :])
         nc.sync.dma_start(m_raw[0][:], m_rows[:, 0, :, :])
         nc.sync.dma_start(table[2][:], e_rows[:, 2, :])
         nc.sync.dma_start(m_raw[1][:], m_rows[:, 1, :, :])
         nc.sync.dma_start(table[3][:], e_rows[:, 3, :])
         nc.sync.dma_start(wi_sb[:], wi)
-        nc.sync.dma_start(cf_sb[:], cf.rearrange("(p t) o -> p (t o)", t=PACK))
-        nc.sync.dma_start(rv_sb[:], rv.rearrange("(p t) o -> p (t o)", t=PACK))
 
         ident = keep.tile([P, P], F32, name="ident")
         make_identity(nc, ident[:])
 
-        head_win = [keep.tile([P, T], F32, name="head_win%d" % b) for b in range(2)]
-        tail_win = [keep.tile([P, T], F32, name="tail_win%d" % b) for b in range(2)]
-        for eng, b in ((nc.vector, 0), (nc.gpsimd, 1)):
-            eng.memset(head_win[b][:].bitcast(U32), 0)
-            eng.memset(tail_win[b][:].bitcast(U32), 0)
+        head_win = [keep.tile([P, T], F32, name="head_win0")]
+        tail_win = [keep.tile([P, T], F32, name="tail_win0")]
+        nc.vector.memset(head_win[0][:].bitcast(U32), 0)
+        nc.vector.memset(tail_win[0][:].bitcast(U32), 0)
 
         e_codes = keep.tile([P, PAIRS], U32, name="e_codes", align_bytes=64)
-        e_scales = keep.tile([P, PAIRS], U8, name="e_scales", align_bytes=64)
+        e_scales = keep.tile([P, PAIRS], U8, name="e_scales", tag="e_scales", align_bytes=64)
         nc.gpsimd.memset(e_codes[:, HALF:], 0)
         nc.gpsimd.memset(e_scales[:, HALF:].bitcast(U32), 0)
 
@@ -101,9 +100,24 @@ def tile_attend_gtransr_E_kernel(tc, eT, M, rv, wi, cf, hoffs, toffs, out):
         md_bf = keep.tile([P, PACK, P, PACK], BF16, name="md_bf", align_bytes=64)
         md_codes = keep.tile([P, F], U32, name="md_codes", align_bytes=64)
         md_scales = keep.tile([P, F], U8, name="md_scales", align_bytes=64)
-        mf_bf = [keep.tile([P, 2, P, PACK], BF16, name="mf_bf%d" % a, align_bytes=64) for a in range(2)]
+        mf_bf = []
         mf_codes = []
-        mf_scales = [keep.tile([P, 2 * P], U8, name="mf_scales%d" % a, align_bytes=64) for a in range(2)]
+        mf_scales = [keep.tile([P, 2 * P], U8, name="mf_scales%d" % a, tag="mf_scales%d" % a, align_bytes=64) for a in range(2)]
+
+        q_codes = [keep.tile([P, HALF], U32, name="q_codes%d" % h, align_bytes=64) for h in range(2)]
+        q_scales = [keep.tile([P, HALF], U8, name="q_scales%d" % h, align_bytes=64) for h in range(2)]
+        q_bf = [keep.tile([P, HALF, PACK], BF16, name="q_bf%d" % h, tag="q_bf%d" % h, align_bytes=64) for h in range(2)]
+        affine = [keep.tile([P, PACK, HALF], F32, name="affine%d" % h, tag="affine%d" % h, align_bytes=64) for h in range(2)]
+        e_bf = [keep.tile([P, HALF, PACK], BF16, name="e_bf%d" % h, tag="e_bf%d" % h, align_bytes=64) for h in range(2)]
+
+        def weave(h):
+            nc.scalar.copy(
+                q_bf[h][:].rearrange("p (c i) t -> p c t i", i=4),
+                q_f32[h][:].rearrange("p t (c i) -> p c t i", i=4),
+            )
+
+        def quantize_q(h):
+            nc.vector.quantize_mx(q_codes[h][:].bitcast(E4M3), q_scales[h][:], q_bf[h][:].rearrange("p i t -> p (i t)"))
 
         def deal(a):
             nc.scalar.copy(
@@ -111,7 +125,8 @@ def tile_attend_gtransr_E_kernel(tc, eT, M, rv, wi, cf, hoffs, toffs, out):
                 m_raw[a][:].rearrange("p j (m t) -> p m j t", t=PACK),
             )
 
-        def turn(a):
+        def turn(a, tag):
+            mf_bf.append(keep.tile([P, 2, P, PACK], BF16, name="mf_bf", tag=tag, align_bytes=64))
             m_dealt = m_raw[a][:].rearrange("p j (m t) -> p j t m", t=PACK)
             for j in range(2):
                 turned = psum.tile([P, PACK, P], F32, name="turned")
@@ -126,24 +141,11 @@ def tile_attend_gtransr_E_kernel(tc, eT, M, rv, wi, cf, hoffs, toffs, out):
         for j in range(PACK):
             gather(j)
         deal(0)
-        turn(0)
+        turn(0, "mf_bf0")
         quantize_mf(0, "mf_codes0")
         deal(1)
-        turn(1)
+        turn(1, "mf_bf1")
         nc.vector.quantize_mx(md_codes[:].bitcast(E4M3), md_scales[:], md_bf[:].rearrange("p t m j -> p (t m j)"))
-
-        q_codes = [keep.tile([P, HALF], U32, name="q_codes%d" % h, align_bytes=64) for h in range(2)]
-        q_scales = [keep.tile([P, HALF], U8, name="q_scales%d" % h, align_bytes=64) for h in range(2)]
-        q_bf = [keep.tile([P, HALF, PACK], BF16, name="q_bf%d" % h, tag="q_bf%d" % h, align_bytes=64) for h in range(2)]
-        affine = [keep.tile([P, PACK, HALF], F32, name="affine%d" % h, tag="affine%d" % h) for h in range(2)]
-        e_bf = [keep.tile([P, HALF, PACK], BF16, name="e_bf%d" % h, align_bytes=64) for h in range(2)]
-
-        def weave(h):
-            nc.scalar.copy(
-                q_bf[h][:].rearrange("p (c i) t -> p c t i", i=4),
-                q_f32[h][:].rearrange("p t (c i) -> p c t i", i=4),
-            )
-            nc.vector.quantize_mx(q_codes[h][:].bitcast(E4M3), q_scales[h][:], q_bf[h][:].rearrange("p i t -> p (i t)"))
 
         def project(h):
             for t in range(PACK):
@@ -195,27 +197,32 @@ def tile_attend_gtransr_E_kernel(tc, eT, M, rv, wi, cf, hoffs, toffs, out):
             nc.vector.tensor_copy(head_win[j % 2][:].indirect(heads[:, cols]), dd)
             nc.vector.tensor_copy(tail_win[j % 2][:].indirect(tails[:, cols]), dd)
 
-        weave(0)
-        weave(1)
+        for h in range(2):
+            weave(h)
+            quantize_q(h)
         project(0)
         quantize_mf(1, "q_bf0")
         project(1)
         weigh(0)
         early = back(0)
         weigh(1)
-        dd_early = keep.tile([P, HALF], F32, name="dd_early", tag="affine1")
+        dd_early = keep.tile([P, HALF], F32, name="dd_early", tag="affine1", align_bytes=64)
         nc.scalar.copy(dd_early[:], early[:, :HALF])
         put(0, dd_early[:], slice(0, HALF_COLS))
 
+        dds = []
         for j in range(PACK):
             acc = back(j)
-            dd = keep.tile([P, PAIRS], F32, name="dd%d" % j)
-            if j == 0:
-                nc.scalar.copy(dd[:, HALF:], acc[:, HALF:])
-                put(j, dd[:, HALF:], slice(HALF_COLS, LIST_COLS))
-            else:
-                nc.scalar.copy(dd[:], acc[:])
-                put(j, dd[:], slice(0, LIST_COLS))
+            dds.append(keep.tile([P, PAIRS], F32, name="dd%d" % j))
+            first = HALF if j == 0 else 0
+            nc.scalar.copy(dds[j][:, first:], acc[:, first:])
+        head_win.append(keep.tile([P, T], F32, name="head_win1", tag="e_bf1", align_bytes=64))
+        tail_win.append(keep.tile([P, T], F32, name="tail_win1", tag="mf_scales0", align_bytes=64))
+        nc.gpsimd.memset(head_win[1][:].bitcast(U32), 0)
+        nc.gpsimd.memset(tail_win[1][:].bitcast(U32), 0)
+        for j in range(PACK):
+            first = HALF if j == 0 else 0
+            put(j, dds[j][:, first:], slice(first // 16, LIST_COLS))
             res = keep.tile([P, T], F32, name="res%d" % j)
             if j < PACK - 1:
                 for c in range(0, T, T // 2):
@@ -223,7 +230,7 @@ def tile_attend_gtransr_E_kernel(tc, eT, M, rv, wi, cf, hoffs, toffs, out):
                     nc.gpsimd.tensor_tensor(res[:, cols], head_win[j % 2][:, cols], tail_win[j % 2][:, cols], ALU.subtract)
                     nc.sync.dma_start(out_rows[:, j, cols], res[:, cols])
             else:
-                for c in range(0, T, TAIL_CHUNK):
-                    cols = slice(c, c + TAIL_CHUNK)
+                for lo, hi in zip(TAIL_EDGES[:-1], TAIL_EDGES[1:]):
+                    cols = slice(lo, hi)
                     nc.vector.tensor_tensor(res[:, cols], head_win[j % 2][:, cols], tail_win[j % 2][:, cols], ALU.subtract)
                     nc.sync.dma_start(out_rows[:, j, cols], res[:, cols])

@@ -66,6 +66,8 @@ def tile_attend_gtransr_E_kernel(tc, eT, M, rv, wi, cf, hoffs, toffs, out):
         tail_win = [keep.tile([P, T], F32, name="tail_win0")]
         nc.vector.memset(head_win[0][:].bitcast(U32), 0)
         nc.vector.memset(tail_win[0][:].bitcast(U32), 0)
+        head_win.append(keep.tile([P, T], F32, name="head_win1"))
+        tail_win.append(keep.tile([P, T], F32, name="tail_win1"))
 
         e_codes = keep.tile([P, PAIRS], U32, name="e_codes", align_bytes=64)
         e_scales = keep.tile([P, PAIRS], U8, name="e_scales", tag="e_scales", align_bytes=64)
@@ -76,6 +78,9 @@ def tile_attend_gtransr_E_kernel(tc, eT, M, rv, wi, cf, hoffs, toffs, out):
         rv_cf2 = keep.tile([P, PACK], F32, name="rv_cf2")
         nc.gpsimd.tensor_tensor(cf2[:], cf_sb[:], cf_sb[:], ALU.mult)
         nc.gpsimd.tensor_tensor(rv_cf2[:], rv_sb[:], cf2[:], ALU.mult)
+
+        nc.gpsimd.memset(head_win[1][:].bitcast(U32), 0)
+        nc.gpsimd.memset(tail_win[1][:].bitcast(U32), 0)
 
         q_f32 = [keep.tile([P, PACK, HALF], F32, name="q_f32_%d" % h) for h in range(2)]
 
@@ -108,7 +113,6 @@ def tile_attend_gtransr_E_kernel(tc, eT, M, rv, wi, cf, hoffs, toffs, out):
         q_scales = [keep.tile([P, HALF], U8, name="q_scales%d" % h, align_bytes=64) for h in range(2)]
         q_bf = [keep.tile([P, HALF, PACK], BF16, name="q_bf%d" % h, tag="q_bf%d" % h, align_bytes=64) for h in range(2)]
         affine = [keep.tile([P, PACK, HALF], F32, name="affine%d" % h, tag="affine%d" % h, align_bytes=64) for h in range(2)]
-        e_bf = [keep.tile([P, HALF, PACK], BF16, name="e_bf%d" % h, tag="e_bf%d" % h, align_bytes=64) for h in range(2)]
 
         def weave(h):
             nc.scalar.copy(
@@ -142,7 +146,6 @@ def tile_attend_gtransr_E_kernel(tc, eT, M, rv, wi, cf, hoffs, toffs, out):
             gather(j)
         deal(0)
         turn(0, "mf_bf0")
-        quantize_mf(0, "mf_codes0")
         deal(1)
         turn(1, "mf_bf1")
         nc.vector.quantize_mx(md_codes[:].bitcast(E4M3), md_scales[:], md_bf[:].rearrange("p t m j -> p (t m j)"))
@@ -169,15 +172,16 @@ def tile_attend_gtransr_E_kernel(tc, eT, M, rv, wi, cf, hoffs, toffs, out):
                         affine[h][:, t, :], u[:, :HALF], ACT.Identity, bias=rv_cf2[:, t : t + 1], scale=cf2[:, t : t + 1]
                     )
 
-        def weigh(h):
+        def weigh(h, eng, tag):
             cols = slice(h * HALF, (h + 1) * HALF)
-            nc.vector.tensor_tensor(
-                e_bf[h][:].rearrange("p (c i) t -> p c t i", i=4),
+            e_bf = keep.tile([P, HALF, PACK], BF16, name="e_bf", tag=tag, align_bytes=64)
+            eng.tensor_tensor(
+                e_bf[:].rearrange("p (c i) t -> p c t i", i=4),
                 affine[h][:].rearrange("p t (c i) -> p c t i", i=4),
                 wi_sb[:, cols].rearrange("p (c i) -> p c i", i=4).unsqueeze(2).to_broadcast([P, HALF // 4, PACK, 4]),
                 ALU.mult,
             )
-            nc.vector.quantize_mx(e_codes[:, cols].bitcast(E5M2), e_scales[:, cols], e_bf[h][:].rearrange("p i t -> p (i t)"))
+            nc.vector.quantize_mx(e_codes[:, cols].bitcast(E5M2), e_scales[:, cols], e_bf[:].rearrange("p i t -> p (i t)"))
 
         def back(j):
             cols = slice((j % 2) * P, (j % 2 + 1) * P)
@@ -194,43 +198,47 @@ def tile_attend_gtransr_E_kernel(tc, eT, M, rv, wi, cf, hoffs, toffs, out):
             return acc
 
         def put(j, dd, cols):
-            nc.vector.tensor_copy(head_win[j % 2][:].indirect(heads[:, cols]), dd)
-            nc.vector.tensor_copy(tail_win[j % 2][:].indirect(tails[:, cols]), dd)
+            nc.vector.tensor_copy(head_win[j % 3][:].indirect(heads[:, cols]), dd)
+            nc.vector.tensor_copy(tail_win[j % 3][:].indirect(tails[:, cols]), dd)
 
         for h in range(2):
             weave(h)
             quantize_q(h)
+        quantize_mf(0, "q_bf0")
         project(0)
-        quantize_mf(1, "q_bf0")
         project(1)
-        weigh(0)
-        early = back(0)
-        weigh(1)
-        dd_early = keep.tile([P, HALF], F32, name="dd_early", tag="affine1", align_bytes=64)
-        nc.scalar.copy(dd_early[:], early[:, :HALF])
-        put(0, dd_early[:], slice(0, HALF_COLS))
+        weigh(0, nc.vector, "e_bf0")
+        quantize_mf(1, "e_bf0")
+        early = [back(0), back(1)]
+        dd_early0 = keep.tile([P, HALF], F32, name="dd_early0")
+        nc.scalar.copy(dd_early0[:], early[0][:, :HALF])
+        put(0, dd_early0[:], slice(0, HALF_COLS))
+        weigh(1, nc.gpsimd, "mf_bf1")
+        dd_early1 = keep.tile([P, HALF], F32, name="dd_early1", tag="affine1", align_bytes=64)
+        nc.scalar.copy(dd_early1[:], early[1][:, :HALF])
+        put(1, dd_early1[:], slice(0, HALF_COLS))
 
         dds = []
         for j in range(PACK):
             acc = back(j)
             dds.append(keep.tile([P, PAIRS], F32, name="dd%d" % j))
-            first = HALF if j == 0 else 0
+            first = HALF if j < 2 else 0
             nc.scalar.copy(dds[j][:, first:], acc[:, first:])
-        head_win.append(keep.tile([P, T], F32, name="head_win1", tag="e_bf1", align_bytes=64))
-        tail_win.append(keep.tile([P, T], F32, name="tail_win1", tag="mf_scales0", align_bytes=64))
-        nc.gpsimd.memset(head_win[1][:].bitcast(U32), 0)
-        nc.gpsimd.memset(tail_win[1][:].bitcast(U32), 0)
+        head_win.append(keep.tile([P, T], F32, name="head_win2", tag="mf_bf1", align_bytes=64))
+        tail_win.append(keep.tile([P, T], F32, name="tail_win2", tag="mf_scales0", align_bytes=64))
+        nc.gpsimd.memset(head_win[2][:].bitcast(U32), 0)
+        nc.gpsimd.memset(tail_win[2][:].bitcast(U32), 0)
         for j in range(PACK):
-            first = HALF if j == 0 else 0
+            first = HALF if j < 2 else 0
             put(j, dds[j][:, first:], slice(first // 16, LIST_COLS))
             res = keep.tile([P, T], F32, name="res%d" % j)
             if j < PACK - 1:
                 for c in range(0, T, T // 2):
                     cols = slice(c, c + T // 2)
-                    nc.gpsimd.tensor_tensor(res[:, cols], head_win[j % 2][:, cols], tail_win[j % 2][:, cols], ALU.subtract)
+                    nc.gpsimd.tensor_tensor(res[:, cols], head_win[j % 3][:, cols], tail_win[j % 3][:, cols], ALU.subtract)
                     nc.sync.dma_start(out_rows[:, j, cols], res[:, cols])
             else:
                 for lo, hi in zip(TAIL_EDGES[:-1], TAIL_EDGES[1:]):
                     cols = slice(lo, hi)
-                    nc.vector.tensor_tensor(res[:, cols], head_win[j % 2][:, cols], tail_win[j % 2][:, cols], ALU.subtract)
+                    nc.vector.tensor_tensor(res[:, cols], head_win[j % 3][:, cols], tail_win[j % 3][:, cols], ALU.subtract)
                     nc.sync.dma_start(out_rows[:, j, cols], res[:, cols])

@@ -32,8 +32,9 @@ def tile_attend_gtransr_E_kernel(tc, eT, M, rv, wi, cf, hoffs, toffs, out):
     with ExitStack() as ctx:
         lists = ctx.enter_context(tc.tile_pool(name="lists", bufs=1))
         keep = ctx.enter_context(tc.tile_pool(name="keep", bufs=1))
-        ring = ctx.enter_context(tc.tile_pool(name="ring", bufs=2))
-        psum = ctx.enter_context(tc.psum_pool(name="psum", bufs=2))
+        shared = ctx.enter_context(tc.tile_pool(name="shared", bufs=1))
+        psum_early = ctx.enter_context(tc.psum_pool(name="psum_early", bufs=1))
+        psum = ctx.enter_context(tc.psum_pool(name="psum", bufs=3))
         psum_u = ctx.enter_context(tc.psum_pool(name="psum_u", bufs=4))
 
         heads = lists.tile([P, LIST_COLS], U16, name="heads")
@@ -41,7 +42,10 @@ def tile_attend_gtransr_E_kernel(tc, eT, M, rv, wi, cf, hoffs, toffs, out):
         e_rows = eT.rearrange("(p j) n -> p j n", j=PACK)
         out_rows = out.rearrange("(p j) n -> p j n", j=PACK)
         table = [keep.tile([P, T], F32, name="table%d" % j) for j in range(PACK)]
-        m_raw = [keep.tile([P, 2, F], F32, name="m_raw%d" % a) for a in range(2)]
+        m_raw = [
+            keep.tile([P, 2, F], F32, name="m_raw0"),
+            shared.tile([P, 2, F], F32, name="m_raw1", offset=2048, align_bytes=64),
+        ]
         m_rows = M.rearrange("(p a j) f -> p a j f", a=2, j=2)
         wi_sb = keep.tile([P, PAIRS], F32, name="wi_sb")
         rv_sb = keep.tile([P, PACK], F32, name="rv_sb")
@@ -50,13 +54,13 @@ def tile_attend_gtransr_E_kernel(tc, eT, M, rv, wi, cf, hoffs, toffs, out):
         nc.sync.dma_start(table[0][:], e_rows[:, 0, :])
         nc.sync.dma_start(tails[:], toffs)
         nc.sync.dma_start(heads[:], hoffs)
+        nc.sync.dma_start(m_raw[0][:], m_rows[:, 0, :, :])
+        nc.sync.dma_start(table[1][:], e_rows[:, 1, :])
+        nc.sync.dma_start(m_raw[1][:], m_rows[:, 1, :, :])
+        nc.sync.dma_start(table[2][:], e_rows[:, 2, :])
+        nc.sync.dma_start(table[3][:], e_rows[:, 3, :])
         nc.sync.dma_start(cf_sb[:], cf.rearrange("(p t) o -> p (t o)", t=PACK))
         nc.sync.dma_start(rv_sb[:], rv.rearrange("(p t) o -> p (t o)", t=PACK))
-        nc.sync.dma_start(table[1][:], e_rows[:, 1, :])
-        nc.sync.dma_start(m_raw[0][:], m_rows[:, 0, :, :])
-        nc.sync.dma_start(table[2][:], e_rows[:, 2, :])
-        nc.sync.dma_start(m_raw[1][:], m_rows[:, 1, :, :])
-        nc.sync.dma_start(table[3][:], e_rows[:, 3, :])
         nc.sync.dma_start(wi_sb[:], wi)
 
         ident = keep.tile([P, P], F32, name="ident")
@@ -65,7 +69,6 @@ def tile_attend_gtransr_E_kernel(tc, eT, M, rv, wi, cf, hoffs, toffs, out):
         head_win = [keep.tile([P, T], F32, name="head_win0")]
         tail_win = [keep.tile([P, T], F32, name="tail_win0")]
         nc.vector.memset(head_win[0][:].bitcast(U32), 0)
-        nc.vector.memset(tail_win[0][:].bitcast(U32), 0)
         head_win.append(keep.tile([P, T], F32, name="head_win1"))
         tail_win.append(keep.tile([P, T], F32, name="tail_win1"))
 
@@ -74,53 +77,46 @@ def tile_attend_gtransr_E_kernel(tc, eT, M, rv, wi, cf, hoffs, toffs, out):
         nc.gpsimd.memset(e_codes[:, HALF:], 0)
         nc.gpsimd.memset(e_scales[:, HALF:].bitcast(U32), 0)
 
+        nc.gpsimd.memset(tail_win[0][:].bitcast(U32), 0)
+        nc.gpsimd.memset(head_win[1][:].bitcast(U32), 0)
+        nc.gpsimd.memset(tail_win[1][:].bitcast(U32), 0)
+
         cf2 = keep.tile([P, PACK], F32, name="cf2")
         rv_cf2 = keep.tile([P, PACK], F32, name="rv_cf2")
         nc.gpsimd.tensor_tensor(cf2[:], cf_sb[:], cf_sb[:], ALU.mult)
         nc.gpsimd.tensor_tensor(rv_cf2[:], rv_sb[:], cf2[:], ALU.mult)
 
-        nc.gpsimd.memset(head_win[1][:].bitcast(U32), 0)
-        nc.gpsimd.memset(tail_win[1][:].bitcast(U32), 0)
+        q_f32 = {}
 
-        q_f32 = [keep.tile([P, PACK, HALF], F32, name="q_f32_%d" % h) for h in range(2)]
-
-        def pick_tails(j, h, tag):
-            picked = keep.tile([P, HALF], F32, name="picked", tag=tag)
+        def pick_tails(j, h, tag, offset=None):
+            if offset is None:
+                picked = keep.tile([P, HALF], F32, name="picked", tag=tag)
+            else:
+                picked = shared.tile([P, HALF], F32, name=tag, offset=offset, align_bytes=64)
             nc.vector.tensor_copy(picked[:], table[j][:].indirect(tails[:, h * HALF_COLS : (h + 1) * HALF_COLS]))
             return picked
 
         def subtract(j, h, picked):
             cols = slice(h * HALF_COLS, (h + 1) * HALF_COLS)
-            nc.vector.tensor_tensor(q_f32[h][:, j, :], table[j][:].indirect(heads[:, cols]), picked[:], ALU.subtract)
-
-        def gather(j):
-            if j < PACK - 1:
-                both = [pick_tails(j, h, "picked%d" % h) for h in range(2)]
-                for h in range(2):
-                    subtract(j, h, both[h])
-            else:
-                for h in range(2):
-                    subtract(j, h, pick_tails(j, h, "picked0"))
+            nc.vector.tensor_tensor(q_f32[j // 2, h][:, j % 2, :], table[j][:].indirect(heads[:, cols]), picked[:], ALU.subtract)
 
         md_bf = keep.tile([P, PACK, P, PACK], BF16, name="md_bf", align_bytes=64)
         md_codes = keep.tile([P, F], U32, name="md_codes", align_bytes=64)
-        md_scales = keep.tile([P, F], U8, name="md_scales", align_bytes=64)
         mf_bf = []
         mf_codes = []
-        mf_scales = [keep.tile([P, 2 * P], U8, name="mf_scales%d" % a, tag="mf_scales%d" % a, align_bytes=64) for a in range(2)]
-
-        q_codes = [keep.tile([P, HALF], U32, name="q_codes%d" % h, align_bytes=64) for h in range(2)]
-        q_scales = [keep.tile([P, HALF], U8, name="q_scales%d" % h, align_bytes=64) for h in range(2)]
-        q_bf = [keep.tile([P, HALF, PACK], BF16, name="q_bf%d" % h, tag="q_bf%d" % h, align_bytes=64) for h in range(2)]
+        mf_scales = []
+        q_codes = []
+        q_scales = [keep.tile([P, HALF], U8, name="q_scales%d" % h, tag="q_scales%d" % h, align_bytes=64) for h in range(2)]
         affine = [keep.tile([P, PACK, HALF], F32, name="affine%d" % h, tag="affine%d" % h, align_bytes=64) for h in range(2)]
 
-        def weave(h):
+        def weave(a, h):
             nc.scalar.copy(
-                q_bf[h][:].rearrange("p (c i) t -> p c t i", i=4),
-                q_f32[h][:].rearrange("p t (c i) -> p c t i", i=4),
+                q_bf[h][:, :, 2 * a : 2 * a + 2].rearrange("p (c i) t -> p c t i", i=4),
+                q_f32[a, h][:].rearrange("p t (c i) -> p c t i", i=4),
             )
 
-        def quantize_q(h):
+        def quantize_q(h, tag):
+            q_codes.append(keep.tile([P, HALF], U32, name="q_codes", tag=tag, align_bytes=64))
             nc.vector.quantize_mx(q_codes[h][:].bitcast(E4M3), q_scales[h][:], q_bf[h][:].rearrange("p i t -> p (i t)"))
 
         def deal(a):
@@ -129,26 +125,46 @@ def tile_attend_gtransr_E_kernel(tc, eT, M, rv, wi, cf, hoffs, toffs, out):
                 m_raw[a][:].rearrange("p j (m t) -> p m j t", t=PACK),
             )
 
-        def turn(a, tag):
-            mf_bf.append(keep.tile([P, 2, P, PACK], BF16, name="mf_bf", tag=tag, align_bytes=64))
-            m_dealt = m_raw[a][:].rearrange("p j (m t) -> p j t m", t=PACK)
-            for j in range(2):
-                turned = psum.tile([P, PACK, P], F32, name="turned")
-                for t in range(PACK):
-                    nc.tensor.transpose(turned[:, t, :], m_dealt[:, j, t, :], ident[:])
-                nc.scalar.copy(mf_bf[a][:, j, :, :], turned[:].rearrange("m t c -> m c t"))
+        md_words = md_bf[:].rearrange("p t m j -> p (t m j)").bitcast(F32).rearrange("p (t m a) -> p t m a", t=PACK, a=2)
 
-        def quantize_mf(a, tag):
-            mf_codes.append(keep.tile([P, 2 * P], U32, name="mf_codes", tag=tag, align_bytes=64))
+        def turn(a):
+            mf_bf.append(shared.tile([P, 2, P, PACK], BF16, name="mf_bf%d" % a, offset=4160 - a * 2048, align_bytes=64))
+            turned = psum.tile([P, PACK * P], F32, name="turned", tag="bank")
+            for t in range(PACK):
+                nc.tensor.transpose(turned[:, t * P : (t + 1) * P], md_words[:, t, :, a], ident[:])
+            nc.scalar.copy(mf_bf[a][:], turned[:].bitcast(BF16).rearrange("m (t c e) -> m e c t", t=PACK, e=2))
+
+        def quantize_mf(a, codes_tag, scales_tag):
+            mf_codes.append(keep.tile([P, 2 * P], U32, name="mf_codes", tag=codes_tag, align_bytes=64))
+            mf_scales.append(keep.tile([P, 2 * P], U8, name="mf_scales", tag=scales_tag, align_bytes=64))
             nc.vector.quantize_mx(mf_codes[a][:].bitcast(E4M3), mf_scales[a][:], mf_bf[a][:].rearrange("p j c t -> p (j c t)"))
 
-        for j in range(PACK):
-            gather(j)
+        for h in range(2):
+            q_f32[0, h] = keep.tile([P, 2, HALF], F32, name="q_f32_low%d" % h)
+        q_f32[1, 0] = shared.tile([P, 2, HALF], F32, name="q_f32_high0", offset=8192, align_bytes=64)
+        for j in range(2):
+            both = [pick_tails(j, h, "picked%d" % h) for h in range(2)]
+            for h in range(2):
+                subtract(j, h, both[h])
         deal(0)
-        turn(0, "mf_bf0")
         deal(1)
-        turn(1, "mf_bf1")
+        q_bf = [shared.tile([P, HALF, PACK], BF16, name="q_bf0", offset=64, align_bytes=64)]
+        weave(0, 0)
+        turn(0)
+        turn(1)
+        third = [pick_tails(2, h, "picked%d" % h) for h in range(2)]
+        subtract(2, 0, third[0])
+        subtract(3, 0, pick_tails(3, 0, "picked2", 10240))
+        md_scales = shared.tile([P, F], U8, name="md_scales", offset=10240, align_bytes=64)
         nc.vector.quantize_mx(md_codes[:].bitcast(E4M3), md_scales[:], md_bf[:].rearrange("p t m j -> p (t m j)"))
+        last_tails = pick_tails(3, 1, "picked3", 10752)
+        weave(1, 0)
+        quantize_q(0, "q_codes0")
+        q_bf.append(shared.tile([P, HALF, PACK], BF16, name="q_bf1", offset=8192, align_bytes=64))
+        weave(0, 1)
+        q_f32[1, 1] = shared.tile([P, 2, HALF], F32, name="q_f32_high1", offset=64, align_bytes=64)
+        subtract(2, 1, third[1])
+        subtract(3, 1, last_tails)
 
         def project(h):
             for t in range(PACK):
@@ -163,7 +179,7 @@ def tile_attend_gtransr_E_kernel(tc, eT, M, rv, wi, cf, hoffs, toffs, out):
                     start=True,
                     stop=True,
                 )
-                if h == 0 and t < 2:
+                if h == 0 and t == PACK - 1:
                     nc.vector.tensor_scalar(
                         affine[h][:, t, :], u[:, :HALF], cf2[:, t : t + 1], rv_cf2[:, t : t + 1], ALU.mult, ALU.add
                     )
@@ -183,9 +199,21 @@ def tile_attend_gtransr_E_kernel(tc, eT, M, rv, wi, cf, hoffs, toffs, out):
             )
             nc.vector.quantize_mx(e_codes[:, cols].bitcast(E5M2), e_scales[:, cols], e_bf[:].rearrange("p i t -> p (i t)"))
 
-        def back(j):
+        def weigh_by_planes(h, tag):
+            cols = slice(h * HALF, (h + 1) * HALF)
+            e_f32 = keep.tile([P, PACK, HALF], F32, name="e_f32", tag="e_f32", align_bytes=64)
+            for t in range(PACK):
+                nc.gpsimd.tensor_tensor(e_f32[:, t, :], affine[h][:, t, :], wi_sb[:, cols], ALU.mult)
+            e_bf = keep.tile([P, HALF, PACK], BF16, name="e_bf", tag=tag, align_bytes=64)
+            nc.scalar.copy(
+                e_bf[:].rearrange("p (c i) t -> p c t i", i=4),
+                e_f32[:].rearrange("p t (c i) -> p c t i", i=4),
+            )
+            nc.vector.quantize_mx(e_codes[:, cols].bitcast(E5M2), e_scales[:, cols], e_bf[:].rearrange("p i t -> p (i t)"))
+
+        def back(j, pool):
             cols = slice((j % 2) * P, (j % 2 + 1) * P)
-            acc = psum.tile([P, PAIRS], F32, name="acc")
+            acc = pool.tile([P, PAIRS], F32, name="acc", tag="bank")
             nc.tensor.matmul_mx(
                 out=acc[:],
                 lhsT=mf_codes[j // 2][:, cols].bitcast(E4M3),
@@ -201,31 +229,34 @@ def tile_attend_gtransr_E_kernel(tc, eT, M, rv, wi, cf, hoffs, toffs, out):
             nc.vector.tensor_copy(head_win[j % 3][:].indirect(heads[:, cols]), dd)
             nc.vector.tensor_copy(tail_win[j % 3][:].indirect(tails[:, cols]), dd)
 
-        for h in range(2):
-            weave(h)
-            quantize_q(h)
-        quantize_mf(0, "q_bf0")
         project(0)
-        project(1)
+        quantize_mf(0, "mf_codes0", "q_scales0")
         weigh(0, nc.vector, "e_bf0")
-        quantize_mf(1, "e_bf0")
-        early = [back(0), back(1)]
+        quantize_mf(1, "q_codes0", "mf_scales1")
+        weave(1, 1)
+        early0 = back(0, psum_early)
         dd_early0 = keep.tile([P, HALF], F32, name="dd_early0")
-        nc.scalar.copy(dd_early0[:], early[0][:, :HALF])
+        nc.scalar.copy(dd_early0[:], early0[:, :HALF])
+        quantize_q(1, "e_bf0")
+        project(1)
         put(0, dd_early0[:], slice(0, HALF_COLS))
-        weigh(1, nc.gpsimd, "mf_bf1")
-        dd_early1 = keep.tile([P, HALF], F32, name="dd_early1", tag="affine1", align_bytes=64)
-        nc.scalar.copy(dd_early1[:], early[1][:, :HALF])
-        put(1, dd_early1[:], slice(0, HALF_COLS))
+        early1 = back(1, psum_early)
+        dd_early1 = keep.tile([P, HALF], F32, name="dd_early1")
+        nc.scalar.copy(dd_early1[:], early1[:, :HALF])
+        nc.vector.tensor_copy(head_win[1][:].indirect(heads[:, :HALF_COLS]), dd_early1[:])
+        weigh_by_planes(1, "e_bf1")
+        dd_held = keep.tile([P, HALF], F32, name="dd_held", tag="e_f32", align_bytes=64)
+        nc.scalar.copy(dd_held[:], early1[:, :HALF])
+        nc.vector.tensor_copy(tail_win[1][:].indirect(tails[:, :HALF_COLS]), dd_held[:])
 
         dds = []
         for j in range(PACK):
-            acc = back(j)
+            acc = back(j, psum)
             dds.append(keep.tile([P, PAIRS], F32, name="dd%d" % j))
             first = HALF if j < 2 else 0
             nc.scalar.copy(dds[j][:, first:], acc[:, first:])
-        head_win.append(keep.tile([P, T], F32, name="head_win2", tag="mf_bf1", align_bytes=64))
-        tail_win.append(keep.tile([P, T], F32, name="tail_win2", tag="mf_scales0", align_bytes=64))
+        head_win.append(keep.tile([P, T], F32, name="head_win2", tag="e_bf1", align_bytes=64))
+        tail_win.append(keep.tile([P, T], F32, name="tail_win2", tag="q_scales0", align_bytes=64))
         nc.gpsimd.memset(head_win[2][:].bitcast(U32), 0)
         nc.gpsimd.memset(tail_win[2][:].bitcast(U32), 0)
         for j in range(PACK):

@@ -20,6 +20,7 @@ F = 512
 PAIRS = 512
 T = 2048
 HALF = PAIRS // 2
+QUARTER = PAIRS // 4
 LIST_COLS = PAIRS // 16
 HALF_COLS = LIST_COLS // 2
 TAIL_EDGES = (0, 256, 768, 1280, 1792, 2048)
@@ -42,22 +43,17 @@ def tile_attend_gtransr_E_kernel(tc, eT, M, rv, wi, cf, hoffs, toffs, out):
         e_rows = eT.rearrange("(p j) n -> p j n", j=PACK)
         out_rows = out.rearrange("(p j) n -> p j n", j=PACK)
         table = [keep.tile([P, T], F32, name="table%d" % j) for j in range(PACK)]
-        m_raw = [
-            keep.tile([P, 2, F], F32, name="m_raw0"),
-            shared.tile([P, 2, F], F32, name="m_raw1", offset=2048, align_bytes=64),
-        ]
-        m_rows = M.rearrange("(p a j) f -> p a j f", a=2, j=2)
+        m_raw = keep.tile([P, PACK, F], F32, name="m_raw")
         wi_sb = keep.tile([P, PAIRS], F32, name="wi_sb")
         rv_sb = keep.tile([P, PACK], F32, name="rv_sb")
-        cf_sb = keep.tile([P, PACK], F32, name="cf_sb")
+        cf_sb = shared.tile([P, PACK], F32, name="cf_sb", offset=8192, align_bytes=64)
 
         nc.sync.dma_start(table[0][:], e_rows[:, 0, :])
         nc.sync.dma_start(tails[:], toffs)
         nc.sync.dma_start(heads[:], hoffs)
-        nc.sync.dma_start(m_raw[0][:], m_rows[:, 0, :, :])
         nc.sync.dma_start(table[1][:], e_rows[:, 1, :])
-        nc.sync.dma_start(m_raw[1][:], m_rows[:, 1, :, :])
         nc.sync.dma_start(table[2][:], e_rows[:, 2, :])
+        nc.sync.dma_start(m_raw[:], M.rearrange("(p j) f -> p j f", j=PACK))
         nc.sync.dma_start(table[3][:], e_rows[:, 3, :])
         nc.sync.dma_start(cf_sb[:], cf.rearrange("(p t) o -> p (t o)", t=PACK))
         nc.sync.dma_start(rv_sb[:], rv.rearrange("(p t) o -> p (t o)", t=PACK))
@@ -69,6 +65,7 @@ def tile_attend_gtransr_E_kernel(tc, eT, M, rv, wi, cf, hoffs, toffs, out):
         head_win = [keep.tile([P, T], F32, name="head_win0")]
         tail_win = [keep.tile([P, T], F32, name="tail_win0")]
         nc.vector.memset(head_win[0][:].bitcast(U32), 0)
+        nc.vector.memset(tail_win[0][:].bitcast(U32), 0)
         head_win.append(keep.tile([P, T], F32, name="head_win1"))
         tail_win.append(keep.tile([P, T], F32, name="tail_win1"))
 
@@ -77,7 +74,6 @@ def tile_attend_gtransr_E_kernel(tc, eT, M, rv, wi, cf, hoffs, toffs, out):
         nc.gpsimd.memset(e_codes[:, HALF:], 0)
         nc.gpsimd.memset(e_scales[:, HALF:].bitcast(U32), 0)
 
-        nc.gpsimd.memset(tail_win[0][:].bitcast(U32), 0)
         nc.gpsimd.memset(head_win[1][:].bitcast(U32), 0)
         nc.gpsimd.memset(tail_win[1][:].bitcast(U32), 0)
 
@@ -86,130 +82,119 @@ def tile_attend_gtransr_E_kernel(tc, eT, M, rv, wi, cf, hoffs, toffs, out):
         nc.gpsimd.tensor_tensor(cf2[:], cf_sb[:], cf_sb[:], ALU.mult)
         nc.gpsimd.tensor_tensor(rv_cf2[:], rv_sb[:], cf2[:], ALU.mult)
 
-        q_f32 = {}
-
-        def pick_tails(j, h, tag, offset=None):
-            if offset is None:
-                picked = keep.tile([P, HALF], F32, name="picked", tag=tag)
-            else:
-                picked = shared.tile([P, HALF], F32, name=tag, offset=offset, align_bytes=64)
+        def pick_tails(j, h, picked):
             nc.vector.tensor_copy(picked[:], table[j][:].indirect(tails[:, h * HALF_COLS : (h + 1) * HALF_COLS]))
             return picked
 
-        def subtract(j, h, picked):
-            cols = slice(h * HALF_COLS, (h + 1) * HALF_COLS)
-            nc.vector.tensor_tensor(q_f32[j // 2, h][:, j % 2, :], table[j][:].indirect(heads[:, cols]), picked[:], ALU.subtract)
+        def subtract(j, lo, hi, q_out, picked):
+            nc.vector.tensor_tensor(q_out, table[j][:].indirect(heads[:, lo // 16 : hi // 16]), picked, ALU.subtract)
+
+        def weave(dst, src):
+            nc.scalar.copy(dst.rearrange("p (c i) t -> p c t i", i=4), src.rearrange("p t (c i) -> p c t i", i=4))
+
+        def quantize(codes, scales, src, fmt):
+            nc.vector.quantize_mx(codes.bitcast(fmt), scales, src.rearrange("p i t -> p (i t)"))
 
         md_bf = keep.tile([P, PACK, P, PACK], BF16, name="md_bf", align_bytes=64)
         md_codes = keep.tile([P, F], U32, name="md_codes", align_bytes=64)
-        mf_bf = []
-        mf_codes = []
-        mf_scales = []
-        q_codes = []
-        q_scales = [keep.tile([P, HALF], U8, name="q_scales%d" % h, tag="q_scales%d" % h, align_bytes=64) for h in range(2)]
-        affine = [keep.tile([P, PACK, HALF], F32, name="affine%d" % h, tag="affine%d" % h, align_bytes=64) for h in range(2)]
-
-        def weave(a, h):
-            nc.scalar.copy(
-                q_bf[h][:, :, 2 * a : 2 * a + 2].rearrange("p (c i) t -> p c t i", i=4),
-                q_f32[a, h][:].rearrange("p t (c i) -> p c t i", i=4),
-            )
-
-        def quantize_q(h, tag):
-            q_codes.append(keep.tile([P, HALF], U32, name="q_codes", tag=tag, align_bytes=64))
-            nc.vector.quantize_mx(q_codes[h][:].bitcast(E4M3), q_scales[h][:], q_bf[h][:].rearrange("p i t -> p (i t)"))
-
-        def deal(a):
-            nc.scalar.copy(
-                md_bf[:, :, :, 2 * a : 2 * a + 2].rearrange("p t m j -> p m j t"),
-                m_raw[a][:].rearrange("p j (m t) -> p m j t", t=PACK),
-            )
-
+        md_scales = shared.tile([P, F], U8, name="md_scales", offset=8192, align_bytes=64)
+        m_dealt = m_raw[:].rearrange("p j (m t) -> p m j t", t=PACK)
+        md_view = md_bf[:].rearrange("p t m j -> p m j t")
         md_words = md_bf[:].rearrange("p t m j -> p (t m j)").bitcast(F32).rearrange("p (t m a) -> p t m a", t=PACK, a=2)
+        mf_bf = []
+        mf_scales = [keep.tile([P, 2 * P], U8, name="mf_scales%d" % a, tag="mf_scales%d" % a, align_bytes=64) for a in range(2)]
+        mf_codes = []
+
+        def turn_raw():
+            mf_bf.append(keep.tile([P, 2 * P, PACK], BF16, name="mf_bf0", align_bytes=64))
+            for j in range(2):
+                turned = psum.tile([P, PACK, P], F32, name="turned", tag="bank")
+                for t in range(PACK):
+                    nc.tensor.transpose(turned[:, t, :], m_dealt[:, :, j, t], ident[:])
+                nc.scalar.copy(mf_bf[0][:, j * P : (j + 1) * P, :], turned[:].rearrange("m t c -> m c t"))
 
         def turn(a):
-            mf_bf.append(shared.tile([P, 2, P, PACK], BF16, name="mf_bf%d" % a, offset=4160 - a * 2048, align_bytes=64))
+            mf_bf.append(shared.tile([P, 2 * P, PACK], BF16, name="mf_bf%d" % a, offset=16384, align_bytes=64))
             turned = psum.tile([P, PACK * P], F32, name="turned", tag="bank")
             for t in range(PACK):
                 nc.tensor.transpose(turned[:, t * P : (t + 1) * P], md_words[:, t, :, a], ident[:])
-            nc.scalar.copy(mf_bf[a][:], turned[:].bitcast(BF16).rearrange("m (t c e) -> m e c t", t=PACK, e=2))
+            nc.scalar.copy(
+                mf_bf[a][:].rearrange("m (e c) t -> m e c t", e=2),
+                turned[:].bitcast(BF16).rearrange("m (t c e) -> m e c t", t=PACK, e=2),
+            )
 
-        def quantize_mf(a, codes_tag, scales_tag):
-            mf_codes.append(keep.tile([P, 2 * P], U32, name="mf_codes", tag=codes_tag, align_bytes=64))
-            mf_scales.append(keep.tile([P, 2 * P], U8, name="mf_scales", tag=scales_tag, align_bytes=64))
-            nc.vector.quantize_mx(mf_codes[a][:].bitcast(E4M3), mf_scales[a][:], mf_bf[a][:].rearrange("p j c t -> p (j c t)"))
+        q_first = shared.tile([P, PACK, HALF], F32, name="q_first", offset=0, align_bytes=64)
+        q_low = keep.tile([P, 2, HALF], F32, name="q_low")
+        q_second = keep.tile([P, HALF, PACK], BF16, name="q_second", align_bytes=64)
+        q_codes = {}
+        q_scales = keep.tile([P, PAIRS], U8, name="q_scales", align_bytes=64)
+        affine = [keep.tile([P, PACK, HALF], F32, name="affine%d" % h, align_bytes=64) for h in range(2)]
 
-        for h in range(2):
-            q_f32[0, h] = keep.tile([P, 2, HALF], F32, name="q_f32_low%d" % h)
-        q_f32[1, 0] = shared.tile([P, 2, HALF], F32, name="q_f32_high0", offset=8192, align_bytes=64)
-        for j in range(2):
-            both = [pick_tails(j, h, "picked%d" % h) for h in range(2)]
-            for h in range(2):
-                subtract(j, h, both[h])
-        deal(0)
-        deal(1)
-        q_bf = [shared.tile([P, HALF, PACK], BF16, name="q_bf0", offset=64, align_bytes=64)]
-        weave(0, 0)
-        turn(0)
-        turn(1)
-        third = [pick_tails(2, h, "picked%d" % h) for h in range(2)]
-        subtract(2, 0, third[0])
-        subtract(3, 0, pick_tails(3, 0, "picked2", 10240))
-        md_scales = shared.tile([P, F], U8, name="md_scales", offset=10240, align_bytes=64)
-        nc.vector.quantize_mx(md_codes[:].bitcast(E4M3), md_scales[:], md_bf[:].rearrange("p t m j -> p (t m j)"))
-        last_tails = pick_tails(3, 1, "picked3", 10752)
-        weave(1, 0)
-        quantize_q(0, "q_codes0")
-        q_bf.append(shared.tile([P, HALF, PACK], BF16, name="q_bf1", offset=8192, align_bytes=64))
-        weave(0, 1)
-        q_f32[1, 1] = shared.tile([P, 2, HALF], F32, name="q_f32_high1", offset=64, align_bytes=64)
-        subtract(2, 1, third[1])
-        subtract(3, 1, last_tails)
+        def gather_early(j):
+            both = [pick_tails(j, h, keep.tile([P, HALF], F32, name="picked", tag="picked%d" % h)) for h in range(2)]
+            subtract(j, 0, HALF, q_first[:, j, :], both[0][:])
+            if j < 2:
+                subtract(j, HALF, PAIRS, q_low[:, j, :], both[1][:])
+            return both[1]
 
-        def project(h):
+        def project(lo, hi):
             for t in range(PACK):
                 cols = slice(t * P, (t + 1) * P)
                 u = psum_u.tile([P, PAIRS], F32, name="u")
                 nc.tensor.matmul_mx(
-                    out=u[:, :HALF],
+                    out=u[:, : hi - lo],
                     lhsT=md_codes[:, cols].bitcast(E4M3),
                     lhsT_scale=md_scales[:, cols],
-                    rhs=q_codes[h][:].bitcast(E4M3),
-                    rhs_scale=q_scales[h][:],
+                    rhs=q_codes[lo][:].bitcast(E4M3),
+                    rhs_scale=q_scales[:, lo:hi],
                     start=True,
                     stop=True,
                 )
-                if h == 0 and t == PACK - 1:
-                    nc.vector.tensor_scalar(
-                        affine[h][:, t, :], u[:, :HALF], cf2[:, t : t + 1], rv_cf2[:, t : t + 1], ALU.mult, ALU.add
-                    )
-                else:
-                    nc.scalar.activation(
-                        affine[h][:, t, :], u[:, :HALF], ACT.Identity, bias=rv_cf2[:, t : t + 1], scale=cf2[:, t : t + 1]
-                    )
+                dst = affine[lo // HALF][:, t, lo % HALF : lo % HALF + hi - lo]
+                nc.scalar.activation(dst, u[:, : hi - lo], ACT.Identity, bias=rv_cf2[:, t : t + 1], scale=cf2[:, t : t + 1])
 
-        def weigh(h, eng, tag):
-            cols = slice(h * HALF, (h + 1) * HALF)
-            e_bf = keep.tile([P, HALF, PACK], BF16, name="e_bf", tag=tag, align_bytes=64)
-            eng.tensor_tensor(
-                e_bf[:].rearrange("p (c i) t -> p c t i", i=4),
-                affine[h][:].rearrange("p t (c i) -> p c t i", i=4),
-                wi_sb[:, cols].rearrange("p (c i) -> p c i", i=4).unsqueeze(2).to_broadcast([P, HALF // 4, PACK, 4]),
+        def weigh(lo, hi, e_bf):
+            nc.vector.tensor_tensor(
+                e_bf.rearrange("p (c i) t -> p c t i", i=4),
+                affine[0][:, :, lo:hi].rearrange("p t (c i) -> p c t i", i=4),
+                wi_sb[:, lo:hi].rearrange("p (c i) -> p c i", i=4).unsqueeze(2).to_broadcast([P, (hi - lo) // 4, PACK, 4]),
                 ALU.mult,
             )
-            nc.vector.quantize_mx(e_codes[:, cols].bitcast(E5M2), e_scales[:, cols], e_bf[:].rearrange("p i t -> p (i t)"))
 
-        def weigh_by_planes(h, tag):
-            cols = slice(h * HALF, (h + 1) * HALF)
-            e_f32 = keep.tile([P, PACK, HALF], F32, name="e_f32", tag="e_f32", align_bytes=64)
-            for t in range(PACK):
-                nc.gpsimd.tensor_tensor(e_f32[:, t, :], affine[h][:, t, :], wi_sb[:, cols], ALU.mult)
-            e_bf = keep.tile([P, HALF, PACK], BF16, name="e_bf", tag=tag, align_bytes=64)
-            nc.scalar.copy(
-                e_bf[:].rearrange("p (c i) t -> p c t i", i=4),
-                e_f32[:].rearrange("p t (c i) -> p c t i", i=4),
-            )
-            nc.vector.quantize_mx(e_codes[:, cols].bitcast(E5M2), e_scales[:, cols], e_bf[:].rearrange("p i t -> p (i t)"))
+        gather_early(0)
+        gather_early(1)
+        weave(q_second[:, :, 0:2], q_low[:])
+        q_high = shared.tile([P, 2, HALF], F32, name="q_high", offset=16384, align_bytes=64)
+        subtract(2, HALF, PAIRS, q_high[:, 0, :], gather_early(2)[:])
+        nc.scalar.copy(md_view, m_dealt)
+        turn_raw()
+        picked = pick_tails(3, 0, keep.tile([P, HALF], F32, name="picked_last"))
+        quarters = ((0, QUARTER), (QUARTER, HALF))
+        for lo, hi in quarters:
+            subtract(3, lo, hi, q_first[:, 3, lo:hi], picked[:, lo:hi])
+        for a in range(2):
+            cols = slice(a * HALF, (a + 1) * HALF)
+            quantize(md_codes[:, cols], md_scales[:, cols], md_bf[:, 2 * a : 2 * a + 2].rearrange("p t m j -> p (t m) j"), E4M3)
+        for lo, hi in quarters:
+            q_bf = keep.tile([P, QUARTER, PACK], BF16, name="q_bf", tag="q_bf%d" % lo, align_bytes=64)
+            weave(q_bf[:], q_first[:, :, lo:hi])
+            q_codes[lo] = keep.tile([P, QUARTER], U32, name="q_codes%d" % lo, align_bytes=64)
+            quantize(q_codes[lo][:], q_scales[:, lo:hi], q_bf[:], E4M3)
+        mf_codes.append(keep.tile([P, 2 * P], U32, name="mf_codes0", tag="q_bf0", align_bytes=64))
+        quantize(mf_codes[0][:], mf_scales[0][:], mf_bf[0][:], E4M3)
+        for lo, hi in quarters:
+            project(lo, hi)
+        last_tails = pick_tails(3, 1, shared.tile([P, HALF], F32, name="last_tails", offset=0, align_bytes=64))
+        subtract(3, HALF, PAIRS, q_high[:, 1, :], last_tails[:])
+
+        e_first = [keep.tile([P, QUARTER, PACK], BF16, name="e_first", tag="e_first%d" % lo, align_bytes=64) for lo, hi in quarters]
+        for (lo, hi), e_bf in zip(quarters, e_first):
+            weigh(lo, hi, e_bf[:])
+        for (lo, hi), e_bf in zip(quarters, e_first):
+            quantize(e_codes[:, lo:hi], e_scales[:, lo:hi], e_bf[:], E5M2)
+        weave(q_second[:, :, 2:4], q_high[:])
+        q_codes[HALF] = keep.tile([P, HALF], U32, name="q_codes_second", tag="e_first0", align_bytes=64)
+        quantize(q_codes[HALF][:], q_scales[:, HALF:], q_second[:], E4M3)
 
         def back(j, pool):
             cols = slice((j % 2) * P, (j % 2 + 1) * P)
@@ -229,25 +214,28 @@ def tile_attend_gtransr_E_kernel(tc, eT, M, rv, wi, cf, hoffs, toffs, out):
             nc.vector.tensor_copy(head_win[j % 3][:].indirect(heads[:, cols]), dd)
             nc.vector.tensor_copy(tail_win[j % 3][:].indirect(tails[:, cols]), dd)
 
-        project(0)
-        quantize_mf(0, "mf_codes0", "q_scales0")
-        weigh(0, nc.vector, "e_bf0")
-        quantize_mf(1, "q_codes0", "mf_scales1")
-        weave(1, 1)
         early0 = back(0, psum_early)
         dd_early0 = keep.tile([P, HALF], F32, name="dd_early0")
         nc.scalar.copy(dd_early0[:], early0[:, :HALF])
-        quantize_q(1, "e_bf0")
-        project(1)
         put(0, dd_early0[:], slice(0, HALF_COLS))
+        project(HALF, PAIRS)
         early1 = back(1, psum_early)
         dd_early1 = keep.tile([P, HALF], F32, name="dd_early1")
         nc.scalar.copy(dd_early1[:], early1[:, :HALF])
         nc.vector.tensor_copy(head_win[1][:].indirect(heads[:, :HALF_COLS]), dd_early1[:])
-        weigh_by_planes(1, "e_bf1")
-        dd_held = keep.tile([P, HALF], F32, name="dd_held", tag="e_f32", align_bytes=64)
-        nc.scalar.copy(dd_held[:], early1[:, :HALF])
-        nc.vector.tensor_copy(tail_win[1][:].indirect(tails[:, :HALF_COLS]), dd_held[:])
+
+        turn(1)
+        mf_codes.append(keep.tile([P, 2 * P], U32, name="mf_codes1", align_bytes=64))
+        quantize(mf_codes[1][:], mf_scales[1][:], mf_bf[1][:], E4M3)
+        e_f32 = keep.tile([P, PACK, HALF], F32, name="e_f32", tag="e_f32", align_bytes=64)
+        for t in range(PACK):
+            nc.gpsimd.tensor_tensor(e_f32[:, t, :], affine[1][:, t, :], wi_sb[:, HALF:], ALU.mult)
+        e_second = keep.tile([P, HALF, PACK], BF16, name="e_second", tag="e_bf1", align_bytes=64)
+        weave(e_second[:], e_f32[:])
+        quantize(e_codes[:, HALF:], e_scales[:, HALF:], e_second[:], E5M2)
+        dd_held1 = keep.tile([P, HALF], F32, name="dd_held1", tag="e_f32", align_bytes=64)
+        nc.scalar.copy(dd_held1[:], early1[:, :HALF])
+        nc.vector.tensor_copy(tail_win[1][:].indirect(tails[:, :HALF_COLS]), dd_held1[:])
 
         dds = []
         for j in range(PACK):
@@ -256,7 +244,7 @@ def tile_attend_gtransr_E_kernel(tc, eT, M, rv, wi, cf, hoffs, toffs, out):
             first = HALF if j < 2 else 0
             nc.scalar.copy(dds[j][:, first:], acc[:, first:])
         head_win.append(keep.tile([P, T], F32, name="head_win2", tag="e_bf1", align_bytes=64))
-        tail_win.append(keep.tile([P, T], F32, name="tail_win2", tag="q_scales0", align_bytes=64))
+        tail_win.append(keep.tile([P, T], F32, name="tail_win2", tag="mf_scales0", align_bytes=64))
         nc.gpsimd.memset(head_win[2][:].bitcast(U32), 0)
         nc.gpsimd.memset(tail_win[2][:].bitcast(U32), 0)
         for j in range(PACK):

@@ -34,29 +34,31 @@ def tile_attend_gtransr_E_kernel(tc, eT, M, rv, wi, cf, hoffs, toffs, out):
         lists = ctx.enter_context(tc.tile_pool(name="lists", bufs=1))
         keep = ctx.enter_context(tc.tile_pool(name="keep", bufs=1))
         shared = ctx.enter_context(tc.tile_pool(name="shared", bufs=1))
-        psum_early = ctx.enter_context(tc.psum_pool(name="psum_early", bufs=1))
-        psum = ctx.enter_context(tc.psum_pool(name="psum", bufs=3))
-        psum_u = ctx.enter_context(tc.psum_pool(name="psum_u", bufs=4))
+        psum = ctx.enter_context(tc.psum_pool(name="psum", bufs=1))
+
+        def bank(b):
+            return psum.tile([P, PAIRS], F32, name="bank%d" % b, tag="bank%d" % b)
 
         heads = lists.tile([P, LIST_COLS], U16, name="heads")
         tails = lists.tile([P, LIST_COLS], U16, name="tails")
         e_rows = eT.rearrange("(p j) n -> p j n", j=PACK)
         out_rows = out.rearrange("(p j) n -> p j n", j=PACK)
         table = [keep.tile([P, T], F32, name="table%d" % j) for j in range(PACK)]
-        m_raw = keep.tile([P, PACK, F], F32, name="m_raw")
+        m_raw = [shared.tile([P, PACK, F // 2], F32, name="m_raw%d" % h, offset=4096 * h, align_bytes=64) for h in range(2)]
         wi_sb = keep.tile([P, PAIRS], F32, name="wi_sb")
         rv_sb = keep.tile([P, PACK], F32, name="rv_sb")
-        cf_sb = shared.tile([P, PACK], F32, name="cf_sb", offset=8192, align_bytes=64)
+        cf_sb = keep.tile([P, PACK], F32, name="cf_sb")
 
         nc.sync.dma_start(table[0][:], e_rows[:, 0, :])
         nc.sync.dma_start(tails[:], toffs)
         nc.sync.dma_start(heads[:], hoffs)
-        nc.sync.dma_start(table[1][:], e_rows[:, 1, :])
-        nc.sync.dma_start(table[2][:], e_rows[:, 2, :])
-        nc.sync.dma_start(m_raw[:], M.rearrange("(p j) f -> p j f", j=PACK))
-        nc.sync.dma_start(table[3][:], e_rows[:, 3, :])
         nc.sync.dma_start(cf_sb[:], cf.rearrange("(p t) o -> p (t o)", t=PACK))
         nc.sync.dma_start(rv_sb[:], rv.rearrange("(p t) o -> p (t o)", t=PACK))
+        for j in range(1, PACK):
+            nc.sync.dma_start(table[j][:], e_rows[:, j, :])
+        m_rows = M.rearrange("(p j) f -> p j f", j=PACK)
+        for h in range(2):
+            nc.sync.dma_start(m_raw[h][:], m_rows[:, :, h * (F // 2) : (h + 1) * (F // 2)])
         nc.sync.dma_start(wi_sb[:], wi)
 
         ident = keep.tile([P, P], F32, name="ident")
@@ -71,6 +73,8 @@ def tile_attend_gtransr_E_kernel(tc, eT, M, rv, wi, cf, hoffs, toffs, out):
 
         e_codes = keep.tile([P, PAIRS], U32, name="e_codes", align_bytes=64)
         e_scales = keep.tile([P, PAIRS], U8, name="e_scales", tag="e_scales", align_bytes=64)
+        zeros = keep.tile([P, QUARTER], F32, name="zeros")
+        nc.gpsimd.memset(zeros[:].bitcast(U32), 0)
         nc.gpsimd.memset(e_codes[:, HALF:], 0)
         nc.gpsimd.memset(e_scales[:, HALF:].bitcast(U32), 0)
 
@@ -97,50 +101,36 @@ def tile_attend_gtransr_E_kernel(tc, eT, M, rv, wi, cf, hoffs, toffs, out):
 
         md_bf = keep.tile([P, PACK, P, PACK], BF16, name="md_bf", align_bytes=64)
         md_codes = keep.tile([P, F], U32, name="md_codes", align_bytes=64)
-        md_scales = shared.tile([P, F], U8, name="md_scales", offset=8192, align_bytes=64)
-        m_dealt = m_raw[:].rearrange("p j (m t) -> p m j t", t=PACK)
+        md_scales = keep.tile([P, F], U8, name="md_scales", align_bytes=64)
         md_view = md_bf[:].rearrange("p t m j -> p m j t")
         md_words = md_bf[:].rearrange("p t m j -> p (t m j)").bitcast(F32).rearrange("p (t m a) -> p t m a", t=PACK, a=2)
-        mf_bf = []
-        mf_scales = [keep.tile([P, 2 * P], U8, name="mf_scales%d" % a, tag="mf_scales%d" % a, align_bytes=64) for a in range(2)]
-        mf_codes = []
+        mf_codes = [keep.tile([P, P], U32, name="mf_codes%d" % j, align_bytes=64) for j in range(2)]
+        mf_scales = [keep.tile([P, P], U8, name="mf_scales%d" % j, tag="mf_scales%d" % j, align_bytes=64) for j in range(2)]
+        late_codes = keep.tile([P, 2 * P], U32, name="late_codes", align_bytes=64)
+        late_scales = keep.tile([P, 2 * P], U8, name="late_scales", align_bytes=64)
 
-        def turn_raw():
-            mf_bf.append(keep.tile([P, 2 * P, PACK], BF16, name="mf_bf0", align_bytes=64))
-            for j in range(2):
-                turned = psum.tile([P, PACK, P], F32, name="turned", tag="bank")
-                for t in range(PACK):
-                    nc.tensor.transpose(turned[:, t, :], m_dealt[:, :, j, t], ident[:])
-                nc.scalar.copy(mf_bf[0][:, j * P : (j + 1) * P, :], turned[:].rearrange("m t c -> m c t"))
-
-        def turn(a):
-            mf_bf.append(shared.tile([P, 2 * P, PACK], BF16, name="mf_bf%d" % a, offset=16384, align_bytes=64))
-            turned = psum.tile([P, PACK * P], F32, name="turned", tag="bank")
+        def turn(a, b):
+            turned = bank(b)
             for t in range(PACK):
                 nc.tensor.transpose(turned[:, t * P : (t + 1) * P], md_words[:, t, :, a], ident[:])
-            nc.scalar.copy(
-                mf_bf[a][:].rearrange("m (e c) t -> m e c t", e=2),
-                turned[:].bitcast(BF16).rearrange("m (t c e) -> m e c t", t=PACK, e=2),
-            )
+            return turned[:].bitcast(BF16).rearrange("m (t c e) -> m e c t", t=PACK, e=2)
 
-        q_first = shared.tile([P, PACK, HALF], F32, name="q_first", offset=0, align_bytes=64)
-        q_low = keep.tile([P, 2, HALF], F32, name="q_low")
-        q_second = keep.tile([P, HALF, PACK], BF16, name="q_second", align_bytes=64)
+        quarters = ((0, QUARTER), (QUARTER, HALF))
+        q_first = keep.tile([P, PACK, HALF], F32, name="q_first")
+        q_rest = shared.tile([P, PACK, HALF], F32, name="q_rest", offset=16384, align_bytes=64)
         q_codes = {}
         q_scales = keep.tile([P, PAIRS], U8, name="q_scales", align_bytes=64)
         affine = [keep.tile([P, PACK, HALF], F32, name="affine%d" % h, align_bytes=64) for h in range(2)]
 
-        def gather_early(j):
+        def gather_early(j, q_out):
             both = [pick_tails(j, h, keep.tile([P, HALF], F32, name="picked", tag="picked%d" % h)) for h in range(2)]
             subtract(j, 0, HALF, q_first[:, j, :], both[0][:])
-            if j < 2:
-                subtract(j, HALF, PAIRS, q_low[:, j, :], both[1][:])
-            return both[1]
+            subtract(j, HALF, PAIRS, q_out, both[1][:])
 
-        def project(lo, hi):
+        def project(lo, hi, banks):
             for t in range(PACK):
                 cols = slice(t * P, (t + 1) * P)
-                u = psum_u.tile([P, PAIRS], F32, name="u")
+                u = bank(banks[t])
                 nc.tensor.matmul_mx(
                     out=u[:, : hi - lo],
                     lhsT=md_codes[:, cols].bitcast(E4M3),
@@ -161,48 +151,56 @@ def tile_attend_gtransr_E_kernel(tc, eT, M, rv, wi, cf, hoffs, toffs, out):
                 ALU.mult,
             )
 
-        gather_early(0)
-        gather_early(1)
-        weave(q_second[:, :, 0:2], q_low[:])
-        q_high = shared.tile([P, 2, HALF], F32, name="q_high", offset=16384, align_bytes=64)
-        subtract(2, HALF, PAIRS, q_high[:, 0, :], gather_early(2)[:])
-        nc.scalar.copy(md_view, m_dealt)
-        turn_raw()
-        picked = pick_tails(3, 0, keep.tile([P, HALF], F32, name="picked_last"))
-        quarters = ((0, QUARTER), (QUARTER, HALF))
-        for lo, hi in quarters:
-            subtract(3, lo, hi, q_first[:, 3, lo:hi], picked[:, lo:hi])
-        for a in range(2):
+        def quantize_md(a):
             cols = slice(a * HALF, (a + 1) * HALF)
             quantize(md_codes[:, cols], md_scales[:, cols], md_bf[:, 2 * a : 2 * a + 2].rearrange("p t m j -> p (t m) j"), E4M3)
+
+        for j in range(PACK - 1):
+            gather_early(j, q_rest[:, j, :])
+        picked = keep.tile([P, HALF], F32, name="picked_last")
         for lo, hi in quarters:
-            q_bf = keep.tile([P, QUARTER, PACK], BF16, name="q_bf", tag="q_bf%d" % lo, align_bytes=64)
-            weave(q_bf[:], q_first[:, :, lo:hi])
-            q_codes[lo] = keep.tile([P, QUARTER], U32, name="q_codes%d" % lo, align_bytes=64)
-            quantize(q_codes[lo][:], q_scales[:, lo:hi], q_bf[:], E4M3)
-        mf_codes.append(keep.tile([P, 2 * P], U32, name="mf_codes0", tag="q_bf0", align_bytes=64))
-        quantize(mf_codes[0][:], mf_scales[0][:], mf_bf[0][:], E4M3)
+            nc.vector.tensor_tensor(picked[:, lo:hi], table[3][:].indirect(tails[:, lo // 16 : hi // 16]), zeros[:], ALU.subtract)
         for lo, hi in quarters:
-            project(lo, hi)
-        last_tails = pick_tails(3, 1, shared.tile([P, HALF], F32, name="last_tails", offset=0, align_bytes=64))
-        subtract(3, HALF, PAIRS, q_high[:, 1, :], last_tails[:])
+            subtract(3, lo, hi, q_first[:, 3, lo:hi], picked[:, lo:hi])
+        nc.scalar.copy(md_view[:, : P // 2], m_raw[0][:].rearrange("p j (m t) -> p m j t", t=PACK))
+        nc.vector.tensor_copy(md_view[:, P // 2 :], m_raw[1][:].rearrange("p j (m t) -> p m j t", t=PACK))
+        turned = turn(0, 4)
+        q_bf = []
+        for c, (lo, hi) in enumerate(quarters):
+            q_bf.append(shared.tile([P, QUARTER, PACK], BF16, name="q_bf%d" % c, offset=1024 * c, align_bytes=64))
+            weave(q_bf[c][:], q_first[:, :, lo:hi])
+        for c, (lo, hi) in enumerate(quarters):
+            quantize_md(c)
+            q_codes[lo] = shared.tile([P, QUARTER], U32, name="q_codes%d" % c, offset=8192 + 4096 * c, align_bytes=64)
+            quantize(q_codes[lo][:], q_scales[:, lo:hi], q_bf[c][:], E4M3)
+        mf_bf0 = keep.tile([P, P, PACK], BF16, name="mf_bf0", align_bytes=64)
+        nc.scalar.copy(mf_bf0[:], turned[:, 0])
+        quantize(mf_codes[0][:], mf_scales[0][:], mf_bf0[:], E4M3)
+        for lo, hi in quarters:
+            project(lo, hi, (0, 1, 2, 3))
+        mf_bf1 = shared.tile([P, P, PACK], BF16, name="mf_bf1", offset=12288 + 256, align_bytes=64)
+        nc.scalar.copy(mf_bf1[:], turned[:, 1])
+        last_tails = pick_tails(3, 1, shared.tile([P, HALF], F32, name="last_tails", offset=1024, align_bytes=64))
+        subtract(3, HALF, PAIRS, q_rest[:, 3, :], last_tails[:])
 
         e_first = [keep.tile([P, QUARTER, PACK], BF16, name="e_first", tag="e_first%d" % lo, align_bytes=64) for lo, hi in quarters]
         for (lo, hi), e_bf in zip(quarters, e_first):
             weigh(lo, hi, e_bf[:])
-        for (lo, hi), e_bf in zip(quarters, e_first):
-            quantize(e_codes[:, lo:hi], e_scales[:, lo:hi], e_bf[:], E5M2)
-        weave(q_second[:, :, 2:4], q_high[:])
-        q_codes[HALF] = keep.tile([P, HALF], U32, name="q_codes_second", tag="e_first0", align_bytes=64)
+        quantize(e_codes[:, :QUARTER], e_scales[:, :QUARTER], e_first[0][:], E5M2)
+        quantize(e_codes[:, QUARTER:HALF], e_scales[:, QUARTER:HALF], e_first[1][:], E5M2)
+        quantize(mf_codes[1][:], mf_scales[1][:], mf_bf1[:], E4M3)
+        q_second = shared.tile([P, HALF, PACK], BF16, name="q_second", offset=12288 + 256 - 2048, align_bytes=64)
+        weave(q_second[:], q_rest[:])
+        q_codes[HALF] = keep.tile([P, HALF], U32, name="q_codes_second", tag="e_first%d" % QUARTER, align_bytes=64)
         quantize(q_codes[HALF][:], q_scales[:, HALF:], q_second[:], E4M3)
 
-        def back(j, pool):
+        def back(j, b):
+            acc = bank(b)
             cols = slice((j % 2) * P, (j % 2 + 1) * P)
-            acc = pool.tile([P, PAIRS], F32, name="acc", tag="bank")
             nc.tensor.matmul_mx(
                 out=acc[:],
-                lhsT=mf_codes[j // 2][:, cols].bitcast(E4M3),
-                lhsT_scale=mf_scales[j // 2][:, cols],
+                lhsT=(mf_codes[j][:] if j < 2 else late_codes[:, cols]).bitcast(E4M3),
+                lhsT_scale=mf_scales[j][:] if j < 2 else late_scales[:, cols],
                 rhs=e_codes[:].bitcast(E5M2),
                 rhs_scale=e_scales[:],
                 start=True,
@@ -214,37 +212,38 @@ def tile_attend_gtransr_E_kernel(tc, eT, M, rv, wi, cf, hoffs, toffs, out):
             nc.vector.tensor_copy(head_win[j % 3][:].indirect(heads[:, cols]), dd)
             nc.vector.tensor_copy(tail_win[j % 3][:].indirect(tails[:, cols]), dd)
 
-        early0 = back(0, psum_early)
+        early0 = back(0, 5)
         dd_early0 = keep.tile([P, HALF], F32, name="dd_early0")
         nc.scalar.copy(dd_early0[:], early0[:, :HALF])
         put(0, dd_early0[:], slice(0, HALF_COLS))
-        project(HALF, PAIRS)
-        early1 = back(1, psum_early)
+        project(HALF, PAIRS, (1, 2, 3, 6))
+        early1 = back(1, 5)
         dd_early1 = keep.tile([P, HALF], F32, name="dd_early1")
         nc.scalar.copy(dd_early1[:], early1[:, :HALF])
         nc.vector.tensor_copy(head_win[1][:].indirect(heads[:, :HALF_COLS]), dd_early1[:])
 
-        turn(1)
-        mf_codes.append(keep.tile([P, 2 * P], U32, name="mf_codes1", align_bytes=64))
-        quantize(mf_codes[1][:], mf_scales[1][:], mf_bf[1][:], E4M3)
-        e_f32 = keep.tile([P, PACK, HALF], F32, name="e_f32", tag="e_f32", align_bytes=64)
+        turned_late = turn(1, 0)
+        e_f32 = shared.tile([P, PACK, HALF], F32, name="e_f32", offset=20480, align_bytes=64)
         for t in range(PACK):
             nc.gpsimd.tensor_tensor(e_f32[:, t, :], affine[1][:, t, :], wi_sb[:, HALF:], ALU.mult)
         e_second = keep.tile([P, HALF, PACK], BF16, name="e_second", tag="e_bf1", align_bytes=64)
         weave(e_second[:], e_f32[:])
         quantize(e_codes[:, HALF:], e_scales[:, HALF:], e_second[:], E5M2)
-        dd_held1 = keep.tile([P, HALF], F32, name="dd_held1", tag="e_f32", align_bytes=64)
+        dd_held1 = shared.tile([P, HALF], F32, name="dd_held1", offset=20480, align_bytes=64)
         nc.scalar.copy(dd_held1[:], early1[:, :HALF])
         nc.vector.tensor_copy(tail_win[1][:].indirect(tails[:, :HALF_COLS]), dd_held1[:])
+        late_bf = shared.tile([P, 2, P, PACK], BF16, name="late_bf", offset=20480 + 1024, align_bytes=64)
+        nc.scalar.copy(late_bf[:], turned_late)
+        quantize(late_codes[:], late_scales[:], late_bf[:].rearrange("m e c t -> m (e c) t"), E4M3)
 
         dds = []
         for j in range(PACK):
-            acc = back(j, psum)
+            acc = back(j, (7, 1, 2, 3)[j])
             dds.append(keep.tile([P, PAIRS], F32, name="dd%d" % j))
             first = HALF if j < 2 else 0
             nc.scalar.copy(dds[j][:, first:], acc[:, first:])
         head_win.append(keep.tile([P, T], F32, name="head_win2", tag="e_bf1", align_bytes=64))
-        tail_win.append(keep.tile([P, T], F32, name="tail_win2", tag="mf_scales0", align_bytes=64))
+        tail_win.append(keep.tile([P, T], F32, name="tail_win2", tag="mf_scales1", align_bytes=64))
         nc.gpsimd.memset(head_win[2][:].bitcast(U32), 0)
         nc.gpsimd.memset(tail_win[2][:].bitcast(U32), 0)
         for j in range(PACK):

@@ -68,8 +68,9 @@ def tile_attend_gtransr_E_kernel(tc, eT, M, rv, wi, cf, hoffs, toffs, out):
         tail_win = [keep.tile([P, T], F32, name="tail_win0")]
         nc.vector.memset(head_win[0][:].bitcast(U32), 0)
         nc.vector.memset(tail_win[0][:].bitcast(U32), 0)
-        head_win.append(keep.tile([P, T], F32, name="head_win1"))
-        tail_win.append(keep.tile([P, T], F32, name="tail_win1"))
+        for w in (1, 2):
+            head_win.append(keep.tile([P, T], F32, name="head_win%d" % w))
+            tail_win.append(keep.tile([P, T], F32, name="tail_win%d" % w))
 
         e_codes = keep.tile([P, PAIRS], U32, name="e_codes", align_bytes=64)
         e_scales = keep.tile([P, PAIRS], U8, name="e_scales", tag="e_scales", align_bytes=64)
@@ -78,8 +79,9 @@ def tile_attend_gtransr_E_kernel(tc, eT, M, rv, wi, cf, hoffs, toffs, out):
         nc.gpsimd.memset(e_codes[:, HALF:], 0)
         nc.gpsimd.memset(e_scales[:, HALF:].bitcast(U32), 0)
 
-        nc.gpsimd.memset(head_win[1][:].bitcast(U32), 0)
-        nc.gpsimd.memset(tail_win[1][:].bitcast(U32), 0)
+        for w in (1, 2):
+            nc.gpsimd.memset(head_win[w][:].bitcast(U32), 0)
+            nc.gpsimd.memset(tail_win[w][:].bitcast(U32), 0)
 
         cf2 = keep.tile([P, PACK], F32, name="cf2")
         rv_cf2 = keep.tile([P, PACK], F32, name="rv_cf2")
@@ -242,10 +244,6 @@ def tile_attend_gtransr_E_kernel(tc, eT, M, rv, wi, cf, hoffs, toffs, out):
             dds.append(keep.tile([P, PAIRS], F32, name="dd%d" % j))
             first = HALF if j < 2 else 0
             nc.scalar.copy(dds[j][:, first:], acc[:, first:])
-        head_win.append(keep.tile([P, T], F32, name="head_win2", tag="e_bf1", align_bytes=64))
-        tail_win.append(keep.tile([P, T], F32, name="tail_win2", tag="mf_scales1", align_bytes=64))
-        nc.gpsimd.memset(head_win[2][:].bitcast(U32), 0)
-        nc.gpsimd.memset(tail_win[2][:].bitcast(U32), 0)
         for j in range(PACK):
             first = HALF if j < 2 else 0
             put(j, dds[j][:, first:], slice(first // 16, LIST_COLS))

@@ -65,12 +65,10 @@ def tile_attend_gtransr_E_kernel(tc, eT, M, rv, wi, cf, hoffs, toffs, out):
         make_identity(nc, ident[:])
 
         head_win = [keep.tile([P, T], F32, name="head_win0")]
-        tail_win = [keep.tile([P, T], F32, name="tail_win0")]
         nc.vector.memset(head_win[0][:].bitcast(U32), 0)
-        nc.vector.memset(tail_win[0][:].bitcast(U32), 0)
         for w in (1, 2):
             head_win.append(keep.tile([P, T], F32, name="head_win%d" % w))
-            tail_win.append(keep.tile([P, T], F32, name="tail_win%d" % w))
+        tail_win = [keep.tile([P, T], F32, name="tail_win%d" % w) for w in range(2)]
 
         e_codes = keep.tile([P, PAIRS], U32, name="e_codes", align_bytes=64)
         e_scales = keep.tile([P, PAIRS], U8, name="e_scales", tag="e_scales", align_bytes=64)
@@ -79,9 +77,8 @@ def tile_attend_gtransr_E_kernel(tc, eT, M, rv, wi, cf, hoffs, toffs, out):
         nc.gpsimd.memset(e_codes[:, HALF:], 0)
         nc.gpsimd.memset(e_scales[:, HALF:].bitcast(U32), 0)
 
-        for w in (1, 2):
-            nc.gpsimd.memset(head_win[w][:].bitcast(U32), 0)
-            nc.gpsimd.memset(tail_win[w][:].bitcast(U32), 0)
+        for win in head_win[1:] + tail_win:
+            nc.gpsimd.memset(win[:].bitcast(U32), 0)
 
         cf2 = keep.tile([P, PACK], F32, name="cf2")
         rv_cf2 = keep.tile([P, PACK], F32, name="rv_cf2")
@@ -180,8 +177,6 @@ def tile_attend_gtransr_E_kernel(tc, eT, M, rv, wi, cf, hoffs, toffs, out):
         quantize(mf_codes[0][:], mf_scales[0][:], mf_bf0[:], E4M3)
         for lo, hi in quarters:
             project(lo, hi, (0, 1, 2, 3))
-        mf_bf1 = shared.tile([P, P, PACK], BF16, name="mf_bf1", offset=12288 + 256, align_bytes=64)
-        nc.scalar.copy(mf_bf1[:], turned[:, 1])
         last_tails = pick_tails(3, 1, shared.tile([P, HALF], F32, name="last_tails", offset=1024, align_bytes=64))
         subtract(3, HALF, PAIRS, q_rest[:, 3, :], last_tails[:])
 
@@ -190,11 +185,13 @@ def tile_attend_gtransr_E_kernel(tc, eT, M, rv, wi, cf, hoffs, toffs, out):
             weigh(lo, hi, e_bf[:])
         quantize(e_codes[:, :QUARTER], e_scales[:, :QUARTER], e_first[0][:], E5M2)
         quantize(e_codes[:, QUARTER:HALF], e_scales[:, QUARTER:HALF], e_first[1][:], E5M2)
-        quantize(mf_codes[1][:], mf_scales[1][:], mf_bf1[:], E4M3)
         q_second = shared.tile([P, HALF, PACK], BF16, name="q_second", offset=12288 + 256 - 2048, align_bytes=64)
         weave(q_second[:], q_rest[:])
         q_codes[HALF] = keep.tile([P, HALF], U32, name="q_codes_second", tag="e_first%d" % QUARTER, align_bytes=64)
         quantize(q_codes[HALF][:], q_scales[:, HALF:], q_second[:], E4M3)
+        mf_bf1 = shared.tile([P, P, PACK], BF16, name="mf_bf1", offset=12288 + 256, align_bytes=64)
+        nc.scalar.copy(mf_bf1[:], turned[:, 1])
+        quantize(mf_codes[1][:], mf_scales[1][:], mf_bf1[:], E4M3)
 
         def back(j, b):
             acc = bank(b)
@@ -212,7 +209,7 @@ def tile_attend_gtransr_E_kernel(tc, eT, M, rv, wi, cf, hoffs, toffs, out):
 
         def put(j, dd, cols):
             nc.vector.tensor_copy(head_win[j % 3][:].indirect(heads[:, cols]), dd)
-            nc.vector.tensor_copy(tail_win[j % 3][:].indirect(tails[:, cols]), dd)
+            nc.vector.tensor_copy(tail_win[j % 2][:].indirect(tails[:, cols]), dd)
 
         early0 = back(0, 5)
         dd_early0 = keep.tile([P, HALF], F32, name="dd_early0")
@@ -224,7 +221,10 @@ def tile_attend_gtransr_E_kernel(tc, eT, M, rv, wi, cf, hoffs, toffs, out):
         nc.scalar.copy(dd_early1[:], early1[:, :HALF])
         nc.vector.tensor_copy(head_win[1][:].indirect(heads[:, :HALF_COLS]), dd_early1[:])
 
-        turned_late = turn(1, 0)
+        turned_late = turn(1, 1)
+        late_bf = keep.tile([P, 2, P, PACK], BF16, name="late_bf", align_bytes=64)
+        nc.scalar.copy(late_bf[:], turned_late)
+        quantize(late_codes[:], late_scales[:], late_bf[:].rearrange("m e c t -> m (e c) t"), E4M3)
         e_f32 = shared.tile([P, PACK, HALF], F32, name="e_f32", offset=20480, align_bytes=64)
         for t in range(PACK):
             nc.gpsimd.tensor_tensor(e_f32[:, t, :], affine[1][:, t, :], wi_sb[:, HALF:], ALU.mult)
@@ -234,9 +234,6 @@ def tile_attend_gtransr_E_kernel(tc, eT, M, rv, wi, cf, hoffs, toffs, out):
         dd_held1 = shared.tile([P, HALF], F32, name="dd_held1", offset=20480, align_bytes=64)
         nc.scalar.copy(dd_held1[:], early1[:, :HALF])
         nc.vector.tensor_copy(tail_win[1][:].indirect(tails[:, :HALF_COLS]), dd_held1[:])
-        late_bf = shared.tile([P, 2, P, PACK], BF16, name="late_bf", offset=20480 + 1024, align_bytes=64)
-        nc.scalar.copy(late_bf[:], turned_late)
-        quantize(late_codes[:], late_scales[:], late_bf[:].rearrange("m e c t -> m (e c) t"), E4M3)
 
         dds = []
         for j in range(PACK):
@@ -251,10 +248,10 @@ def tile_attend_gtransr_E_kernel(tc, eT, M, rv, wi, cf, hoffs, toffs, out):
             if j < PACK - 1:
                 for c in range(0, T, T // 2):
                     cols = slice(c, c + T // 2)
-                    nc.gpsimd.tensor_tensor(res[:, cols], head_win[j % 3][:, cols], tail_win[j % 3][:, cols], ALU.subtract)
+                    nc.gpsimd.tensor_tensor(res[:, cols], head_win[j % 3][:, cols], tail_win[j % 2][:, cols], ALU.subtract)
                     nc.sync.dma_start(out_rows[:, j, cols], res[:, cols])
             else:
                 for lo, hi in zip(TAIL_EDGES[:-1], TAIL_EDGES[1:]):
                     cols = slice(lo, hi)
-                    nc.vector.tensor_tensor(res[:, cols], head_win[j % 3][:, cols], tail_win[j % 3][:, cols], ALU.subtract)
+                    nc.vector.tensor_tensor(res[:, cols], head_win[j % 3][:, cols], tail_win[j % 2][:, cols], ALU.subtract)
                     nc.sync.dma_start(out_rows[:, j, cols], res[:, cols])

@@ -52,13 +52,13 @@ def tile_attend_gtransr_E_kernel(tc, eT, M, rv, wi, cf, hoffs, toffs, out):
         nc.sync.dma_start(table[0][:], e_rows[:, 0, :])
         nc.sync.dma_start(tails[:], toffs)
         nc.sync.dma_start(heads[:], hoffs)
-        nc.sync.dma_start(cf_sb[:], cf.rearrange("(p t) o -> p (t o)", t=PACK))
-        nc.sync.dma_start(rv_sb[:], rv.rearrange("(p t) o -> p (t o)", t=PACK))
         for j in range(1, PACK):
             nc.sync.dma_start(table[j][:], e_rows[:, j, :])
         m_rows = M.rearrange("(p j) f -> p j f", j=PACK)
         for h in range(2):
             nc.sync.dma_start(m_raw[h][:], m_rows[:, :, h * (F // 2) : (h + 1) * (F // 2)])
+        nc.sync.dma_start(cf_sb[:], cf.rearrange("(p t) o -> p (t o)", t=PACK))
+        nc.sync.dma_start(rv_sb[:], rv.rearrange("(p t) o -> p (t o)", t=PACK))
         nc.sync.dma_start(wi_sb[:], wi)
 
         ident = keep.tile([P, P], F32, name="ident")
@@ -82,8 +82,6 @@ def tile_attend_gtransr_E_kernel(tc, eT, M, rv, wi, cf, hoffs, toffs, out):
 
         cf2 = keep.tile([P, PACK], F32, name="cf2")
         rv_cf2 = keep.tile([P, PACK], F32, name="rv_cf2")
-        nc.gpsimd.tensor_tensor(cf2[:], cf_sb[:], cf_sb[:], ALU.mult)
-        nc.gpsimd.tensor_tensor(rv_cf2[:], rv_sb[:], cf2[:], ALU.mult)
 
         def pick_tails(j, h, picked):
             nc.vector.tensor_copy(picked[:], table[j][:].indirect(tails[:, h * HALF_COLS : (h + 1) * HALF_COLS]))
@@ -163,6 +161,7 @@ def tile_attend_gtransr_E_kernel(tc, eT, M, rv, wi, cf, hoffs, toffs, out):
             subtract(3, lo, hi, q_first[:, 3, lo:hi], picked[:, lo:hi])
         nc.scalar.copy(md_view[:, : P // 2], m_raw[0][:].rearrange("p j (m t) -> p m j t", t=PACK))
         nc.vector.tensor_copy(md_view[:, P // 2 :], m_raw[1][:].rearrange("p j (m t) -> p m j t", t=PACK))
+        nc.vector.tensor_tensor(cf2[:], cf_sb[:], cf_sb[:], ALU.mult)
         turned = turn(0, 4)
         q_bf = []
         for c, (lo, hi) in enumerate(quarters):
@@ -172,11 +171,12 @@ def tile_attend_gtransr_E_kernel(tc, eT, M, rv, wi, cf, hoffs, toffs, out):
             quantize_md(c)
             q_codes[lo] = shared.tile([P, QUARTER], U32, name="q_codes%d" % c, offset=8192 + 4096 * c, align_bytes=64)
             quantize(q_codes[lo][:], q_scales[:, lo:hi], q_bf[c][:], E4M3)
+        nc.vector.tensor_tensor(rv_cf2[:], rv_sb[:], cf2[:], ALU.mult)
         mf_bf0 = keep.tile([P, P, PACK], BF16, name="mf_bf0", align_bytes=64)
         nc.scalar.copy(mf_bf0[:], turned[:, 0])
         quantize(mf_codes[0][:], mf_scales[0][:], mf_bf0[:], E4M3)
-        for lo, hi in quarters:
-            project(lo, hi, (0, 1, 2, 3))
+        project(0, QUARTER, (0, 1, 2, 3))
+        project(QUARTER, HALF, (5, 6, 7, 0))
         last_tails = pick_tails(3, 1, shared.tile([P, HALF], F32, name="last_tails", offset=1024, align_bytes=64))
         subtract(3, HALF, PAIRS, q_rest[:, 3, :], last_tails[:])
 
@@ -211,17 +211,17 @@ def tile_attend_gtransr_E_kernel(tc, eT, M, rv, wi, cf, hoffs, toffs, out):
             nc.vector.tensor_copy(head_win[j % 3][:].indirect(heads[:, cols]), dd)
             nc.vector.tensor_copy(tail_win[j % 2][:].indirect(tails[:, cols]), dd)
 
-        early0 = back(0, 5)
+        early0 = back(0, 1)
         dd_early0 = keep.tile([P, HALF], F32, name="dd_early0")
         nc.scalar.copy(dd_early0[:], early0[:, :HALF])
         put(0, dd_early0[:], slice(0, HALF_COLS))
-        project(HALF, PAIRS, (1, 2, 3, 6))
-        early1 = back(1, 5)
+        project(HALF, PAIRS, (2, 3, 5, 6))
+        early1 = back(1, 1)
         dd_early1 = keep.tile([P, HALF], F32, name="dd_early1")
         nc.scalar.copy(dd_early1[:], early1[:, :HALF])
         nc.vector.tensor_copy(head_win[1][:].indirect(heads[:, :HALF_COLS]), dd_early1[:])
 
-        turned_late = turn(1, 1)
+        turned_late = turn(1, 2)
         late_bf = keep.tile([P, 2, P, PACK], BF16, name="late_bf", align_bytes=64)
         nc.scalar.copy(late_bf[:], turned_late)
         quantize(late_codes[:], late_scales[:], late_bf[:].rearrange("m e c t -> m (e c) t"), E4M3)
@@ -237,7 +237,7 @@ def tile_attend_gtransr_E_kernel(tc, eT, M, rv, wi, cf, hoffs, toffs, out):
 
         dds = []
         for j in range(PACK):
-            acc = back(j, (7, 1, 2, 3)[j])
+            acc = back(j, (7, 0, 2, 3)[j])
             dds.append(keep.tile([P, PAIRS], F32, name="dd%d" % j))
             first = HALF if j < 2 else 0
             nc.scalar.copy(dds[j][:, first:], acc[:, first:])

@@ -20,9 +20,8 @@ F = 512
 PAIRS = 512
 T = 2048
 HALF = PAIRS // 2
-QUARTER = PAIRS // 4
+HALVES = ((0, HALF), (HALF, PAIRS))
 LIST_COLS = PAIRS // 16
-HALF_COLS = LIST_COLS // 2
 TAIL_EDGES = (0, 256, 768, 1280, 1792, 2048)
 
 FLOPS = 2 * 2 * D * F * PAIRS
@@ -44,214 +43,170 @@ def tile_attend_gtransr_E_kernel(tc, eT, M, rv, wi, cf, hoffs, toffs, out):
         e_rows = eT.rearrange("(p j) n -> p j n", j=PACK)
         out_rows = out.rearrange("(p j) n -> p j n", j=PACK)
         table = [keep.tile([P, T], F32, name="table%d" % j) for j in range(PACK)]
-        m_raw = [shared.tile([P, PACK, F // 2], F32, name="m_raw%d" % h, offset=4096 * h, align_bytes=64) for h in range(2)]
+        m_raw = keep.tile([P, PACK, F], F32, name="m_raw")
         wi_sb = keep.tile([P, PAIRS], F32, name="wi_sb")
         rv_sb = keep.tile([P, PACK], F32, name="rv_sb")
         cf_sb = keep.tile([P, PACK], F32, name="cf_sb")
 
-        nc.sync.dma_start(table[0][:], e_rows[:, 0, :])
+        nc.sync.dma_start(m_raw[:], M.rearrange("(p j) f -> p j f", j=PACK))
         nc.sync.dma_start(tails[:], toffs)
         nc.sync.dma_start(heads[:], hoffs)
-        for j in range(1, PACK):
+        nc.scalar.dma_start(cf_sb[:], cf.rearrange("(p t) o -> p (t o)", t=PACK))
+        nc.scalar.dma_start(rv_sb[:], rv.rearrange("(p t) o -> p (t o)", t=PACK))
+        for j in range(PACK):
             nc.sync.dma_start(table[j][:], e_rows[:, j, :])
-        m_rows = M.rearrange("(p j) f -> p j f", j=PACK)
-        for h in range(2):
-            nc.sync.dma_start(m_raw[h][:], m_rows[:, :, h * (F // 2) : (h + 1) * (F // 2)])
-        nc.sync.dma_start(cf_sb[:], cf.rearrange("(p t) o -> p (t o)", t=PACK))
-        nc.sync.dma_start(rv_sb[:], rv.rearrange("(p t) o -> p (t o)", t=PACK))
         nc.sync.dma_start(wi_sb[:], wi)
 
         ident = keep.tile([P, P], F32, name="ident")
         make_identity(nc, ident[:])
 
-        head_win = [keep.tile([P, T], F32, name="head_win0")]
-        nc.vector.memset(head_win[0][:].bitcast(U32), 0)
-        for w in (1, 2):
-            head_win.append(keep.tile([P, T], F32, name="head_win%d" % w))
+        head_win = [keep.tile([P, T], F32, name="head_win%d" % w) for w in range(2)]
         tail_win = [keep.tile([P, T], F32, name="tail_win%d" % w) for w in range(2)]
-
-        e_codes = keep.tile([P, PAIRS], U32, name="e_codes", align_bytes=64)
-        e_scales = keep.tile([P, PAIRS], U8, name="e_scales", tag="e_scales", align_bytes=64)
-        zeros = keep.tile([P, QUARTER], F32, name="zeros")
-        nc.gpsimd.memset(zeros[:].bitcast(U32), 0)
-        nc.gpsimd.memset(e_codes[:, HALF:], 0)
-        nc.gpsimd.memset(e_scales[:, HALF:].bitcast(U32), 0)
-
-        for win in head_win[1:] + tail_win:
-            nc.gpsimd.memset(win[:].bitcast(U32), 0)
+        for win in head_win + tail_win:
+            nc.vector.memset(win[:].bitcast(U32), 0)
 
         cf2 = keep.tile([P, PACK], F32, name="cf2")
         rv_cf2 = keep.tile([P, PACK], F32, name="rv_cf2")
 
-        def pick_tails(j, h, picked):
-            nc.vector.tensor_copy(picked[:], table[j][:].indirect(tails[:, h * HALF_COLS : (h + 1) * HALF_COLS]))
-            return picked
+        def entries(offsets, lo, hi):
+            return offsets[:, lo // 16 : hi // 16]
 
-        def subtract(j, lo, hi, q_out, picked):
-            nc.vector.tensor_tensor(q_out, table[j][:].indirect(heads[:, lo // 16 : hi // 16]), picked, ALU.subtract)
+        def woven(dst):
+            return dst.rearrange("p (c i) t -> p c t i", i=4)
 
-        def weave(dst, src):
-            nc.scalar.copy(dst.rearrange("p (c i) t -> p c t i", i=4), src.rearrange("p t (c i) -> p c t i", i=4))
+        def planes(src):
+            return src.rearrange("p t (c i) -> p c t i", i=4)
 
         def quantize(codes, scales, src, fmt):
             nc.vector.quantize_mx(codes.bitcast(fmt), scales, src.rearrange("p i t -> p (i t)"))
 
-        md_bf = keep.tile([P, PACK, P, PACK], BF16, name="md_bf", align_bytes=64)
+        md_bf = shared.tile([P, PACK, P, PACK], BF16, name="md_bf", offset=0, align_bytes=64)
         md_codes = keep.tile([P, F], U32, name="md_codes", align_bytes=64)
         md_scales = keep.tile([P, F], U8, name="md_scales", align_bytes=64)
         md_view = md_bf[:].rearrange("p t m j -> p m j t")
-        md_words = md_bf[:].rearrange("p t m j -> p (t m j)").bitcast(F32).rearrange("p (t m a) -> p t m a", t=PACK, a=2)
-        mf_codes = [keep.tile([P, P], U32, name="mf_codes%d" % j, align_bytes=64) for j in range(2)]
-        mf_scales = [keep.tile([P, P], U8, name="mf_scales%d" % j, tag="mf_scales%d" % j, align_bytes=64) for j in range(2)]
-        late_codes = keep.tile([P, 2 * P], U32, name="late_codes", align_bytes=64)
-        late_scales = keep.tile([P, 2 * P], U8, name="late_scales", align_bytes=64)
+        m_view = m_raw[:].rearrange("p j (m t) -> p m j t", t=PACK)
+        nc.scalar.copy(md_view[:, : P // 2], m_view[:, : P // 2])
+        nc.vector.tensor_copy(md_view[:, P // 2 :], m_view[:, P // 2 :])
+        nc.vector.tensor_tensor(cf2[:], cf_sb[:], cf_sb[:], ALU.mult)
+        quantize(md_codes[:], md_scales[:], md_bf[:].rearrange("p t m j -> p (t m) j"), E4M3)
+        nc.vector.tensor_tensor(rv_cf2[:], rv_sb[:], cf2[:], ALU.mult)
 
-        def turn(a, b):
-            turned = bank(b)
+        md_words = md_bf[:].rearrange("p t m j -> p (t m j)").bitcast(F32).rearrange("p (t m a) -> p t m a", t=PACK, a=2)
+        mf_bf = shared.tile([P, PACK, P, PACK], BF16, name="mf_bf", offset=6144, align_bytes=64)
+        mf_codes = keep.tile([P, D], U32, name="mf_codes", align_bytes=64)
+        mf_scales = keep.tile([P, D], U8, name="mf_scales", align_bytes=64)
+        for a in range(2):
+            turned = bank(4 + a)
             for t in range(PACK):
                 nc.tensor.transpose(turned[:, t * P : (t + 1) * P], md_words[:, t, :, a], ident[:])
-            return turned[:].bitcast(BF16).rearrange("m (t c e) -> m e c t", t=PACK, e=2)
+            nc.scalar.copy(mf_bf[:, 2 * a : 2 * a + 2], turned[:].bitcast(BF16).rearrange("m (t c e) -> m e c t", t=PACK, e=2))
+        quantize(mf_codes[:], mf_scales[:], mf_bf[:].rearrange("m j c t -> m (j c) t"), E4M3)
 
-        quarters = ((0, QUARTER), (QUARTER, HALF))
-        q_first = keep.tile([P, PACK, HALF], F32, name="q_first")
-        q_rest = shared.tile([P, PACK, HALF], F32, name="q_rest", offset=16384, align_bytes=64)
-        q_codes = {}
+        head_win.append(shared.tile([P, T], F32, name="head_win2", offset=0))
+        tail_win.append(shared.tile([P, T], F32, name="tail_win2", offset=8192))
+        for win in (head_win[2], tail_win[2]):
+            nc.gpsimd.memset(win[:].bitcast(U32), 0)
+
+        q_f32 = keep.tile([P, PACK, PAIRS], F32, name="q_f32")
+
+        def pick(j, lo, hi):
+            picked = keep.tile([P, hi - lo], F32, name="picked%d_%d" % (j, lo))
+            nc.scalar.activation(picked[:], table[j][:].indirect(entries(tails, lo, hi)), ACT.Copy)
+            nc.vector.tensor_tensor(q_f32[:, j, lo:hi], table[j][:].indirect(entries(heads, lo, hi)), picked[:], ALU.subtract)
+
+        for j in range(PACK - 1):
+            pick(j, 0, PAIRS)
+
+        q_codes = keep.tile([P, PAIRS], U32, name="q_codes", align_bytes=64)
         q_scales = keep.tile([P, PAIRS], U8, name="q_scales", align_bytes=64)
-        affine = [keep.tile([P, PACK, HALF], F32, name="affine%d" % h, align_bytes=64) for h in range(2)]
+        e_codes = keep.tile([P, PAIRS], U32, name="e_codes", align_bytes=64)
+        e_scales = keep.tile([P, PAIRS], U8, name="e_scales", align_bytes=64)
+        q_bf = [keep.tile([P, HALF, PACK], BF16, name="q_bf%d" % h, align_bytes=64) for h in range(2)]
+        e_bf = [keep.tile([P, HALF, PACK], BF16, name="e_bf%d" % h, align_bytes=64) for h in range(2)]
+        affine = [keep.tile([P, PACK, HALF], F32, name="affine%d" % h) for h in range(2)]
 
-        def gather_early(j, q_out):
-            both = [pick_tails(j, h, keep.tile([P, HALF], F32, name="picked", tag="picked%d" % h)) for h in range(2)]
-            subtract(j, 0, HALF, q_first[:, j, :], both[0][:])
-            subtract(j, HALF, PAIRS, q_out, both[1][:])
-
-        def project(lo, hi, banks):
+        def project(h):
+            lo, hi = HALVES[h]
+            quantize(q_codes[:, lo:hi], q_scales[:, lo:hi], q_bf[h][:], E4M3)
             for t in range(PACK):
                 cols = slice(t * P, (t + 1) * P)
-                u = bank(banks[t])
+                u = bank(PACK * h + t)
                 nc.tensor.matmul_mx(
-                    out=u[:, : hi - lo],
+                    out=u[:, :HALF],
                     lhsT=md_codes[:, cols].bitcast(E4M3),
                     lhsT_scale=md_scales[:, cols],
-                    rhs=q_codes[lo][:].bitcast(E4M3),
+                    rhs=q_codes[:, lo:hi].bitcast(E4M3),
                     rhs_scale=q_scales[:, lo:hi],
                     start=True,
                     stop=True,
                 )
-                dst = affine[lo // HALF][:, t, lo % HALF : lo % HALF + hi - lo]
-                nc.scalar.activation(dst, u[:, : hi - lo], ACT.Identity, bias=rv_cf2[:, t : t + 1], scale=cf2[:, t : t + 1])
+                nc.scalar.activation(affine[h][:, t, :], u[:, :HALF], ACT.Identity, bias=rv_cf2[:, t : t + 1], scale=cf2[:, t : t + 1])
 
-        def weigh(lo, hi, e_bf):
+        def weigh(h):
+            lo, hi = HALVES[h]
             nc.vector.tensor_tensor(
-                e_bf.rearrange("p (c i) t -> p c t i", i=4),
-                affine[0][:, :, lo:hi].rearrange("p t (c i) -> p c t i", i=4),
-                wi_sb[:, lo:hi].rearrange("p (c i) -> p c i", i=4).unsqueeze(2).to_broadcast([P, (hi - lo) // 4, PACK, 4]),
+                woven(e_bf[h][:]),
+                planes(affine[h][:]),
+                wi_sb[:, lo:hi].rearrange("p (c i) -> p c i", i=4).unsqueeze(2).to_broadcast([P, HALF // 4, PACK, 4]),
                 ALU.mult,
             )
 
-        def quantize_md(a):
-            cols = slice(a * HALF, (a + 1) * HALF)
-            quantize(md_codes[:, cols], md_scales[:, cols], md_bf[:, 2 * a : 2 * a + 2].rearrange("p t m j -> p (t m) j"), E4M3)
-
-        for j in range(PACK - 1):
-            gather_early(j, q_rest[:, j, :])
-        picked = keep.tile([P, HALF], F32, name="picked_last")
-        for lo, hi in quarters:
-            nc.vector.tensor_tensor(picked[:, lo:hi], table[3][:].indirect(tails[:, lo // 16 : hi // 16]), zeros[:], ALU.subtract)
-        for lo, hi in quarters:
-            subtract(3, lo, hi, q_first[:, 3, lo:hi], picked[:, lo:hi])
-        nc.scalar.copy(md_view[:, : P // 2], m_raw[0][:].rearrange("p j (m t) -> p m j t", t=PACK))
-        nc.vector.tensor_copy(md_view[:, P // 2 :], m_raw[1][:].rearrange("p j (m t) -> p m j t", t=PACK))
-        nc.vector.tensor_tensor(cf2[:], cf_sb[:], cf_sb[:], ALU.mult)
-        turned = turn(0, 4)
-        q_bf = []
-        for c, (lo, hi) in enumerate(quarters):
-            q_bf.append(shared.tile([P, QUARTER, PACK], BF16, name="q_bf%d" % c, offset=1024 * c, align_bytes=64))
-            weave(q_bf[c][:], q_first[:, :, lo:hi])
-        for c, (lo, hi) in enumerate(quarters):
-            quantize_md(c)
-            q_codes[lo] = shared.tile([P, QUARTER], U32, name="q_codes%d" % c, offset=8192 + 4096 * c, align_bytes=64)
-            quantize(q_codes[lo][:], q_scales[:, lo:hi], q_bf[c][:], E4M3)
-        nc.vector.tensor_tensor(rv_cf2[:], rv_sb[:], cf2[:], ALU.mult)
-        mf_bf0 = keep.tile([P, P, PACK], BF16, name="mf_bf0", align_bytes=64)
-        nc.scalar.copy(mf_bf0[:], turned[:, 0])
-        quantize(mf_codes[0][:], mf_scales[0][:], mf_bf0[:], E4M3)
-        project(0, QUARTER, (0, 1, 2, 3))
-        project(QUARTER, HALF, (5, 6, 7, 0))
-        last_tails = pick_tails(3, 1, shared.tile([P, HALF], F32, name="last_tails", offset=1024, align_bytes=64))
-        subtract(3, HALF, PAIRS, q_rest[:, 3, :], last_tails[:])
-
-        e_first = [keep.tile([P, QUARTER, PACK], BF16, name="e_first", tag="e_first%d" % lo, align_bytes=64) for lo, hi in quarters]
-        for (lo, hi), e_bf in zip(quarters, e_first):
-            weigh(lo, hi, e_bf[:])
-        quantize(e_codes[:, :QUARTER], e_scales[:, :QUARTER], e_first[0][:], E5M2)
-        quantize(e_codes[:, QUARTER:HALF], e_scales[:, QUARTER:HALF], e_first[1][:], E5M2)
-        q_second = shared.tile([P, HALF, PACK], BF16, name="q_second", offset=12288 + 256 - 2048, align_bytes=64)
-        weave(q_second[:], q_rest[:])
-        q_codes[HALF] = keep.tile([P, HALF], U32, name="q_codes_second", tag="e_first%d" % QUARTER, align_bytes=64)
-        quantize(q_codes[HALF][:], q_scales[:, HALF:], q_second[:], E4M3)
-        mf_bf1 = shared.tile([P, P, PACK], BF16, name="mf_bf1", offset=12288 + 256, align_bytes=64)
-        nc.scalar.copy(mf_bf1[:], turned[:, 1])
-        quantize(mf_codes[1][:], mf_scales[1][:], mf_bf1[:], E4M3)
-
-        def back(j, b):
+        def back(j, lo, hi, b):
             acc = bank(b)
-            cols = slice((j % 2) * P, (j % 2 + 1) * P)
+            cols = slice(j * P, (j + 1) * P)
             nc.tensor.matmul_mx(
-                out=acc[:],
-                lhsT=(mf_codes[j][:] if j < 2 else late_codes[:, cols]).bitcast(E4M3),
-                lhsT_scale=mf_scales[j][:] if j < 2 else late_scales[:, cols],
-                rhs=e_codes[:].bitcast(E5M2),
-                rhs_scale=e_scales[:],
+                out=acc[:, : hi - lo],
+                lhsT=mf_codes[:, cols].bitcast(E4M3),
+                lhsT_scale=mf_scales[:, cols],
+                rhs=e_codes[:, lo:hi].bitcast(E5M2),
+                rhs_scale=e_scales[:, lo:hi],
                 start=True,
                 stop=True,
             )
-            return acc
+            return acc[:, : hi - lo]
 
-        def put(j, dd, cols):
-            nc.vector.tensor_copy(head_win[j % 3][:].indirect(heads[:, cols]), dd)
-            nc.vector.tensor_copy(tail_win[j % 2][:].indirect(tails[:, cols]), dd)
+        pick(3, 0, HALF)
+        nc.vector.tensor_copy(woven(q_bf[0][:]), planes(q_f32[:, :, :HALF]))
+        pick(3, HALF, PAIRS)
+        nc.scalar.copy(woven(q_bf[1][:]), planes(q_f32[:, :, HALF:]))
+        project(0)
+        project(1)
+        weigh(0)
+        quantize(e_codes[:, :HALF], e_scales[:, :HALF], e_bf[0][:], E5M2)
+        weigh(1)
+        dd = [keep.tile([P, PAIRS], F32, name="dd%d" % j) for j in range(PACK)]
+        nc.scalar.copy(dd[0][:, :HALF], back(0, 0, HALF, 0))
+        quantize(e_codes[:, HALF:], e_scales[:, HALF:], e_bf[1][:], E5M2)
 
-        early0 = back(0, 1)
-        dd_early0 = keep.tile([P, HALF], F32, name="dd_early0")
-        nc.scalar.copy(dd_early0[:], early0[:, :HALF])
-        put(0, dd_early0[:], slice(0, HALF_COLS))
-        project(HALF, PAIRS, (2, 3, 5, 6))
-        early1 = back(1, 1)
-        dd_early1 = keep.tile([P, HALF], F32, name="dd_early1")
-        nc.scalar.copy(dd_early1[:], early1[:, :HALF])
-        nc.vector.tensor_copy(head_win[1][:].indirect(heads[:, :HALF_COLS]), dd_early1[:])
+        def put_heads(j, lo, hi):
+            nc.vector.tensor_copy(head_win[j % 3][:].indirect(entries(heads, lo, hi)), dd[j][:, lo:hi])
 
-        turned_late = turn(1, 2)
-        late_bf = keep.tile([P, 2, P, PACK], BF16, name="late_bf", align_bytes=64)
-        nc.scalar.copy(late_bf[:], turned_late)
-        quantize(late_codes[:], late_scales[:], late_bf[:].rearrange("m e c t -> m (e c) t"), E4M3)
-        e_f32 = shared.tile([P, PACK, HALF], F32, name="e_f32", offset=20480, align_bytes=64)
-        for t in range(PACK):
-            nc.gpsimd.tensor_tensor(e_f32[:, t, :], affine[1][:, t, :], wi_sb[:, HALF:], ALU.mult)
-        e_second = keep.tile([P, HALF, PACK], BF16, name="e_second", tag="e_bf1", align_bytes=64)
-        weave(e_second[:], e_f32[:])
-        quantize(e_codes[:, HALF:], e_scales[:, HALF:], e_second[:], E5M2)
-        dd_held1 = shared.tile([P, HALF], F32, name="dd_held1", offset=20480, align_bytes=64)
-        nc.scalar.copy(dd_held1[:], early1[:, :HALF])
-        nc.vector.tensor_copy(tail_win[1][:].indirect(tails[:, :HALF_COLS]), dd_held1[:])
+        def put_tails(j, lo, hi):
+            nc.scalar.activation(tail_win[j % 3][:].indirect(entries(tails, lo, hi)), dd[j][:, lo:hi], ACT.Copy)
 
-        dds = []
-        for j in range(PACK):
-            acc = back(j, (7, 0, 2, 3)[j])
-            dds.append(keep.tile([P, PAIRS], F32, name="dd%d" % j))
-            first = HALF if j < 2 else 0
-            nc.scalar.copy(dds[j][:, first:], acc[:, first:])
-        for j in range(PACK):
-            first = HALF if j < 2 else 0
-            put(j, dds[j][:, first:], slice(first // 16, LIST_COLS))
+        def leave(j, edges, engine):
             res = keep.tile([P, T], F32, name="res%d" % j)
-            if j < PACK - 1:
-                for c in range(0, T, T // 2):
-                    cols = slice(c, c + T // 2)
-                    nc.gpsimd.tensor_tensor(res[:, cols], head_win[j % 3][:, cols], tail_win[j % 2][:, cols], ALU.subtract)
-                    nc.sync.dma_start(out_rows[:, j, cols], res[:, cols])
+            for lo, hi in zip(edges[:-1], edges[1:]):
+                cols = slice(lo, hi)
+                engine.tensor_tensor(res[:, cols], head_win[j % 3][:, cols], tail_win[j % 3][:, cols], ALU.subtract)
+                nc.sync.dma_start(out_rows[:, j, cols], res[:, cols])
+
+        put_tails(0, 0, HALF)
+        put_heads(0, 0, HALF)
+        nc.scalar.copy(dd[0][:, HALF:], back(0, HALF, PAIRS, 1))
+        accs = [back(j, 0, PAIRS, 1 + j) for j in range(1, PACK)]
+        put_tails(0, HALF, PAIRS)
+        put_heads(0, HALF, PAIRS)
+        leave(0, (0, T // 2, T), nc.gpsimd)
+        for j in range(1, PACK):
+            if j == 2:
+                nc.vector.tensor_copy(dd[j][:], accs[j - 1])
             else:
-                for lo, hi in zip(TAIL_EDGES[:-1], TAIL_EDGES[1:]):
-                    cols = slice(lo, hi)
-                    nc.vector.tensor_tensor(res[:, cols], head_win[j % 3][:, cols], tail_win[j % 2][:, cols], ALU.subtract)
-                    nc.sync.dma_start(out_rows[:, j, cols], res[:, cols])
+                nc.scalar.copy(dd[j][:], accs[j - 1])
+            for lo, hi in HALVES:
+                put_tails(j, lo, hi)
+            put_heads(j, 0, PAIRS)
+            if j == 1:
+                leave(1, (0, T // 2, T), nc.gpsimd)
+        leave(2, (0, T // 2, T), nc.vector)
+        leave(3, TAIL_EDGES, nc.vector)

@@ -20,9 +20,13 @@ F = 512
 PAIRS = 512
 T = 2048
 HALF = PAIRS // 2
+QUARTER = PAIRS // 4
 HALVES = ((0, HALF), (HALF, PAIRS))
 LIST_COLS = PAIRS // 16
-TAIL_EDGES = (0, 256, 768, 1280, 1792, 2048)
+DEAL = 96
+FIRST_EDGES = (0, 256, 768, 1280, 2048)
+LAST_EDGES = (0, 768, 1280, 1792, 2048)
+POOL_EDGES = (0, 1024, 1536, 2048)
 
 FLOPS = 2 * 2 * D * F * PAIRS
 
@@ -62,8 +66,11 @@ def tile_attend_gtransr_E_kernel(tc, eT, M, rv, wi, cf, hoffs, toffs, out):
 
         head_win = [keep.tile([P, T], F32, name="head_win%d" % w) for w in range(2)]
         tail_win = [keep.tile([P, T], F32, name="tail_win%d" % w) for w in range(2)]
-        for win in head_win + tail_win:
-            nc.vector.memset(win[:].bitcast(U32), 0)
+        for win in head_win:
+            for cols in (slice(0, T // 2 - 1), slice(T // 2 - 1, T)):
+                nc.vector.memset(win[:, cols].bitcast(U32), 0)
+        for win in tail_win:
+            nc.gpsimd.memset(win[:].bitcast(U32), 0)
 
         cf2 = keep.tile([P, PACK], F32, name="cf2")
         rv_cf2 = keep.tile([P, PACK], F32, name="rv_cf2")
@@ -80,59 +87,81 @@ def tile_attend_gtransr_E_kernel(tc, eT, M, rv, wi, cf, hoffs, toffs, out):
         def quantize(codes, scales, src, fmt):
             nc.vector.quantize_mx(codes.bitcast(fmt), scales, src.rearrange("p i t -> p (i t)"))
 
-        md_bf = shared.tile([P, PACK, P, PACK], BF16, name="md_bf", offset=0, align_bytes=64)
+        md_bf = shared.tile([P, PACK, P, PACK], BF16, name="md_bf", offset=2048, align_bytes=64)
         md_codes = keep.tile([P, F], U32, name="md_codes", align_bytes=64)
         md_scales = keep.tile([P, F], U8, name="md_scales", align_bytes=64)
         md_view = md_bf[:].rearrange("p t m j -> p m j t")
         m_view = m_raw[:].rearrange("p j (m t) -> p m j t", t=PACK)
-        nc.scalar.copy(md_view[:, : P // 2], m_view[:, : P // 2])
-        nc.vector.tensor_copy(md_view[:, P // 2 :], m_view[:, P // 2 :])
+        nc.scalar.copy(md_view[:, :DEAL], m_view[:, :DEAL])
+        nc.vector.tensor_copy(md_view[:, DEAL:], m_view[:, DEAL:])
         nc.vector.tensor_tensor(cf2[:], cf_sb[:], cf_sb[:], ALU.mult)
         quantize(md_codes[:], md_scales[:], md_bf[:].rearrange("p t m j -> p (t m) j"), E4M3)
         nc.vector.tensor_tensor(rv_cf2[:], rv_sb[:], cf2[:], ALU.mult)
 
         md_words = md_bf[:].rearrange("p t m j -> p (t m j)").bitcast(F32).rearrange("p (t m a) -> p t m a", t=PACK, a=2)
-        mf_bf = shared.tile([P, PACK, P, PACK], BF16, name="mf_bf", offset=6144, align_bytes=64)
+        mf_bf = shared.tile([P, PACK, P, PACK], BF16, name="mf_bf", offset=8192, align_bytes=64)
         mf_codes = keep.tile([P, D], U32, name="mf_codes", align_bytes=64)
         mf_scales = keep.tile([P, D], U8, name="mf_scales", align_bytes=64)
-        for a in range(2):
+        for a, copy in enumerate((nc.vector.tensor_copy, nc.scalar.copy)):
             turned = bank(4 + a)
             for t in range(PACK):
                 nc.tensor.transpose(turned[:, t * P : (t + 1) * P], md_words[:, t, :, a], ident[:])
-            nc.scalar.copy(mf_bf[:, 2 * a : 2 * a + 2], turned[:].bitcast(BF16).rearrange("m (t c e) -> m e c t", t=PACK, e=2))
-        quantize(mf_codes[:], mf_scales[:], mf_bf[:].rearrange("m j c t -> m (j c) t"), E4M3)
+            copy(mf_bf[:, 2 * a : 2 * a + 2], turned[:].bitcast(BF16).rearrange("m (t c e) -> m e c t", t=PACK, e=2))
 
-        head_win.append(shared.tile([P, T], F32, name="head_win2", offset=0))
-        tail_win.append(shared.tile([P, T], F32, name="tail_win2", offset=8192))
-        for win in (head_win[2], tail_win[2]):
-            nc.gpsimd.memset(win[:].bitcast(U32), 0)
+        q_pairs = [
+            shared.tile([P, 2, PAIRS], F32, name="q_pair0", offset=0),
+            keep.tile([P, 2, PAIRS], F32, name="q_pair1"),
+        ]
+        whole = [
+            keep.tile([P, PAIRS], F32, name="picked0"),
+            shared.tile([P, PAIRS], F32, name="picked1", offset=4096),
+            keep.tile([P, PAIRS], F32, name="picked2"),
+        ]
+        whole.append(keep.tile([P, PAIRS], F32, name="picked3"))
 
-        q_f32 = keep.tile([P, PACK, PAIRS], F32, name="q_f32")
+        def picked(j, lo, hi):
+            return whole[j][:, lo:hi]
 
-        def pick(j, lo, hi):
-            picked = keep.tile([P, hi - lo], F32, name="picked%d_%d" % (j, lo))
-            nc.scalar.activation(picked[:], table[j][:].indirect(entries(tails, lo, hi)), ACT.Copy)
-            nc.vector.tensor_tensor(q_f32[:, j, lo:hi], table[j][:].indirect(entries(heads, lo, hi)), picked[:], ALU.subtract)
+        def pick_tails(j, lo, hi):
+            nc.scalar.activation(picked(j, lo, hi), table[j][:].indirect(entries(tails, lo, hi)), ACT.Copy)
 
-        for j in range(PACK - 1):
-            pick(j, 0, PAIRS)
+        def pick_heads(j, lo, hi):
+            nc.vector.tensor_tensor(
+                q_pairs[j // 2][:, j % 2, lo:hi], table[j][:].indirect(entries(heads, lo, hi)), picked(j, lo, hi), ALU.subtract
+            )
 
         q_codes = keep.tile([P, PAIRS], U32, name="q_codes", align_bytes=64)
         q_scales = keep.tile([P, PAIRS], U8, name="q_scales", align_bytes=64)
         e_codes = keep.tile([P, PAIRS], U32, name="e_codes", align_bytes=64)
         e_scales = keep.tile([P, PAIRS], U8, name="e_scales", align_bytes=64)
         q_bf = [keep.tile([P, HALF, PACK], BF16, name="q_bf%d" % h, align_bytes=64) for h in range(2)]
-        e_bf = [keep.tile([P, HALF, PACK], BF16, name="e_bf%d" % h, align_bytes=64) for h in range(2)]
-        affine = [keep.tile([P, PACK, HALF], F32, name="affine%d" % h) for h in range(2)]
+        e_bf = [
+            keep.tile([P, HALF, PACK], BF16, name="e_bf0", align_bytes=64),
+            shared.tile([P, HALF, PACK], BF16, name="e_bf1", offset=16384, align_bytes=64),
+        ]
+        affine = [
+            keep.tile([P, PACK, HALF], F32, name="affine0"),
+            shared.tile([P, PACK, HALF], F32, name="affine1", offset=28672),
+        ]
 
-        def project(h):
-            lo, hi = HALVES[h]
-            quantize(q_codes[:, lo:hi], q_scales[:, lo:hi], q_bf[h][:], E4M3)
+        def part(tiles, lo, hi):
+            return tiles[lo // HALF][:, lo % HALF : lo % HALF + hi - lo]
+
+        def weave_pair(copy, a, lo, hi):
+            copy(woven(part(q_bf, lo, hi)[:, :, 2 * a : 2 * a + 2]), planes(q_pairs[a][:, :, lo:hi]))
+
+        def quantize_q(lo, hi):
+            quantize(q_codes[:, lo:hi], q_scales[:, lo:hi], part(q_bf, lo, hi), E4M3)
+
+        def quantize_e(lo, hi):
+            quantize(e_codes[:, lo:hi], e_scales[:, lo:hi], part(e_bf, lo, hi), E5M2)
+
+        def project(lo, hi, first_bank):
             for t in range(PACK):
                 cols = slice(t * P, (t + 1) * P)
-                u = bank(PACK * h + t)
+                u = bank(first_bank + t)
                 nc.tensor.matmul_mx(
-                    out=u[:, :HALF],
+                    out=u[:, : hi - lo],
                     lhsT=md_codes[:, cols].bitcast(E4M3),
                     lhsT_scale=md_scales[:, cols],
                     rhs=q_codes[:, lo:hi].bitcast(E4M3),
@@ -140,16 +169,30 @@ def tile_attend_gtransr_E_kernel(tc, eT, M, rv, wi, cf, hoffs, toffs, out):
                     start=True,
                     stop=True,
                 )
-                nc.scalar.activation(affine[h][:, t, :], u[:, :HALF], ACT.Identity, bias=rv_cf2[:, t : t + 1], scale=cf2[:, t : t + 1])
+                dst = affine[lo // HALF][:, t, lo % HALF : lo % HALF + hi - lo]
+                nc.scalar.activation(dst, u[:, : hi - lo], ACT.Identity, bias=rv_cf2[:, t : t + 1], scale=cf2[:, t : t + 1])
 
-        def weigh(h):
-            lo, hi = HALVES[h]
+        def weigh(lo, hi):
             nc.vector.tensor_tensor(
-                woven(e_bf[h][:]),
-                planes(affine[h][:]),
-                wi_sb[:, lo:hi].rearrange("p (c i) -> p c i", i=4).unsqueeze(2).to_broadcast([P, HALF // 4, PACK, 4]),
+                woven(part(e_bf, lo, hi)),
+                planes(affine[lo // HALF][:, :, lo % HALF : lo % HALF + hi - lo]),
+                wi_sb[:, lo:hi].rearrange("p (c i) -> p c i", i=4).unsqueeze(2).to_broadcast([P, (hi - lo) // 4, PACK, 4]),
                 ALU.mult,
             )
+
+        pick_tails(0, 0, PAIRS)
+        pick_heads(0, 0, PAIRS)
+        quantize(mf_codes[:], mf_scales[:], mf_bf[:].rearrange("m j c t -> m (j c) t"), E4M3)
+        head_win.append(shared.tile([P, T], F32, name="head_win2", offset=8192))
+        nc.gpsimd.memset(head_win[2][:].bitcast(U32), 0)
+        for lo, hi in HALVES:
+            pick_tails(1, lo, hi)
+            pick_heads(1, lo, hi)
+        weave_pair(nc.vector.tensor_copy, 0, 0, HALF)
+        for lo, hi in HALVES:
+            pick_tails(2, lo, hi)
+            pick_heads(2, lo, hi)
+        weave_pair(nc.scalar.copy, 0, HALF, PAIRS)
 
         def back(j, lo, hi, b):
             acc = bank(b)
@@ -165,48 +208,74 @@ def tile_attend_gtransr_E_kernel(tc, eT, M, rv, wi, cf, hoffs, toffs, out):
             )
             return acc[:, : hi - lo]
 
-        pick(3, 0, HALF)
-        nc.vector.tensor_copy(woven(q_bf[0][:]), planes(q_f32[:, :, :HALF]))
-        pick(3, HALF, PAIRS)
-        nc.scalar.copy(woven(q_bf[1][:]), planes(q_f32[:, :, HALF:]))
-        project(0)
-        project(1)
-        weigh(0)
-        quantize(e_codes[:, :HALF], e_scales[:, :HALF], e_bf[0][:], E5M2)
-        weigh(1)
-        dd = [keep.tile([P, PAIRS], F32, name="dd%d" % j) for j in range(PACK)]
-        nc.scalar.copy(dd[0][:, :HALF], back(0, 0, HALF, 0))
-        quantize(e_codes[:, HALF:], e_scales[:, HALF:], e_bf[1][:], E5M2)
+        quarters = ((0, QUARTER), (QUARTER, HALF))
+        late = ((HALF, HALF + QUARTER), (HALF + QUARTER, PAIRS))
+        for lo, hi in quarters + late:
+            pick_tails(3, lo, hi)
+        for lo, hi in quarters:
+            pick_heads(3, lo, hi)
+        for c, (lo, hi) in enumerate(quarters):
+            weave_pair(nc.vector.tensor_copy, 1, lo, hi)
+            pick_heads(3, HALF + lo, HALF + hi)
+            quantize_q(lo, hi)
+            project(lo, hi, PACK * c)
+        weave_pair(nc.vector.tensor_copy, 1, HALF, PAIRS)
+        quantize_q(HALF, PAIRS)
+        for c, (lo, hi) in enumerate(late):
+            project(lo, hi, PACK * c)
+        for lo, hi in quarters:
+            weigh(lo, hi)
+        for lo, hi in quarters:
+            quantize_e(lo, hi)
+        dd = [keep.tile([P, PAIRS], F32, name="dd%d" % j) for j in range(PACK - 1)]
+        dd_last = [shared.tile([P, HALF], F32, name="dd3_0", offset=32768), keep.tile([P, HALF], F32, name="dd3_1")]
 
-        def put_heads(j, lo, hi):
-            nc.vector.tensor_copy(head_win[j % 3][:].indirect(entries(heads, lo, hi)), dd[j][:, lo:hi])
+        def gradient(j, lo, hi):
+            return dd[j][:, lo:hi] if j < PACK - 1 else dd_last[lo // HALF][:]
 
-        def put_tails(j, lo, hi):
-            nc.scalar.activation(tail_win[j % 3][:].indirect(entries(tails, lo, hi)), dd[j][:, lo:hi], ACT.Copy)
+        early = back(0, 0, HALF, 0)
+        nc.scalar.copy(dd[0][:, :HALF], early)
+        for lo, hi in late:
+            weigh(lo, hi)
+        dd_own = shared.tile([P, HALF], F32, name="dd_own", offset=28672)
+        nc.vector.tensor_copy(dd_own[:], early)
+        quantize_e(HALF, PAIRS)
+        tail_win.append(shared.tile([P, T], F32, name="tail_win2", offset=16384))
+        nc.gpsimd.memset(tail_win[2][:].bitcast(U32), 0)
 
-        def leave(j, edges, engine):
-            res = keep.tile([P, T], F32, name="res%d" % j)
+        def put_vector(wins, offsets, j, lo, hi):
+            nc.vector.tensor_copy(wins[j % 3][:].indirect(entries(offsets, lo, hi)), gradient(j, lo, hi))
+
+        def put_scalar(wins, offsets, j, lo, hi):
+            nc.scalar.activation(wins[j % 3][:].indirect(entries(offsets, lo, hi)), gradient(j, lo, hi), ACT.Copy)
+
+        def leave(j, edges, engine, res):
             for lo, hi in zip(edges[:-1], edges[1:]):
                 cols = slice(lo, hi)
                 engine.tensor_tensor(res[:, cols], head_win[j % 3][:, cols], tail_win[j % 3][:, cols], ALU.subtract)
                 nc.sync.dma_start(out_rows[:, j, cols], res[:, cols])
 
-        put_tails(0, 0, HALF)
-        put_heads(0, 0, HALF)
+        put_scalar(tail_win, tails, 0, 0, HALF)
+        nc.vector.tensor_copy(head_win[0][:].indirect(entries(heads, 0, HALF)), dd_own[:])
         nc.scalar.copy(dd[0][:, HALF:], back(0, HALF, PAIRS, 1))
         accs = [back(j, 0, PAIRS, 1 + j) for j in range(1, PACK)]
-        put_tails(0, HALF, PAIRS)
-        put_heads(0, HALF, PAIRS)
-        leave(0, (0, T // 2, T), nc.gpsimd)
-        for j in range(1, PACK):
-            if j == 2:
-                nc.vector.tensor_copy(dd[j][:], accs[j - 1])
-            else:
-                nc.scalar.copy(dd[j][:], accs[j - 1])
+        nc.scalar.copy(dd[1][:], accs[0])
+        nc.vector.tensor_copy(dd[2][:], accs[1])
+        put_scalar(tail_win, tails, 0, HALF, PAIRS)
+        put_vector(head_win, heads, 0, HALF, PAIRS)
+        leave(0, (0, T // 2, T), nc.gpsimd, keep.tile([P, T], F32, name="res0"))
+        put_scalar(tail_win, tails, 1, 0, HALF)
+        put_scalar(head_win, heads, 2, 0, HALF)
+        put_scalar(tail_win, tails, 1, HALF, PAIRS)
+        put_vector(head_win, heads, 1, 0, PAIRS)
+        for h, (lo, hi) in enumerate(HALVES):
+            nc.vector.tensor_copy(dd_last[h][:], accs[2][:, lo:hi])
+        leave(1, POOL_EDGES, nc.gpsimd, keep.tile([P, T], F32, name="res1"))
+        put_vector(head_win, heads, 2, HALF, PAIRS)
+        for j in (2, 3):
             for lo, hi in HALVES:
-                put_tails(j, lo, hi)
-            put_heads(j, 0, PAIRS)
-            if j == 1:
-                leave(1, (0, T // 2, T), nc.gpsimd)
-        leave(2, (0, T // 2, T), nc.vector)
-        leave(3, TAIL_EDGES, nc.vector)
+                put_scalar(tail_win, tails, j, lo, hi)
+        put_vector(head_win, heads, 3, HALF, PAIRS)
+        put_vector(head_win, heads, 3, 0, HALF)
+        leave(2, FIRST_EDGES, nc.vector, shared.tile([P, T], F32, name="res2", offset=32768))
+        leave(3, LAST_EDGES, nc.vector, keep.tile([P, T], F32, name="res3"))

@@ -24,6 +24,7 @@ QUARTER = PAIRS // 4
 HALVES = ((0, HALF), (HALF, PAIRS))
 LIST_COLS = PAIRS // 16
 DEAL = 96
+SLIVER = 32
 FIRST_EDGES = (0, 256, 768, 1280, 2048)
 LAST_EDGES = (0, 768, 1280, 1792, 2048)
 POOL_EDGES = (0, 1024, 1536, 2048)
@@ -87,7 +88,7 @@ def tile_attend_gtransr_E_kernel(tc, eT, M, rv, wi, cf, hoffs, toffs, out):
         def quantize(codes, scales, src, fmt):
             nc.vector.quantize_mx(codes.bitcast(fmt), scales, src.rearrange("p i t -> p (i t)"))
 
-        md_bf = shared.tile([P, PACK, P, PACK], BF16, name="md_bf", offset=2048, align_bytes=64)
+        md_bf = shared.tile([P, PACK, P, PACK], BF16, name="md_bf", offset=5120, align_bytes=64)
         md_codes = keep.tile([P, F], U32, name="md_codes", align_bytes=64)
         md_scales = keep.tile([P, F], U8, name="md_scales", align_bytes=64)
         md_view = md_bf[:].rearrange("p t m j -> p m j t")
@@ -99,7 +100,7 @@ def tile_attend_gtransr_E_kernel(tc, eT, M, rv, wi, cf, hoffs, toffs, out):
         nc.vector.tensor_tensor(rv_cf2[:], rv_sb[:], cf2[:], ALU.mult)
 
         md_words = md_bf[:].rearrange("p t m j -> p (t m j)").bitcast(F32).rearrange("p (t m a) -> p t m a", t=PACK, a=2)
-        mf_bf = shared.tile([P, PACK, P, PACK], BF16, name="mf_bf", offset=8192, align_bytes=64)
+        mf_bf = shared.tile([P, PACK, P, PACK], BF16, name="mf_bf", offset=12288, align_bytes=64)
         mf_codes = keep.tile([P, D], U32, name="mf_codes", align_bytes=64)
         mf_scales = keep.tile([P, D], U8, name="mf_scales", align_bytes=64)
         for a, copy in enumerate((nc.vector.tensor_copy, nc.scalar.copy)):
@@ -108,27 +109,19 @@ def tile_attend_gtransr_E_kernel(tc, eT, M, rv, wi, cf, hoffs, toffs, out):
                 nc.tensor.transpose(turned[:, t * P : (t + 1) * P], md_words[:, t, :, a], ident[:])
             copy(mf_bf[:, 2 * a : 2 * a + 2], turned[:].bitcast(BF16).rearrange("m (t c e) -> m e c t", t=PACK, e=2))
 
-        q_pairs = [
-            shared.tile([P, 2, PAIRS], F32, name="q_pair0", offset=0),
-            keep.tile([P, 2, PAIRS], F32, name="q_pair1"),
-        ]
-        whole = [
-            keep.tile([P, PAIRS], F32, name="picked0"),
-            shared.tile([P, PAIRS], F32, name="picked1", offset=4096),
-            keep.tile([P, PAIRS], F32, name="picked2"),
-        ]
-        whole.append(keep.tile([P, PAIRS], F32, name="picked3"))
+        q_early = [shared.tile([P, 2, HALF], F32, name="q_early%d" % h, offset=8192 - 2048 * h) for h in range(2)]
+        early_tails = [keep.tile([P, PAIRS], F32, name="tails0"), shared.tile([P, PAIRS], F32, name="tails1", offset=4096)]
+        late_heads = shared.tile([P, 2, PAIRS], F32, name="late_heads", offset=2048)
+        late_tails = keep.tile([P, 2, PAIRS], F32, name="late_tails")
 
-        def picked(j, lo, hi):
-            return whole[j][:, lo:hi]
+        def pick_scalar(dst, j, offsets, lo, hi):
+            nc.scalar.activation(dst[:, lo:hi], table[j][:].indirect(entries(offsets, lo, hi)), ACT.Copy)
 
-        def pick_tails(j, lo, hi):
-            nc.scalar.activation(picked(j, lo, hi), table[j][:].indirect(entries(tails, lo, hi)), ACT.Copy)
+        def pick_vector(dst, j, offsets, lo, hi):
+            nc.vector.tensor_copy(dst[:, lo:hi], table[j][:].indirect(entries(offsets, lo, hi)))
 
-        def pick_heads(j, lo, hi):
-            nc.vector.tensor_tensor(
-                q_pairs[j // 2][:, j % 2, lo:hi], table[j][:].indirect(entries(heads, lo, hi)), picked(j, lo, hi), ALU.subtract
-            )
+        def subtract_early(j, lo, hi):
+            nc.vector.tensor_tensor(q_early[lo // HALF][:, j, :], table[j][:].indirect(entries(heads, lo, hi)), early_tails[j][:, lo:hi], ALU.subtract)
 
         q_codes = keep.tile([P, PAIRS], U32, name="q_codes", align_bytes=64)
         q_scales = keep.tile([P, PAIRS], U8, name="q_scales", align_bytes=64)
@@ -147,8 +140,13 @@ def tile_attend_gtransr_E_kernel(tc, eT, M, rv, wi, cf, hoffs, toffs, out):
         def part(tiles, lo, hi):
             return tiles[lo // HALF][:, lo % HALF : lo % HALF + hi - lo]
 
-        def weave_pair(copy, a, lo, hi):
-            copy(woven(part(q_bf, lo, hi)[:, :, 2 * a : 2 * a + 2]), planes(q_pairs[a][:, :, lo:hi]))
+        def weave_early(copy, lo, hi):
+            copy(woven(part(q_bf, lo, hi)[:, :, :2]), planes(q_early[lo // HALF][:]))
+
+        def weave_late(lo, hi):
+            nc.vector.tensor_tensor(
+                woven(part(q_bf, lo, hi)[:, :, 2:]), planes(late_heads[:, :, lo:hi]), planes(late_tails[:, :, lo:hi]), ALU.subtract
+            )
 
         def quantize_q(lo, hi):
             quantize(q_codes[:, lo:hi], q_scales[:, lo:hi], part(q_bf, lo, hi), E4M3)
@@ -180,19 +178,19 @@ def tile_attend_gtransr_E_kernel(tc, eT, M, rv, wi, cf, hoffs, toffs, out):
                 ALU.mult,
             )
 
-        pick_tails(0, 0, PAIRS)
-        pick_heads(0, 0, PAIRS)
+        pick_scalar(early_tails[0], 0, tails, 0, PAIRS)
+        for lo, hi in HALVES:
+            subtract_early(0, lo, hi)
         quantize(mf_codes[:], mf_scales[:], mf_bf[:].rearrange("m j c t -> m (j c) t"), E4M3)
+        for lo, hi in HALVES:
+            pick_scalar(early_tails[1], 1, tails, lo, hi)
+            subtract_early(1, lo, hi)
+        weave_early(nc.vector.tensor_copy, 0, HALF)
         head_win.append(shared.tile([P, T], F32, name="head_win2", offset=8192))
         nc.gpsimd.memset(head_win[2][:].bitcast(U32), 0)
-        for lo, hi in HALVES:
-            pick_tails(1, lo, hi)
-            pick_heads(1, lo, hi)
-        weave_pair(nc.vector.tensor_copy, 0, 0, HALF)
-        for lo, hi in HALVES:
-            pick_tails(2, lo, hi)
-            pick_heads(2, lo, hi)
-        weave_pair(nc.scalar.copy, 0, HALF, PAIRS)
+        pick_vector(late_heads[:, 0], 2, heads, 0, PAIRS)
+        pick_scalar(late_tails[:, 0], 2, tails, 0, PAIRS)
+        weave_early(nc.scalar.copy, HALF, PAIRS)
 
         def back(j, lo, hi, b):
             acc = bank(b)
@@ -210,16 +208,20 @@ def tile_attend_gtransr_E_kernel(tc, eT, M, rv, wi, cf, hoffs, toffs, out):
 
         quarters = ((0, QUARTER), (QUARTER, HALF))
         late = ((HALF, HALF + QUARTER), (HALF + QUARTER, PAIRS))
-        for lo, hi in quarters + late:
-            pick_tails(3, lo, hi)
         for lo, hi in quarters:
-            pick_heads(3, lo, hi)
-        for c, (lo, hi) in enumerate(quarters):
-            weave_pair(nc.vector.tensor_copy, 1, lo, hi)
-            pick_heads(3, HALF + lo, HALF + hi)
-            quantize_q(lo, hi)
-            project(lo, hi, PACK * c)
-        weave_pair(nc.vector.tensor_copy, 1, HALF, PAIRS)
+            pick_vector(late_heads[:, 1], 3, heads, lo, hi)
+            pick_scalar(late_tails[:, 1], 3, tails, lo, hi)
+        for lo, hi in late:
+            pick_scalar(late_tails[:, 1], 3, tails, lo, hi)
+            pick_scalar(late_heads[:, 1], 3, heads, lo, hi)
+        for lo, hi in quarters:
+            weave_late(lo, hi)
+        quantize_q(0, QUARTER)
+        project(0, QUARTER, 0)
+        quantize_q(QUARTER, HALF)
+        project(QUARTER, HALF, PACK)
+        for lo, hi in late:
+            weave_late(lo, hi)
         quantize_q(HALF, PAIRS)
         for c, (lo, hi) in enumerate(late):
             project(lo, hi, PACK * c)
@@ -235,7 +237,7 @@ def tile_attend_gtransr_E_kernel(tc, eT, M, rv, wi, cf, hoffs, toffs, out):
 
         early = back(0, 0, HALF, 0)
         nc.scalar.copy(dd[0][:, :HALF], early)
-        for lo, hi in late:
+        for lo, hi in ((HALF, HALF + SLIVER), (HALF + SLIVER, HALF + QUARTER), late[1]):
             weigh(lo, hi)
         dd_own = shared.tile([P, HALF], F32, name="dd_own", offset=28672)
         nc.vector.tensor_copy(dd_own[:], early)
@@ -258,10 +260,10 @@ def tile_attend_gtransr_E_kernel(tc, eT, M, rv, wi, cf, hoffs, toffs, out):
         put_scalar(tail_win, tails, 0, 0, HALF)
         nc.vector.tensor_copy(head_win[0][:].indirect(entries(heads, 0, HALF)), dd_own[:])
         nc.scalar.copy(dd[0][:, HALF:], back(0, HALF, PAIRS, 1))
-        accs = [back(j, 0, PAIRS, 1 + j) for j in range(1, PACK)]
-        nc.scalar.copy(dd[1][:], accs[0])
-        nc.vector.tensor_copy(dd[2][:], accs[1])
+        accs = [back(j, 0, PAIRS, b) for j, b in ((1, 2), (2, 1), (3, 3))]
+        nc.vector.tensor_copy(dd[1][:], accs[0])
         put_scalar(tail_win, tails, 0, HALF, PAIRS)
+        nc.scalar.copy(dd[2][:], accs[1])
         put_vector(head_win, heads, 0, HALF, PAIRS)
         leave(0, (0, T // 2, T), nc.gpsimd, keep.tile([P, T], F32, name="res0"))
         put_scalar(tail_win, tails, 1, 0, HALF)

@@ -23,11 +23,11 @@ HALF = PAIRS // 2
 QUARTER = PAIRS // 4
 HALVES = ((0, HALF), (HALF, PAIRS))
 LIST_COLS = PAIRS // 16
-DEAL = 96
+DEAL = 72
 SLIVER = 32
-FIRST_EDGES = (0, 256, 768, 1280, 2048)
-LAST_EDGES = (0, 768, 1280, 1792, 2048)
-POOL_EDGES = (0, 1024, 1536, 2048)
+FIRST_EDGES = (0, 256, 768, 1408, 2048)
+LAST_EDGES = (0, 640, 1280, 1792, 2048)
+POOL_EDGES = (0, 1024, 1792, 2048)
 
 FLOPS = 2 * 2 * D * F * PAIRS
 
@@ -65,8 +65,8 @@ def tile_attend_gtransr_E_kernel(tc, eT, M, rv, wi, cf, hoffs, toffs, out):
         ident = keep.tile([P, P], F32, name="ident")
         make_identity(nc, ident[:])
 
-        head_win = [keep.tile([P, T], F32, name="head_win%d" % w) for w in range(2)]
-        tail_win = [keep.tile([P, T], F32, name="tail_win%d" % w) for w in range(2)]
+        head_win = [keep.tile([P, T], F32, name="head_win0"), shared.tile([P, T], F32, name="head_win1", offset=32768)]
+        tail_win = [keep.tile([P, T], F32, name="tail_win0"), shared.tile([P, T], F32, name="tail_win1", offset=40960)]
         for win in head_win:
             for cols in (slice(0, T // 2 - 1), slice(T // 2 - 1, T)):
                 nc.vector.memset(win[:, cols].bitcast(U32), 0)
@@ -229,12 +229,7 @@ def tile_attend_gtransr_E_kernel(tc, eT, M, rv, wi, cf, hoffs, toffs, out):
             weigh(lo, hi)
         for lo, hi in quarters:
             quantize_e(lo, hi)
-        dd = [keep.tile([P, PAIRS], F32, name="dd%d" % j) for j in range(PACK - 1)]
-        dd_last = [shared.tile([P, HALF], F32, name="dd3_0", offset=32768), keep.tile([P, HALF], F32, name="dd3_1")]
-
-        def gradient(j, lo, hi):
-            return dd[j][:, lo:hi] if j < PACK - 1 else dd_last[lo // HALF][:]
-
+        dd = [keep.tile([P, PAIRS], F32, name="dd%d" % j) for j in range(PACK)]
         early = back(0, 0, HALF, 0)
         nc.scalar.copy(dd[0][:, :HALF], early)
         for lo, hi in ((HALF, HALF + SLIVER), (HALF + SLIVER, HALF + QUARTER), late[1]):
@@ -246,10 +241,10 @@ def tile_attend_gtransr_E_kernel(tc, eT, M, rv, wi, cf, hoffs, toffs, out):
         nc.gpsimd.memset(tail_win[2][:].bitcast(U32), 0)
 
         def put_vector(wins, offsets, j, lo, hi):
-            nc.vector.tensor_copy(wins[j % 3][:].indirect(entries(offsets, lo, hi)), gradient(j, lo, hi))
+            nc.vector.tensor_copy(wins[j % 3][:].indirect(entries(offsets, lo, hi)), dd[j][:, lo:hi])
 
         def put_scalar(wins, offsets, j, lo, hi):
-            nc.scalar.activation(wins[j % 3][:].indirect(entries(offsets, lo, hi)), gradient(j, lo, hi), ACT.Copy)
+            nc.scalar.activation(wins[j % 3][:].indirect(entries(offsets, lo, hi)), dd[j][:, lo:hi], ACT.Copy)
 
         def leave(j, edges, engine, res):
             for lo, hi in zip(edges[:-1], edges[1:]):
@@ -263,21 +258,19 @@ def tile_attend_gtransr_E_kernel(tc, eT, M, rv, wi, cf, hoffs, toffs, out):
         accs = [back(j, 0, PAIRS, b) for j, b in ((1, 2), (2, 1), (3, 3))]
         nc.vector.tensor_copy(dd[1][:], accs[0])
         put_scalar(tail_win, tails, 0, HALF, PAIRS)
-        nc.scalar.copy(dd[2][:], accs[1])
         put_vector(head_win, heads, 0, HALF, PAIRS)
-        leave(0, (0, T // 2, T), nc.gpsimd, keep.tile([P, T], F32, name="res0"))
+        nc.vector.tensor_copy(dd[2][:], accs[1])
+        leave(0, (0, T), nc.gpsimd, keep.tile([P, T], F32, name="res0"))
         put_scalar(tail_win, tails, 1, 0, HALF)
         put_scalar(head_win, heads, 2, 0, HALF)
         put_scalar(tail_win, tails, 1, HALF, PAIRS)
         put_vector(head_win, heads, 1, 0, PAIRS)
-        for h, (lo, hi) in enumerate(HALVES):
-            nc.vector.tensor_copy(dd_last[h][:], accs[2][:, lo:hi])
+        nc.vector.tensor_copy(dd[3][:], accs[2])
         leave(1, POOL_EDGES, nc.gpsimd, keep.tile([P, T], F32, name="res1"))
         put_vector(head_win, heads, 2, HALF, PAIRS)
         for j in (2, 3):
             for lo, hi in HALVES:
                 put_scalar(tail_win, tails, j, lo, hi)
-        put_vector(head_win, heads, 3, HALF, PAIRS)
-        put_vector(head_win, heads, 3, 0, HALF)
+        put_vector(head_win, heads, 3, 0, PAIRS)
         leave(2, FIRST_EDGES, nc.vector, shared.tile([P, T], F32, name="res2", offset=32768))
-        leave(3, LAST_EDGES, nc.vector, keep.tile([P, T], F32, name="res3"))
+        leave(3, LAST_EDGES, nc.vector, shared.tile([P, T], F32, name="res3", offset=40960))

@@ -19,15 +19,33 @@ D = 512
 F = 512
 PAIRS = 512
 T = 2048
+BAND = 16
+LIST_COLS = PAIRS // BAND
+RUN = 4
+WINDOWS = 3
+
 HALF = PAIRS // 2
 QUARTER = PAIRS // 4
 HALVES = ((0, HALF), (HALF, PAIRS))
-LIST_COLS = PAIRS // 16
+FIRST_QUARTERS = ((0, QUARTER), (QUARTER, HALF))
+LAST_QUARTERS = ((HALF, HALF + QUARTER), (HALF + QUARTER, PAIRS))
+
 DEAL = 72
 SLIVER = 32
-FIRST_EDGES = (0, 256, 768, 1408, 2048)
-LAST_EDGES = (0, 640, 1280, 1792, 2048)
-POOL_EDGES = (0, 1024, 1792, 2048)
+PLANE1_EDGES = (0, 1024, 1792, T)
+PLANE2_EDGES = (0, 256, 768, 1408, T)
+PLANE3_EDGES = (0, 640, 1280, 1792, T)
+
+AT_LATE_HEADS = 2048
+AT_TAILS1 = 4096
+AT_MD = 5120
+AT_Q_EARLY = (8192, 6144)
+AT_HEAD_WIN2 = 8192
+AT_MF = 12288
+AT_E_SECOND = 16384
+AT_AFFINE_SECOND = 28672
+AT_HEAD_WIN1 = 32768
+AT_TAIL_WIN1 = 40960
 
 FLOPS = 2 * 2 * D * F * PAIRS
 
@@ -56,17 +74,17 @@ def tile_attend_gtransr_E_kernel(tc, eT, M, rv, wi, cf, hoffs, toffs, out):
         nc.sync.dma_start(m_raw[:], M.rearrange("(p j) f -> p j f", j=PACK))
         nc.sync.dma_start(tails[:], toffs)
         nc.sync.dma_start(heads[:], hoffs)
-        nc.scalar.dma_start(cf_sb[:], cf.rearrange("(p t) o -> p (t o)", t=PACK))
-        nc.scalar.dma_start(rv_sb[:], rv.rearrange("(p t) o -> p (t o)", t=PACK))
         for j in range(PACK):
             nc.sync.dma_start(table[j][:], e_rows[:, j, :])
+        nc.sync.dma_start(cf_sb[:], cf.rearrange("(p t) o -> p (t o)", t=PACK))
+        nc.sync.dma_start(rv_sb[:], rv.rearrange("(p t) o -> p (t o)", t=PACK))
         nc.sync.dma_start(wi_sb[:], wi)
 
         ident = keep.tile([P, P], F32, name="ident")
         make_identity(nc, ident[:])
 
-        head_win = [keep.tile([P, T], F32, name="head_win0"), shared.tile([P, T], F32, name="head_win1", offset=32768)]
-        tail_win = [keep.tile([P, T], F32, name="tail_win0"), shared.tile([P, T], F32, name="tail_win1", offset=40960)]
+        head_win = [keep.tile([P, T], F32, name="head_win0"), shared.tile([P, T], F32, name="head_win1", offset=AT_HEAD_WIN1)]
+        tail_win = [keep.tile([P, T], F32, name="tail_win0"), shared.tile([P, T], F32, name="tail_win1", offset=AT_TAIL_WIN1)]
         for win in head_win:
             for cols in (slice(0, T // 2 - 1), slice(T // 2 - 1, T)):
                 nc.vector.memset(win[:, cols].bitcast(U32), 0)
@@ -77,41 +95,39 @@ def tile_attend_gtransr_E_kernel(tc, eT, M, rv, wi, cf, hoffs, toffs, out):
         rv_cf2 = keep.tile([P, PACK], F32, name="rv_cf2")
 
         def entries(offsets, lo, hi):
-            return offsets[:, lo // 16 : hi // 16]
+            return offsets[:, lo // BAND : hi // BAND]
 
         def woven(dst):
-            return dst.rearrange("p (c i) t -> p c t i", i=4)
+            return dst.rearrange("p (c i) t -> p c t i", i=RUN)
 
         def planes(src):
-            return src.rearrange("p t (c i) -> p c t i", i=4)
+            return src.rearrange("p t (c i) -> p c t i", i=RUN)
 
         def quantize(codes, scales, src, fmt):
             nc.vector.quantize_mx(codes.bitcast(fmt), scales, src.rearrange("p i t -> p (i t)"))
 
-        md_bf = shared.tile([P, PACK, P, PACK], BF16, name="md_bf", offset=5120, align_bytes=64)
+        md_bf = shared.tile([P, PACK, P, PACK], BF16, name="md_bf", offset=AT_MD, align_bytes=64)
         md_codes = keep.tile([P, F], U32, name="md_codes", align_bytes=64)
         md_scales = keep.tile([P, F], U8, name="md_scales", align_bytes=64)
         md_view = md_bf[:].rearrange("p t m j -> p m j t")
         m_view = m_raw[:].rearrange("p j (m t) -> p m j t", t=PACK)
         nc.scalar.copy(md_view[:, :DEAL], m_view[:, :DEAL])
         nc.vector.tensor_copy(md_view[:, DEAL:], m_view[:, DEAL:])
-        nc.vector.tensor_tensor(cf2[:], cf_sb[:], cf_sb[:], ALU.mult)
         quantize(md_codes[:], md_scales[:], md_bf[:].rearrange("p t m j -> p (t m) j"), E4M3)
-        nc.vector.tensor_tensor(rv_cf2[:], rv_sb[:], cf2[:], ALU.mult)
 
         md_words = md_bf[:].rearrange("p t m j -> p (t m j)").bitcast(F32).rearrange("p (t m a) -> p t m a", t=PACK, a=2)
-        mf_bf = shared.tile([P, PACK, P, PACK], BF16, name="mf_bf", offset=12288, align_bytes=64)
+        mf_bf = shared.tile([P, PACK, P, PACK], BF16, name="mf_bf", offset=AT_MF, align_bytes=64)
         mf_codes = keep.tile([P, D], U32, name="mf_codes", align_bytes=64)
         mf_scales = keep.tile([P, D], U8, name="mf_scales", align_bytes=64)
         for a, copy in enumerate((nc.vector.tensor_copy, nc.scalar.copy)):
-            turned = bank(4 + a)
+            turned = bank(PACK + a)
             for t in range(PACK):
                 nc.tensor.transpose(turned[:, t * P : (t + 1) * P], md_words[:, t, :, a], ident[:])
             copy(mf_bf[:, 2 * a : 2 * a + 2], turned[:].bitcast(BF16).rearrange("m (t c e) -> m e c t", t=PACK, e=2))
 
-        q_early = [shared.tile([P, 2, HALF], F32, name="q_early%d" % h, offset=8192 - 2048 * h) for h in range(2)]
-        early_tails = [keep.tile([P, PAIRS], F32, name="tails0"), shared.tile([P, PAIRS], F32, name="tails1", offset=4096)]
-        late_heads = shared.tile([P, 2, PAIRS], F32, name="late_heads", offset=2048)
+        q_early = [shared.tile([P, 2, HALF], F32, name="q_early%d" % h, offset=AT_Q_EARLY[h]) for h in range(2)]
+        early_tails = [keep.tile([P, PAIRS], F32, name="tails0"), shared.tile([P, PAIRS], F32, name="tails1", offset=AT_TAILS1)]
+        late_heads = shared.tile([P, 2, PAIRS], F32, name="late_heads", offset=AT_LATE_HEADS)
         late_tails = keep.tile([P, 2, PAIRS], F32, name="late_tails")
 
         def pick_scalar(dst, j, offsets, lo, hi):
@@ -121,7 +137,8 @@ def tile_attend_gtransr_E_kernel(tc, eT, M, rv, wi, cf, hoffs, toffs, out):
             nc.vector.tensor_copy(dst[:, lo:hi], table[j][:].indirect(entries(offsets, lo, hi)))
 
         def subtract_early(j, lo, hi):
-            nc.vector.tensor_tensor(q_early[lo // HALF][:, j, :], table[j][:].indirect(entries(heads, lo, hi)), early_tails[j][:, lo:hi], ALU.subtract)
+            picked_heads = table[j][:].indirect(entries(heads, lo, hi))
+            nc.vector.tensor_tensor(q_early[lo // HALF][:, j, :], picked_heads, early_tails[j][:, lo:hi], ALU.subtract)
 
         q_codes = keep.tile([P, PAIRS], U32, name="q_codes", align_bytes=64)
         q_scales = keep.tile([P, PAIRS], U8, name="q_scales", align_bytes=64)
@@ -130,15 +147,18 @@ def tile_attend_gtransr_E_kernel(tc, eT, M, rv, wi, cf, hoffs, toffs, out):
         q_bf = [keep.tile([P, HALF, PACK], BF16, name="q_bf%d" % h, align_bytes=64) for h in range(2)]
         e_bf = [
             keep.tile([P, HALF, PACK], BF16, name="e_bf0", align_bytes=64),
-            shared.tile([P, HALF, PACK], BF16, name="e_bf1", offset=16384, align_bytes=64),
+            shared.tile([P, HALF, PACK], BF16, name="e_bf1", offset=AT_E_SECOND, align_bytes=64),
         ]
         affine = [
             keep.tile([P, PACK, HALF], F32, name="affine0"),
-            shared.tile([P, PACK, HALF], F32, name="affine1", offset=28672),
+            shared.tile([P, PACK, HALF], F32, name="affine1", offset=AT_AFFINE_SECOND),
         ]
 
+        def within(lo, hi):
+            return slice(lo % HALF, lo % HALF + hi - lo)
+
         def part(tiles, lo, hi):
-            return tiles[lo // HALF][:, lo % HALF : lo % HALF + hi - lo]
+            return tiles[lo // HALF][:, within(lo, hi)]
 
         def weave_early(copy, lo, hi):
             copy(woven(part(q_bf, lo, hi)[:, :, :2]), planes(q_early[lo // HALF][:]))
@@ -167,14 +187,14 @@ def tile_attend_gtransr_E_kernel(tc, eT, M, rv, wi, cf, hoffs, toffs, out):
                     start=True,
                     stop=True,
                 )
-                dst = affine[lo // HALF][:, t, lo % HALF : lo % HALF + hi - lo]
+                dst = affine[lo // HALF][:, t, within(lo, hi)]
                 nc.scalar.activation(dst, u[:, : hi - lo], ACT.Identity, bias=rv_cf2[:, t : t + 1], scale=cf2[:, t : t + 1])
 
         def weigh(lo, hi):
             nc.vector.tensor_tensor(
                 woven(part(e_bf, lo, hi)),
-                planes(affine[lo // HALF][:, :, lo % HALF : lo % HALF + hi - lo]),
-                wi_sb[:, lo:hi].rearrange("p (c i) -> p c i", i=4).unsqueeze(2).to_broadcast([P, (hi - lo) // 4, PACK, 4]),
+                planes(affine[lo // HALF][:, :, within(lo, hi)]),
+                wi_sb[:, lo:hi].rearrange("p (c i) -> p c i", i=RUN).unsqueeze(2).to_broadcast([P, (hi - lo) // RUN, PACK, RUN]),
                 ALU.mult,
             )
 
@@ -186,7 +206,7 @@ def tile_attend_gtransr_E_kernel(tc, eT, M, rv, wi, cf, hoffs, toffs, out):
             pick_scalar(early_tails[1], 1, tails, lo, hi)
             subtract_early(1, lo, hi)
         weave_early(nc.vector.tensor_copy, 0, HALF)
-        head_win.append(shared.tile([P, T], F32, name="head_win2", offset=8192))
+        head_win.append(shared.tile([P, T], F32, name="head_win2", offset=AT_HEAD_WIN2))
         nc.gpsimd.memset(head_win[2][:].bitcast(U32), 0)
         pick_vector(late_heads[:, 0], 2, heads, 0, PAIRS)
         pick_scalar(late_tails[:, 0], 2, tails, 0, PAIRS)
@@ -206,71 +226,73 @@ def tile_attend_gtransr_E_kernel(tc, eT, M, rv, wi, cf, hoffs, toffs, out):
             )
             return acc[:, : hi - lo]
 
-        quarters = ((0, QUARTER), (QUARTER, HALF))
-        late = ((HALF, HALF + QUARTER), (HALF + QUARTER, PAIRS))
-        for lo, hi in quarters:
+        for lo, hi in FIRST_QUARTERS:
             pick_vector(late_heads[:, 1], 3, heads, lo, hi)
             pick_scalar(late_tails[:, 1], 3, tails, lo, hi)
-        for lo, hi in late:
+        for lo, hi in LAST_QUARTERS:
             pick_scalar(late_tails[:, 1], 3, tails, lo, hi)
             pick_scalar(late_heads[:, 1], 3, heads, lo, hi)
-        for lo, hi in quarters:
+        nc.scalar.activation(cf2[:], cf_sb[:], ACT.Square)
+        for t in range(PACK):
+            nc.scalar.activation(rv_cf2[:, t : t + 1], rv_sb[:, t : t + 1], ACT.Copy, scale=cf2[:, t : t + 1])
+        for lo, hi in FIRST_QUARTERS:
             weave_late(lo, hi)
         quantize_q(0, QUARTER)
         project(0, QUARTER, 0)
         quantize_q(QUARTER, HALF)
         project(QUARTER, HALF, PACK)
-        for lo, hi in late:
+        for lo, hi in LAST_QUARTERS:
             weave_late(lo, hi)
         quantize_q(HALF, PAIRS)
-        for c, (lo, hi) in enumerate(late):
+        for c, (lo, hi) in enumerate(LAST_QUARTERS):
             project(lo, hi, PACK * c)
-        for lo, hi in quarters:
+        for lo, hi in FIRST_QUARTERS:
             weigh(lo, hi)
-        for lo, hi in quarters:
+        for lo, hi in FIRST_QUARTERS:
             quantize_e(lo, hi)
         dd = [keep.tile([P, PAIRS], F32, name="dd%d" % j) for j in range(PACK)]
-        early = back(0, 0, HALF, 0)
-        nc.scalar.copy(dd[0][:, :HALF], early)
-        for lo, hi in ((HALF, HALF + SLIVER), (HALF + SLIVER, HALF + QUARTER), late[1]):
+        first_acc = back(0, 0, HALF, 0)
+        nc.scalar.copy(dd[0][:, :HALF], first_acc)
+        for lo, hi in ((HALF, HALF + SLIVER), (HALF + SLIVER, HALF + QUARTER), LAST_QUARTERS[1]):
             weigh(lo, hi)
-        dd_own = shared.tile([P, HALF], F32, name="dd_own", offset=28672)
-        nc.vector.tensor_copy(dd_own[:], early)
+        dd_own = shared.tile([P, HALF], F32, name="dd_own", offset=AT_AFFINE_SECOND)
+        nc.vector.tensor_copy(dd_own[:], first_acc)
         quantize_e(HALF, PAIRS)
-        tail_win.append(shared.tile([P, T], F32, name="tail_win2", offset=16384))
+        tail_win.append(shared.tile([P, T], F32, name="tail_win2", offset=AT_E_SECOND))
         nc.gpsimd.memset(tail_win[2][:].bitcast(U32), 0)
 
         def put_vector(wins, offsets, j, lo, hi):
-            nc.vector.tensor_copy(wins[j % 3][:].indirect(entries(offsets, lo, hi)), dd[j][:, lo:hi])
+            nc.vector.tensor_copy(wins[j % WINDOWS][:].indirect(entries(offsets, lo, hi)), dd[j][:, lo:hi])
 
         def put_scalar(wins, offsets, j, lo, hi):
-            nc.scalar.activation(wins[j % 3][:].indirect(entries(offsets, lo, hi)), dd[j][:, lo:hi], ACT.Copy)
+            nc.scalar.activation(wins[j % WINDOWS][:].indirect(entries(offsets, lo, hi)), dd[j][:, lo:hi], ACT.Copy)
 
         def leave(j, edges, engine, res):
             for lo, hi in zip(edges[:-1], edges[1:]):
                 cols = slice(lo, hi)
-                engine.tensor_tensor(res[:, cols], head_win[j % 3][:, cols], tail_win[j % 3][:, cols], ALU.subtract)
+                engine.tensor_tensor(res[:, cols], head_win[j % WINDOWS][:, cols], tail_win[j % WINDOWS][:, cols], ALU.subtract)
                 nc.sync.dma_start(out_rows[:, j, cols], res[:, cols])
 
         put_scalar(tail_win, tails, 0, 0, HALF)
         nc.vector.tensor_copy(head_win[0][:].indirect(entries(heads, 0, HALF)), dd_own[:])
         nc.scalar.copy(dd[0][:, HALF:], back(0, HALF, PAIRS, 1))
-        accs = [back(j, 0, PAIRS, b) for j, b in ((1, 2), (2, 1), (3, 3))]
-        nc.vector.tensor_copy(dd[1][:], accs[0])
+        accs = {j: back(j, 0, PAIRS, b) for j, b in ((1, 2), (2, 1), (3, 3))}
+        nc.scalar.copy(dd[1][:, :HALF], accs[1][:, :HALF])
         put_scalar(tail_win, tails, 0, HALF, PAIRS)
         put_vector(head_win, heads, 0, HALF, PAIRS)
-        nc.vector.tensor_copy(dd[2][:], accs[1])
+        nc.vector.tensor_copy(dd[1][:, HALF:], accs[1][:, HALF:])
+        nc.vector.tensor_copy(dd[2][:], accs[2])
         leave(0, (0, T), nc.gpsimd, keep.tile([P, T], F32, name="res0"))
         put_scalar(tail_win, tails, 1, 0, HALF)
         put_scalar(head_win, heads, 2, 0, HALF)
         put_scalar(tail_win, tails, 1, HALF, PAIRS)
         put_vector(head_win, heads, 1, 0, PAIRS)
-        nc.vector.tensor_copy(dd[3][:], accs[2])
-        leave(1, POOL_EDGES, nc.gpsimd, keep.tile([P, T], F32, name="res1"))
+        nc.vector.tensor_copy(dd[3][:], accs[3])
+        leave(1, PLANE1_EDGES, nc.gpsimd, keep.tile([P, T], F32, name="res1"))
         put_vector(head_win, heads, 2, HALF, PAIRS)
         for j in (2, 3):
             for lo, hi in HALVES:
                 put_scalar(tail_win, tails, j, lo, hi)
         put_vector(head_win, heads, 3, 0, PAIRS)
-        leave(2, FIRST_EDGES, nc.vector, shared.tile([P, T], F32, name="res2", offset=32768))
-        leave(3, LAST_EDGES, nc.vector, shared.tile([P, T], F32, name="res3", offset=40960))
+        leave(2, PLANE2_EDGES, nc.vector, shared.tile([P, T], F32, name="res2", offset=AT_HEAD_WIN1))
+        leave(3, PLANE3_EDGES, nc.vector, shared.tile([P, T], F32, name="res3", offset=AT_TAIL_WIN1))

@@ -30,7 +30,8 @@ HALVES = ((0, HALF), (HALF, PAIRS))
 FIRST_QUARTERS = ((0, QUARTER), (QUARTER, HALF))
 LAST_QUARTERS = ((HALF, HALF + QUARTER), (HALF + QUARTER, PAIRS))
 
-DEAL = 72
+DEAL = 48
+VECTOR_ZEROS = 1280
 SLIVER = 32
 PLANE1_EDGES = (0, 1024, 1792, T)
 PLANE2_EDGES = (0, 256, 768, 1408, T)
@@ -44,8 +45,9 @@ AT_HEAD_WIN2 = 8192
 AT_MF = 12288
 AT_E_SECOND = 16384
 AT_AFFINE_SECOND = 28672
+AT_IDENT = 49152
 AT_HEAD_WIN1 = 32768
-AT_TAIL_WIN1 = 40960
+AT_TAIL_WIN1 = 49152
 
 FLOPS = 2 * 2 * D * F * PAIRS
 
@@ -80,16 +82,16 @@ def tile_attend_gtransr_E_kernel(tc, eT, M, rv, wi, cf, hoffs, toffs, out):
         nc.sync.dma_start(rv_sb[:], rv.rearrange("(p t) o -> p (t o)", t=PACK))
         nc.sync.dma_start(wi_sb[:], wi)
 
-        ident = keep.tile([P, P], F32, name="ident")
+        ident = shared.tile([P, P], F32, name="ident", offset=AT_IDENT)
         make_identity(nc, ident[:])
 
         head_win = [keep.tile([P, T], F32, name="head_win0"), shared.tile([P, T], F32, name="head_win1", offset=AT_HEAD_WIN1)]
-        tail_win = [keep.tile([P, T], F32, name="tail_win0"), shared.tile([P, T], F32, name="tail_win1", offset=AT_TAIL_WIN1)]
-        for win in head_win:
-            for cols in (slice(0, T // 2 - 1), slice(T // 2 - 1, T)):
+        tail_win = [keep.tile([P, T], F32, name="tail_win0")]
+        for win, width in zip(head_win, (T, VECTOR_ZEROS)):
+            for cols in (slice(0, width // 2 - 1), slice(width // 2 - 1, width)):
                 nc.vector.memset(win[:, cols].bitcast(U32), 0)
-        for win in tail_win:
-            nc.gpsimd.memset(win[:].bitcast(U32), 0)
+        for win in (tail_win[0][:], head_win[1][:, VECTOR_ZEROS:]):
+            nc.gpsimd.memset(win.bitcast(U32), 0)
 
         cf2 = keep.tile([P, PACK], F32, name="cf2")
         rv_cf2 = keep.tile([P, PACK], F32, name="rv_cf2")
@@ -124,6 +126,8 @@ def tile_attend_gtransr_E_kernel(tc, eT, M, rv, wi, cf, hoffs, toffs, out):
             for t in range(PACK):
                 nc.tensor.transpose(turned[:, t * P : (t + 1) * P], md_words[:, t, :, a], ident[:])
             copy(mf_bf[:, 2 * a : 2 * a + 2], turned[:].bitcast(BF16).rearrange("m (t c e) -> m e c t", t=PACK, e=2))
+        tail_win.append(shared.tile([P, T], F32, name="tail_win1", offset=AT_TAIL_WIN1))
+        nc.gpsimd.memset(tail_win[1][:].bitcast(U32), 0)
 
         q_early = [shared.tile([P, 2, HALF], F32, name="q_early%d" % h, offset=AT_Q_EARLY[h]) for h in range(2)]
         early_tails = [keep.tile([P, PAIRS], F32, name="tails0"), shared.tile([P, PAIRS], F32, name="tails1", offset=AT_TAILS1)]

@@ -35,7 +35,7 @@ VECTOR_ZEROS = 1280
 SLIVER = 32
 PLANE1_EDGES = (0, 1024, 1792, T)
 PLANE2_EDGES = (0, 256, 768, 1408, T)
-PLANE3_EDGES = (0, 640, 1280, 1792, T)
+PLANE3_EDGES = (0, 640, 1280, 1792, 1920, T)
 
 AT_LATE_HEADS = 2048
 AT_TAILS1 = 4096
@@ -45,8 +45,8 @@ AT_HEAD_WIN2 = 8192
 AT_MF = 12288
 AT_E_SECOND = 16384
 AT_AFFINE_SECOND = 28672
-AT_IDENT = 49152
 AT_HEAD_WIN1 = 32768
+AT_IDENT = 49152
 AT_TAIL_WIN1 = 49152
 
 FLOPS = 2 * 2 * D * F * PAIRS
@@ -247,7 +247,8 @@ def tile_attend_gtransr_E_kernel(tc, eT, M, rv, wi, cf, hoffs, toffs, out):
         project(QUARTER, HALF, PACK)
         for lo, hi in LAST_QUARTERS:
             weave_late(lo, hi)
-        quantize_q(HALF, PAIRS)
+        for lo, hi in LAST_QUARTERS:
+            quantize_q(lo, hi)
         for c, (lo, hi) in enumerate(LAST_QUARTERS):
             project(lo, hi, PACK * c)
         for lo, hi in FIRST_QUARTERS:
@@ -260,8 +261,9 @@ def tile_attend_gtransr_E_kernel(tc, eT, M, rv, wi, cf, hoffs, toffs, out):
         for lo, hi in ((HALF, HALF + SLIVER), (HALF + SLIVER, HALF + QUARTER), LAST_QUARTERS[1]):
             weigh(lo, hi)
         dd_own = shared.tile([P, HALF], F32, name="dd_own", offset=AT_AFFINE_SECOND)
+        quantize_e(*LAST_QUARTERS[0])
         nc.vector.tensor_copy(dd_own[:], first_acc)
-        quantize_e(HALF, PAIRS)
+        quantize_e(*LAST_QUARTERS[1])
         tail_win.append(shared.tile([P, T], F32, name="tail_win2", offset=AT_E_SECOND))
         nc.gpsimd.memset(tail_win[2][:].bitcast(U32), 0)
 

@@ -283,22 +283,18 @@ def tile_attend_gtransr_E_kernel(tc, eT, M, rv, wi, cf, hoffs, toffs, out):
         nc.vector.tensor_copy(head_win[0][:].indirect(entries(heads, 0, HALF)), dd_own[:])
         nc.scalar.copy(dd[0][:, HALF:], back(0, HALF, PAIRS, 1))
         accs = {j: back(j, 0, PAIRS, b) for j, b in ((1, 2), (2, 1), (3, 3))}
-        nc.scalar.copy(dd[1][:, :HALF], accs[1][:, :HALF])
-        put_scalar(tail_win, tails, 0, HALF, PAIRS)
-        put_vector(head_win, heads, 0, HALF, PAIRS)
-        nc.vector.tensor_copy(dd[1][:, HALF:], accs[1][:, HALF:])
-        nc.vector.tensor_copy(dd[2][:], accs[2])
+        nc.scalar.copy(dd[1][:], accs[1])
+        put_scalar(head_win, heads, 0, HALF, PAIRS)
+        put_vector(tail_win, tails, 0, HALF, PAIRS)
         leave(0, (0, T), nc.gpsimd, keep.tile([P, T], F32, name="res0"))
-        put_scalar(tail_win, tails, 1, 0, HALF)
-        put_scalar(head_win, heads, 2, 0, HALF)
-        put_scalar(tail_win, tails, 1, HALF, PAIRS)
-        put_vector(head_win, heads, 1, 0, PAIRS)
-        nc.vector.tensor_copy(dd[3][:], accs[3])
+        for j in (1, 2):
+            put_vector(head_win, heads, j, 0, PAIRS)
+            put_scalar(tail_win, tails, j, 0, HALF)
+            nc.scalar.copy(dd[j + 1][:], accs[j + 1])
+            put_scalar(tail_win, tails, j, HALF, PAIRS)
         leave(1, PLANE1_EDGES, nc.gpsimd, keep.tile([P, T], F32, name="res1"))
-        put_vector(head_win, heads, 2, HALF, PAIRS)
-        for j in (2, 3):
-            for lo, hi in HALVES:
-                put_scalar(tail_win, tails, j, lo, hi)
         put_vector(head_win, heads, 3, 0, PAIRS)
+        for lo, hi in HALVES:
+            put_scalar(tail_win, tails, 3, lo, hi)
         leave(2, PLANE2_EDGES, nc.vector, shared.tile([P, T], F32, name="res2", offset=AT_HEAD_WIN1))
         leave(3, PLANE3_EDGES, nc.vector, shared.tile([P, T], F32, name="res3", offset=AT_TAIL_WIN1))

@@ -33,9 +33,9 @@ LAST_QUARTERS = ((HALF, HALF + QUARTER), (HALF + QUARTER, PAIRS))
 DEAL = 48
 VECTOR_ZEROS = 1280
 SLIVER = 32
-PLANE1_EDGES = (0, 1024, 1792, T)
-PLANE2_EDGES = (0, 256, 768, 1408, T)
-PLANE3_EDGES = (0, 640, 1280, 1792, 1920, T)
+PLANE1_EDGES = (0, 1152, 1760, T)
+PLANE2_EDGES = (0, 320, 704, 1120, 1568, T)
+PLANE3_EDGES = (0, 512, 1024, 1536, T)
 
 AT_LATE_HEADS = 2048
 AT_TAILS1 = 4096

from contextlib import ExitStack

import concourse.mybir as mybir
from concourse.masks import make_identity

F32 = mybir.dt.float32
BF16 = mybir.dt.bfloat16
U32 = mybir.dt.uint32
U16 = mybir.dt.uint16
U8 = mybir.dt.uint8
E4M3 = mybir.dt.float8_e4m3fn_x4
E5M2 = mybir.dt.float8_e5m2_x4
ALU = mybir.AluOpType
ACT = mybir.ActivationFunctionType

P = 128
PACK = 4
D = 512
F = 512
PAIRS = 512
T = 2048
BAND = 16
LIST_COLS = PAIRS // BAND
RUN = 4
WINDOWS = 3

HALF = PAIRS // 2
QUARTER = PAIRS // 4
HALVES = ((0, HALF), (HALF, PAIRS))
FIRST_QUARTERS = ((0, QUARTER), (QUARTER, HALF))
LAST_QUARTERS = ((HALF, HALF + QUARTER), (HALF + QUARTER, PAIRS))

DEAL = 48
VECTOR_ZEROS = 1280
SLIVER = 32
PLANE1_EDGES = (0, 1152, 1760, T)
PLANE2_EDGES = (0, 320, 704, 1120, 1568, T)
PLANE3_EDGES = (0, 512, 1024, 1536, T)

AT_LATE_HEADS = 2048
AT_TAILS1 = 4096
AT_MD = 5120
AT_Q_EARLY = (8192, 6144)
AT_HEAD_WIN2 = 8192
AT_MF = 12288
AT_E_SECOND = 16384
AT_AFFINE_SECOND = 28672
AT_HEAD_WIN1 = 32768
AT_IDENT = 49152
AT_TAIL_WIN1 = 49152

FLOPS = 2 * 2 * D * F * PAIRS


def tile_attend_gtransr_E_kernel(tc, eT, M, rv, wi, cf, hoffs, toffs, out):
    nc = tc.nc
    with ExitStack() as ctx:
        lists = ctx.enter_context(tc.tile_pool(name="lists", bufs=1))
        keep = ctx.enter_context(tc.tile_pool(name="keep", bufs=1))
        shared = ctx.enter_context(tc.tile_pool(name="shared", bufs=1))
        psum = ctx.enter_context(tc.psum_pool(name="psum", bufs=1))

        def bank(b):
            return psum.tile([P, PAIRS], F32, name="bank%d" % b, tag="bank%d" % b)

        heads = lists.tile([P, LIST_COLS], U16, name="heads")
        tails = lists.tile([P, LIST_COLS], U16, name="tails")
        e_rows = eT.rearrange("(p j) n -> p j n", j=PACK)
        out_rows = out.rearrange("(p j) n -> p j n", j=PACK)
        table = [keep.tile([P, T], F32, name="table%d" % j) for j in range(PACK)]
        m_raw = keep.tile([P, PACK, F], F32, name="m_raw")
        wi_sb = keep.tile([P, PAIRS], F32, name="wi_sb")
        rv_sb = keep.tile([P, PACK], F32, name="rv_sb")
        cf_sb = keep.tile([P, PACK], F32, name="cf_sb")

        nc.sync.dma_start(m_raw[:], M.rearrange("(p j) f -> p j f", j=PACK))
        nc.sync.dma_start(tails[:], toffs)
        nc.sync.dma_start(heads[:], hoffs)
        for j in range(PACK):
            nc.sync.dma_start(table[j][:], e_rows[:, j, :])
        nc.sync.dma_start(cf_sb[:], cf.rearrange("(p t) o -> p (t o)", t=PACK))
        nc.sync.dma_start(rv_sb[:], rv.rearrange("(p t) o -> p (t o)", t=PACK))
        nc.sync.dma_start(wi_sb[:], wi)

        ident = shared.tile([P, P], F32, name="ident", offset=AT_IDENT)
        make_identity(nc, ident[:])

        head_win = [keep.tile([P, T], F32, name="head_win0"), shared.tile([P, T], F32, name="head_win1", offset=AT_HEAD_WIN1)]
        tail_win = [keep.tile([P, T], F32, name="tail_win0")]
        for win, width in zip(head_win, (T, VECTOR_ZEROS)):
            for cols in (slice(0, width // 2 - 1), slice(width // 2 - 1, width)):
                nc.vector.memset(win[:, cols].bitcast(U32), 0)
        for win in (tail_win[0][:], head_win[1][:, VECTOR_ZEROS:]):
            nc.gpsimd.memset(win.bitcast(U32), 0)

        cf2 = keep.tile([P, PACK], F32, name="cf2")
        rv_cf2 = keep.tile([P, PACK], F32, name="rv_cf2")

        def entries(offsets, lo, hi):
            return offsets[:, lo // BAND : hi // BAND]

        def woven(dst):
            return dst.rearrange("p (c i) t -> p c t i", i=RUN)

        def planes(src):
            return src.rearrange("p t (c i) -> p c t i", i=RUN)

        def quantize(codes, scales, src, fmt):
            nc.vector.quantize_mx(codes.bitcast(fmt), scales, src.rearrange("p i t -> p (i t)"))

        md_bf = shared.tile([P, PACK, P, PACK], BF16, name="md_bf", offset=AT_MD, align_bytes=64)
        md_codes = keep.tile([P, F], U32, name="md_codes", align_bytes=64)
        md_scales = keep.tile([P, F], U8, name="md_scales", align_bytes=64)
        md_view = md_bf[:].rearrange("p t m j -> p m j t")
        m_view = m_raw[:].rearrange("p j (m t) -> p m j t", t=PACK)
        nc.scalar.copy(md_view[:, :DEAL], m_view[:, :DEAL])
        nc.vector.tensor_copy(md_view[:, DEAL:], m_view[:, DEAL:])
        quantize(md_codes[:], md_scales[:], md_bf[:].rearrange("p t m j -> p (t m) j"), E4M3)

        md_words = md_bf[:].rearrange("p t m j -> p (t m j)").bitcast(F32).rearrange("p (t m a) -> p t m a", t=PACK, a=2)
        mf_bf = shared.tile([P, PACK, P, PACK], BF16, name="mf_bf", offset=AT_MF, align_bytes=64)
        mf_codes = keep.tile([P, D], U32, name="mf_codes", align_bytes=64)
        mf_scales = keep.tile([P, D], U8, name="mf_scales", align_bytes=64)
        for a, copy in enumerate((nc.vector.tensor_copy, nc.scalar.copy)):
            turned = bank(PACK + a)
            for t in range(PACK):
                nc.tensor.transpose(turned[:, t * P : (t + 1) * P], md_words[:, t, :, a], ident[:])
            copy(mf_bf[:, 2 * a : 2 * a + 2], turned[:].bitcast(BF16).rearrange("m (t c e) -> m e c t", t=PACK, e=2))
        tail_win.append(shared.tile([P, T], F32, name="tail_win1", offset=AT_TAIL_WIN1))
        nc.gpsimd.memset(tail_win[1][:].bitcast(U32), 0)

        q_early = [shared.tile([P, 2, HALF], F32, name="q_early%d" % h, offset=AT_Q_EARLY[h]) for h in range(2)]
        early_tails = [keep.tile([P, PAIRS], F32, name="tails0"), shared.tile([P, PAIRS], F32, name="tails1", offset=AT_TAILS1)]
        late_heads = shared.tile([P, 2, PAIRS], F32, name="late_heads", offset=AT_LATE_HEADS)
        late_tails = keep.tile([P, 2, PAIRS], F32, name="late_tails")

        def pick_scalar(dst, j, offsets, lo, hi):
            nc.scalar.activation(dst[:, lo:hi], table[j][:].indirect(entries(offsets, lo, hi)), ACT.Copy)

        def pick_vector(dst, j, offsets, lo, hi):
            nc.vector.tensor_copy(dst[:, lo:hi], table[j][:].indirect(entries(offsets, lo, hi)))

        def subtract_early(j, lo, hi):
            picked_heads = table[j][:].indirect(entries(heads, lo, hi))
            nc.vector.tensor_tensor(q_early[lo // HALF][:, j, :], picked_heads, early_tails[j][:, lo:hi], ALU.subtract)

        q_codes = keep.tile([P, PAIRS], U32, name="q_codes", align_bytes=64)
        q_scales = keep.tile([P, PAIRS], U8, name="q_scales", align_bytes=64)
        e_codes = keep.tile([P, PAIRS], U32, name="e_codes", align_bytes=64)
        e_scales = keep.tile([P, PAIRS], U8, name="e_scales", align_bytes=64)
        q_bf = [keep.tile([P, HALF, PACK], BF16, name="q_bf%d" % h, align_bytes=64) for h in range(2)]
        e_bf = [
            keep.tile([P, HALF, PACK], BF16, name="e_bf0", align_bytes=64),
            shared.tile([P, HALF, PACK], BF16, name="e_bf1", offset=AT_E_SECOND, align_bytes=64),
        ]
        affine = [
            keep.tile([P, PACK, HALF], F32, name="affine0"),
            shared.tile([P, PACK, HALF], F32, name="affine1", offset=AT_AFFINE_SECOND),
        ]

        def within(lo, hi):
            return slice(lo % HALF, lo % HALF + hi - lo)

        def part(tiles, lo, hi):
            return tiles[lo // HALF][:, within(lo, hi)]

        def weave_early(copy, lo, hi):
            copy(woven(part(q_bf, lo, hi)[:, :, :2]), planes(q_early[lo // HALF][:]))

        def weave_late(lo, hi):
            nc.vector.tensor_tensor(
                woven(part(q_bf, lo, hi)[:, :, 2:]), planes(late_heads[:, :, lo:hi]), planes(late_tails[:, :, lo:hi]), ALU.subtract
            )

        def quantize_q(lo, hi):
            quantize(q_codes[:, lo:hi], q_scales[:, lo:hi], part(q_bf, lo, hi), E4M3)

        def quantize_e(lo, hi):
            quantize(e_codes[:, lo:hi], e_scales[:, lo:hi], part(e_bf, lo, hi), E5M2)

        def project(lo, hi, first_bank):
            for t in range(PACK):
                cols = slice(t * P, (t + 1) * P)
                u = bank(first_bank + t)
                nc.tensor.matmul_mx(
                    out=u[:, : hi - lo],
                    lhsT=md_codes[:, cols].bitcast(E4M3),
                    lhsT_scale=md_scales[:, cols],
                    rhs=q_codes[:, lo:hi].bitcast(E4M3),
                    rhs_scale=q_scales[:, lo:hi],
                    start=True,
                    stop=True,
                )
                dst = affine[lo // HALF][:, t, within(lo, hi)]
                nc.scalar.activation(dst, u[:, : hi - lo], ACT.Identity, bias=rv_cf2[:, t : t + 1], scale=cf2[:, t : t + 1])

        def weigh(lo, hi):
            nc.vector.tensor_tensor(
                woven(part(e_bf, lo, hi)),
                planes(affine[lo // HALF][:, :, within(lo, hi)]),
                wi_sb[:, lo:hi].rearrange("p (c i) -> p c i", i=RUN).unsqueeze(2).to_broadcast([P, (hi - lo) // RUN, PACK, RUN]),
                ALU.mult,
            )

        pick_scalar(early_tails[0], 0, tails, 0, PAIRS)
        for lo, hi in HALVES:
            subtract_early(0, lo, hi)
        quantize(mf_codes[:], mf_scales[:], mf_bf[:].rearrange("m j c t -> m (j c) t"), E4M3)
        for lo, hi in HALVES:
            pick_scalar(early_tails[1], 1, tails, lo, hi)
            subtract_early(1, lo, hi)
        weave_early(nc.vector.tensor_copy, 0, HALF)
        head_win.append(shared.tile([P, T], F32, name="head_win2", offset=AT_HEAD_WIN2))
        nc.gpsimd.memset(head_win[2][:].bitcast(U32), 0)
        pick_vector(late_heads[:, 0], 2, heads, 0, PAIRS)
        pick_scalar(late_tails[:, 0], 2, tails, 0, PAIRS)
        weave_early(nc.scalar.copy, HALF, PAIRS)

        def back(j, lo, hi, b):
            acc = bank(b)
            cols = slice(j * P, (j + 1) * P)
            nc.tensor.matmul_mx(
                out=acc[:, : hi - lo],
                lhsT=mf_codes[:, cols].bitcast(E4M3),
                lhsT_scale=mf_scales[:, cols],
                rhs=e_codes[:, lo:hi].bitcast(E5M2),
                rhs_scale=e_scales[:, lo:hi],
                start=True,
                stop=True,
            )
            return acc[:, : hi - lo]

        for lo, hi in FIRST_QUARTERS:
            pick_vector(late_heads[:, 1], 3, heads, lo, hi)
            pick_scalar(late_tails[:, 1], 3, tails, lo, hi)
        for lo, hi in LAST_QUARTERS:
            pick_scalar(late_tails[:, 1], 3, tails, lo, hi)
            pick_scalar(late_heads[:, 1], 3, heads, lo, hi)
        nc.scalar.activation(cf2[:], cf_sb[:], ACT.Square)
        for t in range(PACK):
            nc.scalar.activation(rv_cf2[:, t : t + 1], rv_sb[:, t : t + 1], ACT.Copy, scale=cf2[:, t : t + 1])
        for lo, hi in FIRST_QUARTERS:
            weave_late(lo, hi)
        quantize_q(0, QUARTER)
        project(0, QUARTER, 0)
        quantize_q(QUARTER, HALF)
        project(QUARTER, HALF, PACK)
        for lo, hi in LAST_QUARTERS:
            weave_late(lo, hi)
        for lo, hi in LAST_QUARTERS:
            quantize_q(lo, hi)
        for c, (lo, hi) in enumerate(LAST_QUARTERS):
            project(lo, hi, PACK * c)
        for lo, hi in FIRST_QUARTERS:
            weigh(lo, hi)
        for lo, hi in FIRST_QUARTERS:
            quantize_e(lo, hi)
        dd = [keep.tile([P, PAIRS], F32, name="dd%d" % j) for j in range(PACK)]
        first_acc = back(0, 0, HALF, 0)
        nc.scalar.copy(dd[0][:, :HALF], first_acc)
        for lo, hi in ((HALF, HALF + SLIVER), (HALF + SLIVER, HALF + QUARTER), LAST_QUARTERS[1]):
            weigh(lo, hi)
        dd_own = shared.tile([P, HALF], F32, name="dd_own", offset=AT_AFFINE_SECOND)
        quantize_e(*LAST_QUARTERS[0])
        nc.vector.tensor_copy(dd_own[:], first_acc)
        quantize_e(*LAST_QUARTERS[1])
        tail_win.append(shared.tile([P, T], F32, name="tail_win2", offset=AT_E_SECOND))
        nc.gpsimd.memset(tail_win[2][:].bitcast(U32), 0)

        def put_vector(wins, offsets, j, lo, hi):
            nc.vector.tensor_copy(wins[j % WINDOWS][:].indirect(entries(offsets, lo, hi)), dd[j][:, lo:hi])

        def put_scalar(wins, offsets, j, lo, hi):
            nc.scalar.activation(wins[j % WINDOWS][:].indirect(entries(offsets, lo, hi)), dd[j][:, lo:hi], ACT.Copy)

        def leave(j, edges, engine, res):
            for lo, hi in zip(edges[:-1], edges[1:]):
                cols = slice(lo, hi)
                engine.tensor_tensor(res[:, cols], head_win[j % WINDOWS][:, cols], tail_win[j % WINDOWS][:, cols], ALU.subtract)
                nc.sync.dma_start(out_rows[:, j, cols], res[:, cols])

        put_scalar(tail_win, tails, 0, 0, HALF)
        nc.vector.tensor_copy(head_win[0][:].indirect(entries(heads, 0, HALF)), dd_own[:])
        nc.scalar.copy(dd[0][:, HALF:], back(0, HALF, PAIRS, 1))
        accs = {j: back(j, 0, PAIRS, b) for j, b in ((1, 2), (2, 1), (3, 3))}
        nc.scalar.copy(dd[1][:], accs[1])
        put_scalar(head_win, heads, 0, HALF, PAIRS)
        put_vector(tail_win, tails, 0, HALF, PAIRS)
        leave(0, (0, T), nc.gpsimd, keep.tile([P, T], F32, name="res0"))
        for j in (1, 2):
            put_vector(head_win, heads, j, 0, PAIRS)
            put_scalar(tail_win, tails, j, 0, HALF)
            nc.scalar.copy(dd[j + 1][:], accs[j + 1])
            put_scalar(tail_win, tails, j, HALF, PAIRS)
        leave(1, PLANE1_EDGES, nc.gpsimd, keep.tile([P, T], F32, name="res1"))
        put_vector(head_win, heads, 3, 0, PAIRS)
        for lo, hi in HALVES:
            put_scalar(tail_win, tails, 3, lo, hi)
        leave(2, PLANE2_EDGES, nc.vector, shared.tile([P, T], F32, name="res2", offset=AT_HEAD_WIN1))
        leave(3, PLANE3_EDGES, nc.vector, shared.tile([P, T], F32, name="res3", offset=AT_TAIL_WIN1))
